import numpy as np, ml_dtypes
CORES = [9,25,41,57]
N = 4
BF = ml_dtypes.bfloat16
V, P, B, C, RO, LG = 2048, 256, 8, 64, 4, 2
PAR = np.array([bin(i).count("1") % 2 for i in range(N)]).reshape(N, 1)
GRP = np.arange(8).reshape(1, 8)
def base(rng):
    nbr = rng.integers(0, V, (8, 16, V)); w = rng.integers(100, 256, (8, 16, V)); b = rng.integers(2 ** 12, 2 ** 19, (8, 16, 1))
    return nbr, w, b, b + rng.integers(0, 100, (N, 8, 16, V))
def stir(rng, x, up, down):
    hi = rng.random((N, 8, V)) < up; lo = (rng.random((N, 8, V)) < down) & ~hi
    m = rng.random(x.shape) < rng.random((N, 8, 1, V))
    a = np.exp2(6 + 13 * rng.random(x.shape)).astype(np.int64); d = np.exp2(12 * rng.random(x.shape)).astype(np.int64)
    x = np.where(hi[:, :, None, :] & m, np.minimum(x + a, 2 ** 20 - 1), x)
    return np.where(lo[:, :, None, :] & m, np.maximum(x - d, 0), x), hi
def names(rng, hi):
    o = np.argsort(rng.random((N, 8, V)) - hi, axis=-1); h = np.add.reduce(hi.astype(np.int64), axis=-1)[:, :, None]
    a = np.take_along_axis(o, (rng.random((N, 8, 16 * P)) * h).astype(np.int64), -1)
    return np.where(rng.random(a.shape) < 0.5, a, rng.integers(0, V, a.shape)).reshape(N, 8, 16, P)
def heights(rng):
    e = rng.choice(np.array([0.1, 0.25, 0.4, 0.6]), (N, 8, 1))
    return np.where(rng.random((N, 8, P)) < e, 0, rng.integers(1, 17, (N, 8, P)))
def pack(nbr, w, x, st, n):
    st = np.where(np.arange(16)[:, None] < n[:, :, None, :], st, 0)
    return {"nb": np.tile(nbr.reshape(1, 128, V), (N, 1, 1)).astype(np.int32), "ln": np.tile(w.reshape(1, 128, V), (N, 1, 1)).astype(np.float32).astype(BF),
            "lab": np.ascontiguousarray(x.reshape(N, 128, V)).astype(np.int32), "stk": np.ascontiguousarray(st.reshape(N, 128, P)).astype(np.int32), "cnt": n.astype(np.int32)}
def setup_inputs(rng):
    nbr, w, b, x = base(rng)
    x, hi = stir(rng, x, rng.choice(np.array([0.02, 0.04, 0.08, 0.16]), (N, 8, 1)), rng.choice(np.array([0.0, 0.001, 0.004]), (N, 8, 1)))
    return pack(nbr, w, x, names(rng, hi), heights(rng))
def setup_inputs_spread(rng):
    nbr, w, b, x = base(rng)
    nbr[1::2] = (V * rng.random((4, 16, V)) ** 3).astype(np.int64); w[1::2] = np.exp2(8 * rng.random((4, 16, V))).astype(np.int64)
    b = np.minimum(np.exp2(20 * rng.random((8, 16, 1))).astype(np.int64), 2 ** 20 - 5000)
    x, hi = stir(rng, b + rng.integers(0, 100, x.shape), 0.06, 0.002)
    x[:, 1::2] = np.minimum((np.exp2(20 * rng.random((N, 4, 1, V))) * rng.random((N, 4, 16, V))).astype(np.int64), 2 ** 20 - 1)
    return pack(nbr, w, x, names(rng, hi), heights(rng))
def setup_inputs_ends(rng):
    e = np.array([0, V - 1])
    nbr = np.where(rng.random((8, 16, V)) < 0.75, rng.choice(e, (8, 16, V)), rng.integers(0, V, (8, 16, V)))
    w = rng.choice(np.array([1, 255]), (8, 16, V))
    k = rng.random((N, 8, 1, V)); x = (2 ** 20 - 1) * np.where(k < 0.7, 1, np.where(k < 0.8, 0, rng.integers(0, 2, (N, 8, 16, V))))
    x[..., e] = (2 ** 20 - 1) * rng.integers(0, 2, (N, 8, 16, 2))
    full = rng.random((N, 8, P)) < rng.choice(np.array([0.3, 0.5, 0.7]), (N, 8, 1))
    n = np.where(rng.random((N, 8, P)) < 0.8, 16 * full, rng.choice(np.array([1, 2, B + 1, B + 2, 15]), (N, 8, P)))
    st = np.where(rng.random((N, 8, 16, P)) < 0.75, rng.choice(e, (N, 8, 16, P)), rng.integers(0, V, (N, 8, 16, P)))
    n[N - 1, 7, P - 1] = 16; st[N - 1, 7, 15, P - 1] = V - 1; n[0, 7, P - 1] = 0; n[0, 0, 0] = 16; st[0, 0, 15, 0] = 0
    return pack(nbr, w, x, st, n)
def setup_inputs_corners(rng):
    nbr, w, b, x = base(rng); v = np.arange(V)
    nbr[1] = v; nbr[2] = rng.choice(np.array([0, V - 1]), (16, V)); nbr[3] = (v + 1) % V; nbr[4] = np.where(rng.random((16, V)) < 0.5, v, V - 1 - v)
    y, hi = stir(rng, x, 0.05, 0.002); x[:, 6:] = y[:, 6:]
    w[0] = rng.choice(np.array([1, 255]), (16, V)); x[:, 0] = b[0] + rng.integers(0, 2, (N, 16, V))
    w[5] = 255; x[:, 5] = 255 * rng.integers(0, 2, (N, 16, V))
    sn = rng.choice(np.array([0, 1, C - 1, C, C + 1, P - C - 1]), (N, 8)); em = rng.choice(np.array([0, 1, C - 1, C, C + 1]), (N, 8))
    sn[0] = (C, C + 1, C, C - 1, 0, C + 1, 1, C); em[1] = (C, C, C + 1, C + 1, C + 1, 0, C, 1)
    sn[N - 1] = (1, P - C - 1, 0, C, C + 1, C - 1, C, C); em[N - 2] = (C, C, C, C - 1, C, C, C, C + 1)
    pos = np.argsort(rng.random((N, 8, P)), axis=-1); sn = sn[:, :, None]; em = em[:, :, None]
    n = np.where(pos < sn, rng.choice(np.array([B + 2, 15, 16]), pos.shape), np.where(pos < sn + em, rng.integers(0, 2, pos.shape), rng.choice(np.array([2, B, B + 1]), pos.shape)))
    return pack(nbr, w, x, names(rng, hi), n)
def setup_inputs_crowd(rng):
    nbr, w, b, x = base(rng); c = rng.integers(1, V - 1, 8); c[0] = 0; c[7] = V - 1
    full = (PAR + GRP) % 2 == 0
    nbr[0:2, :8] = rng.choice(np.array([5, 6, V - 2]), (2, 8, V)); nbr[:, 15] = c[:, None]
    n = np.where(full, 16, 0)[:, :, None] * np.ones((1, 1, P), np.int64)
    st = np.tile(c.reshape(1, 8, 1, 1), (N, 1, 16, P))
    st[:, 3::4] = rng.integers(0, V, (N, 2, 16, 1))
    for q in range(8):
        u = int(c[q]); a = nbr[q, :, u].copy(); a = np.where(a == u, (u + 1) % V, a)
        if q % 2 == 1: a[15] = u
        nbr[q, :, u] = a
        if q % 4 == 2: st[:, q] = rng.choice(np.array([u, 0, V - 1]), (N, 16, P))
        for r in range(N):
            if q % 4 == 1: st[r, q, :, int(rng.integers(0, P))] = rng.integers(0, V, 16)
            if full[r, q] or q >= 4: x[r, q, :, u] = 0
            if q >= 4: n[r, q, int(rng.integers(0, P))] = 0 if full[r, q] else 1
    return pack(nbr, w, x, st, n)
def setup_inputs_calm(rng):
    nbr, w, b, x = base(rng); w = rng.choice(np.array([1, 255]), w.shape)
    b = rng.integers(2 ** 19, 2 ** 20 - 3, b.shape); b[2:4] = 2 ** 20 - 2; b[6:8] = 2 ** 20 - 3; x = b + rng.integers(0, 2, x.shape)
    x[:, 4:] = np.where(rng.random((N, 4, 16, V)) < 0.0005, b[4:] + 2, x[:, 4:])
    r = np.arange(N).reshape(N, 1)
    big = (np.where(GRP % 4 == 2, 0, np.where(GRP % 4 == 3, 1, (PAR + GRP) % 2)) == 1)[:, :, None]
    h = ((r + GRP + rng.integers(0, 4)) % 4)[:, :, None]; few = ((3 * r + GRP + rng.integers(0, 4)) % 4)[:, :, None]
    pos = np.argsort(rng.random((N, 8, P)), axis=-1)
    n = np.where(pos < few, np.where(big, RO, B + 1 + RO), np.where(big, B + RO + rng.integers(0, 2, pos.shape), h + RO - 1))
    return pack(nbr, w, x, rng.integers(0, V, (N, 8, 16, P)), n)
def check_inputs(d):
    bad = []
    for k, lo, hi in (("nb", 0, V - 1), ("ln", 1, 255), ("lab", 0, 2 ** 20 - 1), ("stk", 0, V - 1), ("cnt", 0, 16)):
        a = np.asarray(d[k]).astype(np.float64)
        if not (np.min(a) >= lo and np.max(a) <= hi): bad.append("range of " + k)
        if k == "ln" and not np.all(a == np.floor(a)): bad.append("whole numbers in ln")
        if k in ("nb", "ln") and not np.all(a == a[:1]): bad.append(k + " alike on all ranks")
    s = np.asarray(d["stk"]).reshape(N, 8, 16, P); n = np.asarray(d["cnt"]).reshape(N, 8, 1, P)
    if np.any((np.arange(16)[:, None] >= n) & (s != 0)): bad.append("zeros in the empty slots of stk")
    return bad
def reference(nb, ln, lab, stk, cnt):
    nbr = nb.astype(np.int64).reshape(N, 8, 16, V); w = ln.astype(np.float32).astype(np.int64).reshape(N, 8, 16, V)
    x = lab.astype(np.int64).reshape(N, 8, 16, V); st = stk.astype(np.int64).reshape(N, 8, 16, P); n = cnt.astype(np.int64).reshape(N, 8, P)
    for t in range(RO):
        live = n > 0
        v = np.take_along_axis(st, np.maximum(n - 1, 0)[:, :, None, :], 2)
        k = np.take_along_axis(nbr, v, 3)
        kk = np.ascontiguousarray(k.transpose(0, 1, 3, 2)).reshape(N, 8, 1, 16 * P)
        xk = np.take_along_axis(x, kk, 3).reshape(N, 8, 16, P, 16); wk = np.take_along_axis(w, kk, 3).reshape(N, 8, 16, P, 16)
        y = np.minimum(np.take_along_axis(x, v, 3), np.min(xk, axis=4) + np.take_along_axis(w, v, 3))
        hit = np.any(xk > y[..., None] + wk, axis=2) & live[..., None]
        a, g, l = np.nonzero(live); x[a, g, :, v[a, g, 0, l]] = y[a, g, :, l]
        n = n - live.astype(np.int64); st = np.where(np.arange(16)[:, None] < n[:, :, None, :], st, 0)
        rank = np.add.accumulate(hit.astype(np.int64), axis=3); slot = n[..., None] + rank - 1
        a, g, l, i = np.nonzero(hit & (slot < 16)); st[a, g, slot[a, g, l, i], l] = k[a, g, i, l]
        n = np.minimum(n + rank[..., 15], 16)
        x2, st2, n2 = x.copy(), st.copy(), n.copy()
        for r in range(N):
            q = r ^ (1 << (t % LG))
            for g in range(8):
                give = np.nonzero(n[r, g] > B)[0]; get = np.nonzero(n[q, g] == 0)[0]
                m = min(len(give), len(get), C); give, get = give[:m], get[:m]
                s = st[r, g]; e = s[:B][:, give]
                st2[r, g][:, give] = np.concatenate([s[B:][:, give], np.zeros((B, m), np.int64)]); n2[r, g][give] = n[r, g][give] - B
                st2[q, g][:B, get] = e; n2[q, g][get] = B
                u = e.reshape(-1); x2[q, g][:, u] = np.minimum(x[q, g][:, u], x[r, g][:, u])
        x, st, n = x2, st2, n2
    return {"ylab": x.reshape(N, 128, V).astype(np.float32), "ystk": st.reshape(N, 128, P).astype(np.float32), "ycnt": n.astype(np.float32)}

@@ -1,0 +1,621 @@
+from concourse.mybir import AluOpType, ActivationFunctionType
+
+NM = "float16"
+N1 = 13
+STEPS = 4
+XW = 2080
+RW = 328
+
+F, B, I, U = "float32", "bfloat16", "int32", "uint16"
+_S = {
+    "X": (XW, F), "D": (2064, F), "NB": (2064, F), "WB": (2064, B), "LABI": (2048, I), "NBI": (2048, I),
+    "STI": (256, I), "STF": (256, F), "XK": (256 * N1, F), "XV": (256, F), "DK": (4096, F), "CMP": (4096, B),
+    "PI": (8, I), "COL": (24, F), "IM": (256, F), "IS": (256, F), "LDD": (2048, NM), "FU": (768, NM),
+    "M0": (144, B), "CT": (256, B), "ROW": (256, B), "DA": (32, F), "HOLD": (256, F),
+    "LST": (64, U), "SPI": (256, I), "SPJ": (256, I), "SPR": (256, F), "C4K": (512, F), "JB": (4, F), "JT": (32, F),
+    "VB": (16, F), "V16": (16, NM), "VJ": (32, U), "VU": (16, U), "KJ": (512, F), "KJT": (512, F),
+    "KA": (256, F), "KT": (256, U), "WV": (256, F), "AB": (512, F), "AV": (256, F), "SC": (512, F), "SM": (48, F),
+    "ZO": (32, U), "JO": (64, U), "S0": (256, F), "S1": (256, F), "ZS": (256, F), "HIT": (256, B), "TI": (256, I),
+    "TA": (256, I), "RH": (256, F), "E0": (128, F), "E1": (128, F), "KY": (256, F), "ST": (256, NM), "ST1": (256, F),
+    "C2": (256, F), "TM": (256, F), "OWB": (256, F), "DLT": (256, F), "NP": (16, F), "NN": (16, F), "NX": (256, B),
+    "FL": (32, B), "CODE": (32, F), "GG": (32, F), "FS": (256, B), "FE": (256, B), "JK": (256, B), "SA": (4, F),
+    "SL": (4, U), "STA": (264, F), "GA": (64, NM), "GU": (32, U), "RE": (16, U), "MSK": (32, F), "RV": (32, NM),
+    "RU": (32, U), "R7": (RW, F), "RA": (RW, F), "RCV": (256, F), "OWN": (512, F), "PB": (256, F), "YS": (256, F),
+    "YC": (256, F), "CNI": (256, I), "CNF": (256, F),
+}
+POOL = {}
+for _n, _d, _l in (("CB", B, "ONE NONE IB NIB TRI TRX TXM BO NBO BT NBT TT TH D1 D2"),
+                   ("CF", F, "IG ONE32 I32 NI32 I7 BO32 NBO32 T2 SI E8")):
+    for _k, _c in enumerate(_l.split()):
+        POOL[_c] = (_n, 128 * _k)
+    _S[_n] = (128 * len(_l.split()), _d)
+POOL["I16"] = ("FU", 640)
+for _t in range(STEPS):
+    _S["MO%d" % _t] = (64, F)
+    _S["MI%d" % _t] = (64, F)
+    _S["LO%d" % _t] = (512, F)
+    _S["LI%d" % _t] = (512, F)
+SCRATCH = {k: ("sbuf", [128, w], d) for k, (w, d) in _S.items()}
+PSUM = ["W0", "W1", "W2", "W3", "P4", "P5", "P6", "P7"]
+for _k in PSUM:
+    SCRATCH[_k] = ("psum", [128, 512], F)
+NDMA = 16
+SEMAPHORES = ["ev", "ea", "ep", "eg", "sent"] + ["d%d" % k for k in range(NDMA)] + \
+    [k + str(t) for t in range(STEPS) for k in ("nm", "la", "lb")]
+
+OP = AluOpType
+AF = ActivationFunctionType
+SPREAD = 33825.0 * 256.0
+BITS = 0x888800
+
+
+def rank_program(g, core, T, topo):
+    rank = T.rank_of(core)
+    if rank is None:
+        return
+    ops = []
+    Q = {"v": g.vector, "a": g.scalar, "p": g.tensor, "g": g, "s": g.sync}
+
+    def A(n, lo=0, hi=None, st=1, p=128):
+        if n in POOL:
+            hi = POOL[n][1] + (128 if hi is None else hi)
+            lo = POOL[n][1] + lo
+            n = POOL[n][0]
+        if hi is None:
+            hi = SCRATCH[n][1][1]
+        ap = T[n][0:p, lo:hi:st] if st != 1 else T[n][0:p, lo:hi]
+        return (ap, [(n, lo, hi, st)], [])
+
+    def HF(n, hf, base=0):
+        return A(n, base + 128 * hf, base + 128 * hf + 128)
+
+    def C(n, c):
+        return A(n, c, c + 1)
+
+    def G(n, hi, on, c, d):
+        return (T[n][:, 0:hi].indirect(T[on][:, c:d]), [(n, 0, hi, 1)], [(on, c, d, 1)])
+
+    def val(x):
+        return x[0] if isinstance(x, tuple) else x
+
+    def add(eng, fn, out, ins, kind="c", sem=None):
+        rd, wr = [], []
+        for o in out:
+            wr += o[1]
+            rd += o[2]
+        for x in ins:
+            if isinstance(x, tuple):
+                rd += x[1] + x[2]
+        ops.append({"e": eng, "fn": fn, "r": rd, "w": wr, "k": kind, "sem": sem})
+
+    def tt(o, a, b, op):
+        add("v", lambda: g.vector.tensor_tensor(o[0], a[0], b[0], op), [o], [a, b])
+
+    def ts(o, a, s1, op0, s2=None, op1=None):
+        if op1 is None:
+            add("v", lambda: g.vector.tensor_scalar(o[0], a[0], val(s1), None, op0), [o], [a, s1])
+        else:
+            add("v", lambda: g.vector.tensor_scalar(o[0], a[0], val(s1), val(s2), op0, op1), [o], [a, s1, s2])
+
+    def cp(o, a):
+        add("v", lambda: g.vector.tensor_copy(o[0], a[0]), [o], [a])
+
+    def ms(o, c):
+        add("v", lambda: g.vector.memset(o[0], c), [o], [])
+
+    def scan(o, d0, d1, init, op0, op1):
+        add("v", lambda: g.vector.tensor_tensor_scan(o[0], d0[0], d1[0], init, op0, op1), [o], [d0, d1])
+
+    def act(o, a, f=AF.Copy, bias=None, scale=None, acc=None):
+        kw = {}
+        if bias is not None:
+            kw["bias"] = val(bias)
+        if scale is not None:
+            kw["scale"] = scale
+        if acc is not None:
+            kw["accum_out"] = acc[0]
+        add("a", lambda: g.scalar.activation(o[0], a[0], f, **kw), [o] + ([acc] if acc else []), [a, bias])
+
+    def mm(o, l, r, st=True, sp=True):
+        add("p", lambda: g.tensor.matmul(o[0], l[0], r[0], st, sp), [o], [l, r])
+
+    def iota(o, pat, base=0, cm=0, isint=False):
+        if isint:
+            add("g", lambda: g.iota(o[0], pat, base, cm), [o], [])
+        else:
+            add("g", lambda: g.iota(o[0], pat, base, cm, allow_small_or_imprecise_dtypes=True), [o], [])
+
+    def sel(o, a, cmpop, fill):
+        add("g", lambda: g.affine_select(o[0], a[0], [[1, 128]], cmpop, fill, 0, -1), [o], [a])
+
+    nd = [0]
+
+    def dma(q, o, a):
+        s = "d%d" % nd[0]
+        nd[0] += 1
+        add(q, lambda: Q[q].dma_start(o[0], a[0]), [o], [a], kind="d", sem=s)
+
+    def H(ap):
+        return (ap, [], [])
+
+    nsent = [0]
+
+    def send(src, dst, sem, peer, lo=0, hi=None):
+        rid, pid, _ = topo.addr(peer)
+        m = topo.mask(core, peer)
+        nsent[0] += len(topo.engines(core, peer))
+        o, a = A(dst, lo, hi), A(src, lo, hi)
+        add("g", lambda: g.remote_dma(o[0], a[0], T.sem[sem], T.sem.sent, pid, rid, m), [], [a], kind="r")
+        ops.append({"e": "x", "fn": None, "r": [], "w": o[1], "k": "x", "sem": (sem, len(topo.engines(peer, core)))})
+
+    ms(A("WB", 0, 16), 1.0)
+    dma("s", A("CNI", p=8), H(T.cnt[:, :]))
+    dma("s", A("STI"), H(T.stk[:, :]))
+    dma("a", A("NBI", 0, 1024), H(T.nb[:, 0:1024]))
+    dma("s", A("NBI", 1024, 2048), H(T.nb[:, 1024:2048]))
+    dma("a", (T.WB[:, 1:2049], [("WB", 0, 2064, 1)], []), H(T.ln[:, :]))
+    dma("s", A("LABI", 0, 1024), H(T.lab[:, 0:1024]))
+    dma("a", A("LABI", 1024, 2048), H(T.lab[:, 1024:2048]))
+
+    iota(C("PI", 0), [[0, 1]], 0, 1, True)
+    iota(A("IG"), [[16, 8], [0, 16]])
+    iota(A("IS"), [[0, 16], [1, 16]], 1)
+    iota(A("IM"), [[1, 256]])
+    ms(A("ONE32"), 1.0)
+    ms(A("ONE"), 1.0)
+    ms(A("NONE"), -1.0)
+    ms(A("C4K"), 4096.0)
+    sel(A("I32"), A("ONE32"), OP.is_equal, 0.0)
+    for k, m in enumerate((15, 112, 16, 8)):
+        ts(C("PI", 1 + k), C("PI", 0), m, OP.bitwise_and)
+    cp(A("COL", 0, 5), A("PI", 0, 5))
+    cP, cA, cG, c16, c8 = C("COL", 0), C("COL", 1), C("COL", 2), C("COL", 3), C("COL", 4)
+
+    def col(k, src, m, a):
+        ts(C("COL", k), src, m, OP.mult, a, OP.add)
+        return C("COL", k)
+    cA1 = col(5, cA, 1.0, 1.0)
+    cWin = col(6, cA, -4096.0, 61440.0)
+    cP16 = col(18, cP, 16.0, 0.0)
+    cPick = col(9, cA, 32.0, c16)
+    ts(A("E8"), A("IG"), cP16, OP.is_equal)
+    ts(A("BO32"), A("IG"), cG, OP.is_equal)
+    EXP, PERM, PICK = 0, 16, 32
+    ts(A("HOLD"), A("IS"), cA1, OP.is_le, 1052672.0, OP.mult)
+    cp(A("LST", 0, 16), A("IM", 0, 16))
+    ts(A("LST", 32, 48), A("IM", 0, 16), cPick, OP.add)
+    ts(A("HOLD"), A("HOLD"), -4096.0, OP.add)
+    sel(A("T2"), A("BO32"), OP.not_equal, -1.0)
+    sel(A("IB"), A("ONE"), OP.is_equal, 0.0)
+    sel(A("NIB"), A("NONE"), OP.is_equal, 0.0)
+    iota(A("CT"), [[0, 16], [-1, 16]], 15)
+    act(A("BO"), A("BO32"))
+    act(A("NBO"), A("BO32"), scale=-1.0)
+    act(A("NBO32"), A("BO32"), scale=-1.0)
+    act(A("NI32"), A("I32"), scale=-1.0)
+    sel(A("BT"), A("BO"), OP.is_gt, 0.0)
+    sel(A("NBT"), A("NBO"), OP.is_gt, 0.0)
+    sel(A("TH"), A("NBT"), OP.not_equal, 31.0)
+    iota(A("D1"), [[0, 8], [1, 16]], -15)
+    sel(A("D2"), A("D1"), OP.is_equal, 0.0)
+    sel(A("TRI"), A("ONE"), OP.is_ge, 0.0)
+    sel(A("TRX"), A("ONE"), OP.is_gt, 0.0)
+    sel(A("TXM"), A("TRX"), OP.not_equal, -64.0)
+    iota(A("ROW"), [[1, 256]], 1)
+
+    def lst(k):
+        return ("LST", k, k + 16)
+
+    def pick(src):
+        scan(A("SC", 0, 256), A("HOLD"), src, 0.0, OP.add, OP.min)
+        return A("SC", 15, 256, 16)
+
+    def names_to_lists(src):
+        picked = pick(src)
+        for f in range(2):
+            ts(A("VJ", f, 32, 2), picked, cWin, OP.add)
+        act(A("KJ"), G("NB", 2049, "VJ", 0, 32))
+        ts(A("VU"), picked, cWin, OP.add)
+        ts(A("V16"), picked, cWin, OP.add)
+        ts(A("VB"), picked, cWin, OP.add)
+
+    def neighbour_tiles():
+        def tr(q):
+            o, a = A("KJT", 128 * q, 128 * q + 128), A("KJ", 128 * q, 128 * q + 128)
+            add("v", lambda: g.vector.transpose(o[0], a[0]), [o], [a])
+
+        def pk(q):
+            cp(A("KT", 64 * q, 64 * q + 64), G("KJT", 512, "LST", PICK + 4 * q, PICK + 4 * q + 4))
+        return [(lambda f, q: lambda: f(q))(f, q) for f in (tr, pk) for q in range(4)]
+
+    def own_vertex():
+        act(A("WV"), G("WB", 2049, "VU", 0, 16))
+        act(A("KA"), G("NB", 2049, "VU", 0, 16))
+        act(A("P4", 0, 256), A("WV"))
+        for hf in range(2):
+            mm(HF("P6", hf, 256), HF("KA", hf), A("I32"))
+
+    def diffs(src, n, bank, out):
+        for a in range(16):
+            mm(A(bank, a, 16 * n, 16), A("LDD", 128 * a, 128 * a + 128), src)
+        act(A(out, 0, 16 * n), A(bank, 0, 16 * n), AF.Abs, scale=131072.0)
+
+    def unique(src, n, ab, out):
+        return [lambda: scan(A("SC", 0, 16 * n), A("C4K", 0, 16 * n), A(ab, 0, 16 * n), 0.0, OP.add, OP.min),
+                lambda: tt(A("SM", 0, n), src, A("SC", 15, 16 * n, 16), OP.subtract),
+                lambda: ts(A(out, 0, 2 * n, 2), A("SM", 0, n), cWin, OP.add, cDum, OP.min)]
+
+    cp(A("CNF", p=8), A("CNI", p=8))
+    ts(A("STF"), A("STI"), 1.0, OP.add)
+    mm(A("P5", 0, 256), A("E8", p=8), A("CNF", p=8))
+    for hf in range(2):
+        mm(A("P7", 8 * hf, 8 * hf + 8), A("CNF", 128 * hf, 128 * hf + 128, p=8), A("I32", 0, 8, p=8))
+    ts(A("TM"), A("P5", 0, 256), cA1, OP.is_equal)
+    ts(A("OWB"), A("P5", 0, 256), cA1, OP.is_gt)
+    tt(A("TM"), A("TM"), A("STF"), OP.mult)
+    mm(A("P5", 256, 512), A("BO32"), A("TM"))
+    ms(A("NB", 0, 1), 0.0)
+    ts(A("NB", 1, 1025), A("NBI", 0, 1024), 1.0, OP.add)
+    tt(A("ST1"), A("OWB"), A("STF"), OP.mult)
+    cp(A("NN"), A("P7", 0, 16))
+    ts(A("NB", 1025, 2049), A("NBI", 1024, 2048), 1.0, OP.add)
+    names_to_lists(A("P5", 256, 512))
+    own_vertex()
+    for q in range(4):
+        act(A("W%d" % q), A("WB", 1 + 512 * q, 513 + 512 * q))
+    ms(A("X", 0, 1), 0.0)
+    ms(A("X", 2049, XW), 0.0)
+    ms(A("D", 0, 1), 1.0)
+    ts(A("DA", 0, 16), A("IM", 0, 16), cA, OP.is_equal)
+    ts(A("DA", 16, 32), A("IM", 0, 16), cA, OP.is_equal, -1.0, OP.add)
+    for a in range(16):
+        ts(A("LDD", 128 * a, 128 * a + 128), A("T2"), C("DA", 16 + a), OP.max, C("DA", a), OP.min)
+    for f in neighbour_tiles():
+        f()
+    for q in range(2):
+        ts(A("X", 1 + 1024 * q, 1025 + 1024 * q), A("LABI", 1024 * q, 1024 * q + 1024), -1.0, OP.mult)
+    cDum = C("COL", 7)
+    cCap = C("COL", 19)
+    cRe = C("COL", 20)
+
+    def late_constants():
+        col(7, cA, 1.0, 2049.0)
+        cA16 = col(8, cA, 16.0, 0.0)
+        cG15 = col(10, cG, 1.0, 15.0)
+        ts(A("SPI"), A("IS"), -1.0, OP.add, SPREAD, OP.mult)
+        ts(A("SPJ"), A("SPI"), BITS, OP.bitwise_and)
+        ts(A("M0"), A("IM", 0, 144), cG15, OP.is_equal)
+        cp(A("SPR"), A("SPJ"))
+        ts(A("LST", 16, 32), A("IM", 0, 16), cA16, OP.add)
+        cp(A("I16"), A("I32"))
+        ts(A("I7"), A("I32"), C("DA", 23), OP.mult, -1.0, OP.mult)
+        cP8 = col(11, cP, 1.0, 8.0)
+        cM8 = col(12, cP, 1.0, -8.0)
+        cGe = col(13, c8, 0.125, 0.0)
+        cLt = col(14, c8, -0.125, 1.0)
+        cJ = col(16, cA, 2.0, 1.0)
+        cJT = col(17, c8, 0.25, -256.0)
+        cBig = col(15, C("DA", 15), -1048576.0, -4096.0)
+        col(20, cWin, 1.0, 63.0)
+        im = A("IM", 0, 128)
+        ts(A("FU", 0, 128), im, cP, OP.is_equal, cLt, OP.mult)
+        ts(A("FU", 128, 256), im, cP8, OP.is_equal, cLt, OP.mult)
+        ts(A("FU", 256, 384), im, cM8, OP.is_equal, cGe, OP.mult)
+        col(19, cA, -4096.0, cBig)
+        for e in range(2):
+            ts(A("FU", 384 + 128 * e, 512 + 128 * e), A("BO32"), C("DA", 8 * e + 7), OP.mult)
+        tt(A("SI"), A("FU", 256, 384), A("I32"), OP.subtract)
+        ts(A("JB"), A("IM", 0, 4), 32.0, OP.mult, cJ, OP.add)
+        ts(A("JT"), A("IM", 0, 32), 4.0, OP.mult, cJT, OP.add)
+        ms(A("STA", 256, 264), 0.0)
+        ms(A("R7", 64, RW), 0.0)
+        ms(A("RA", 64, RW), 0.0)
+        tt(A("TT"), A("BT"), A("D2"), OP.add)
+    FOLD = [A("FU", 0, 128), A("FU", 128, 256)]
+    UNF = [A("FU", 0, 128), A("FU", 256, 384)]
+    UN7 = [A("FU", 384, 512), A("FU", 512, 640)]
+
+    def heights(t):
+        return [lambda: tt(A("GG"), A("CODE"), A("MI%d" % t, 32, 64), OP.is_lt),
+                lambda: tt(A("SM", 32, 48), A("GG", 16, 32), A("GG", 0, 16), OP.subtract),
+                lambda: ts(A("SM", 32, 48), A("SM", 32, 48), 8.0, OP.mult),
+                lambda: tt(A("NN"), A("SM", 32, 48), A("NP"), OP.add),
+                lambda: tt(A("PB"), G("GG", 16, *lst(EXP)), A("DLT"), OP.mult)]
+
+    def got_stacks():
+        for e in range(2):
+            mm(A("P7", 256 + e, 320, 2), UNF[e], A("RV"))
+        act(A("RA", 0, 64), A("P7", 256, 320))
+        act(A("RCV"), G("RA", RW, "RE", 0, 16))
+
+    for t in range(STEPS):
+        last = t == STEPS - 1
+        peer = T.cores[rank ^ (1 << (t % 2))]
+        MO, MI, LO, LI = "MO%d" % t, "MI%d" % t, "LO%d" % t, "LI%d" % t
+
+        act(A("XV"), G("X", 2049, "VU", 0, 16))
+        c0 = 0
+        for n in (2, 3, 3, 4, 4):
+            n = min(n, N1 - c0)
+            if n > 0:
+                act(A("XK", 256 * c0, 256 * (c0 + n)), G("X", 2049, "KT", 16 * c0, 16 * (c0 + n)))
+            c0 += n
+        for q in range(4):
+            tt(A("D", 1 + 512 * q, 513 + 512 * q), A("X", 1 + 512 * q, 513 + 512 * q), A("W%d" % q), OP.add)
+        if t == 0:
+            late_constants()
+            diffs(A("V16"), 16, "P5", "AV")
+            act(A("NX"), G("NN", 16, *lst(EXP)), AF.Relu, bias=-1.0)
+        mm(A("P7", 0, 256), A("NI32"), A("SPR"), True, False)
+        if t > 0:
+            mm(A("P7", 0, 256), A("I32"), A("PB"), False, False)
+            for hf in range(2):
+                mm(HF("P7", hf), HF("RCV", hf), A("I7"), False, False)
+        for hf in range(2):
+            mm(HF("P7", hf), HF("ST1", hf), A("I32"), False, hf == 1)
+        c0 = 0
+        for n in (2, 2, 4, 4, 2, 2):
+            act(A("DK", 256 * c0, 256 * (c0 + n)), G("D", 2049, "KT", 16 * c0, 16 * (c0 + n)))
+            c0 += n
+        act(A("C2"), A("P7", 0, 256), scale=-1.0)
+        P = A("P4", 0, 256)
+        Z = A("P4", 256, 512)
+
+        def XK(i):
+            return A("XK", 256 * i, 256 * i + 256)
+        tt(P, A("XV"), P, OP.add)
+        tt(Z, XK(1), XK(2), OP.max)
+        prev = XK(0)
+        own = list(range(N1, 16))
+        for i in range(3, N1):
+            if own and i % 2 == 1:
+                k = own.pop(0)
+                cur = A("S%d" % (k % 2))
+                tt(cur, G("X", 2049, "KT", 16 * k, 16 * k + 16), prev, OP.max)
+                prev = cur
+            c = P if (N1 - i) % 2 == 1 else Z
+            tt(c, XK(i), c, OP.max)
+        assert not own
+        later = unique(A("VB"), 16, "AV", "ZO")
+        tt(A("ZS"), prev, Z, OP.max)
+        later.pop(0)()
+        tt(P, A("ZS"), P, OP.max)
+        later.pop(0)()
+        tt(Z, P, A("WV"), OP.subtract)
+        later.pop(0)()
+        mm(A("P6", 0, 256), A("IB"), A("NX"), True, False)
+        mm(A("P6", 0, 256), A("IB"), A("CT"), False, False)
+        for i in range(16):
+            tt(A("CMP", 256 * i, 256 * i + 256), A("DK", 256 * i, 256 * i + 256), Z, OP.is_lt)
+            mm(A("P5", 0, 256), A("M0", 15 - i, 143 - i), A("CMP", 256 * i, 256 * i + 256), i == 0, i == 15)
+        mm(A("P7", 0, 256), A("NIB"), A("NX"), True, False)
+        cp(A("ZS"), Z)
+        zs = [0]
+
+        def zscat(n):
+            for _ in range(n):
+                b = zs[0]
+                if b < 16:
+                    cp(G("X", XW, "ZO", 2 * b, 2 * b + 1), A("ZS", 16 * b, 16 * b + 16))
+                    zs[0] += 1
+        act(A("HIT"), A("P5", 0, 256), AF.Sign)
+        for hf in range(2):
+            mm(HF("P6", hf), HF("HIT", hf), A("TT"), False, hf == 1)
+        for hf in range(2):
+            mm(HF("P7", hf), HF("HIT", hf), A("TH"), False, hf == 1)
+        mm(A("P5", 256, 512), A("IB"), A("NX"), True, False)
+        for hf in range(2):
+            mm(HF("P5", hf, 256), HF("HIT", hf), A("BO"), False, hf == 1)
+        act(A("RH"), A("P7", 0, 256), AF.Relu, bias=-61440.0, scale=4096.0)
+        act(A("FS"), A("P5", 256, 512), AF.Sign, bias=-8.5)
+        zscat(6)
+        ts(A("TI"), A("P6", 0, 256), SPREAD, OP.mult)
+        tt(A("P6", 256, 512), A("RH"), A("P6", 256, 512), OP.min)
+        ts(A("TA"), A("TI"), BITS, OP.bitwise_and)
+        mm(A("P4", 0, 256), A("IB"), A("ROW"), True, False)
+        mm(A("P4", 0, 128), HF("FS", 0), A("TRI"), False, False)
+        mm(A("P4", 128, 256), HF("FS", 0), A("ONE"), False, False)
+        mm(A("P4", 128, 256), HF("FS", 1), A("TRI"), False, True)
+        ts(A("NP"), A("P5", 256, 512, 16), 16.0, OP.min)
+        for c in range(4):
+            act(A("JK"), A("P4", 0, 256), AF.Sign, bias=C("JB", c), scale=-1.0, acc=C("SA", c))
+        act(A("FE"), A("P5", 256, 512), AF.Sign, bias=0.5, scale=-1.0)
+        tt(A("E0"), A("TA", 0, 256, 2), A("P6", 256, 512, 2), OP.add)
+        tt(A("P6", 0, 128), A("TA", 1, 256, 2), A("P6", 257, 512, 2), OP.add)
+        ts(A("FL", 0, 16), A("NP"), 8.5, OP.is_gt)
+        ts(A("FL", 16, 32), A("NP"), 0.5, OP.is_lt)
+        mm(A("P7", 0, 32), A("TXM"), A("FL"), True, False)
+        mm(A("P7", 8, 16), A("ONE"), A("FL", 0, 8), False, False)
+        mm(A("P7", 24, 32), A("ONE"), A("FL", 16, 24), False, True)
+        for k in range(4):
+            s = 16 - 16 * (k // 2)
+            mm(A("P7", 32 + 8 * k, 40 + 8 * k), A("ONE"), A("FL", s, s + 8), True, False)
+            mm(A("P7", 32 + 8 * k, 40 + 8 * k), A("ONE"), A("FL", s + 8, s + 16), False, True)
+        if not last:
+            mm(A("P5", 0, 256), A("BO"), A("HIT"), True, False)
+            for hf in range(2):
+                mm(HF("P5", hf), HF("NX", hf), A("IB"), False, hf == 1)
+            act(A("P5", 0, 256), A("P5", 0, 256), AF.Relu, bias=cCap, scale=4096.0)
+        for s in range(4):
+            e, o = "E%d" % (s % 2), 128 * (s % 2)
+            if s < 3:
+                e2, o2 = "E%d" % (1 - s % 2), 128 - o
+                for k, op in enumerate((OP.min, OP.max)):
+                    tt(A(e2, 64 * k, 64 * k + 64), A(e, 0, 128, 2), A("P6", o, o + 128, 2), op)
+                    tt(A("P6", o2 + 64 * k, o2 + 64 * k + 64), A(e, 1, 128, 2), A("P6", o + 1, o + 128, 2), op)
+            else:
+                for k, op in enumerate((OP.min, OP.max)):
+                    tt(HF("KY", k), A(e), A("P6", o, o + 128), op)
+            if s == 1:
+                ts(A(MO, 32, 64), A("P7", 32, 64), 64.0, OP.min, -64.0, OP.add)
+            elif s == 2:
+                zscat(1)
+            elif s == 3:
+                ts(A("SL"), A("SA"), 0.5, OP.mult, 128.0, OP.add)
+            else:
+                zscat(1)
+        tt(A("ST"), G("KY", 256, *lst(PERM)), A("C2"), OP.subtract)
+        for hf in range(2):
+            mm(HF("P4", hf), HF("ST", hf), A("I16"))
+        act(A("STA", 0, 256), A("P4", 0, 256))
+        zscat(6)
+        cp(A("GA"), G("STA", 264, "SL", 0, 4))
+        mm(A("P7", 128, 160), FOLD[0], A("GA", 0, 64, 2), True, False)
+        mm(A("P7", 128, 160), FOLD[1], A("GA", 1, 64, 2), False, True)
+        if not last:
+            tt(A("ST1"), A("STA", 0, 256), A("P5", 0, 256), OP.min)
+        else:
+            zscat(2)
+        cp(A(MO, 0, 32), A("P7", 128, 160))
+        send(MO, MI, "nm%d" % t, peer)
+        zscat(1)
+        cp(A("GU"), A("P7", 128, 160))
+        zscat(16)
+        act(A(LO, 256, 512), G("X", 2049, "GU", 16, 32))
+        cp(A(LO, 0, 256), G("X", 2049, "GU", 0, 16))
+        send(LO, LI, "la%d" % t, peer, 0, 256)
+        send(LO, LI, "lb%d" % t, peer, 256, 512)
+        for hf in range(2):
+            mm(A("P7", 64, 66), HF("FE", hf), A("ONE", 0, 2), hf == 0, hf == 1)
+        mm(A("P4", 256, 512), A("IB"), A("ROW"), True, False)
+        mm(A("P4", 256, 384), HF("FE", 0), A("TXM"), False, False)
+        mm(A("P4", 384, 512), HF("FE", 0), A("ONE"), False, False)
+        mm(A("P4", 384, 512), HF("FE", 1), A("TXM"), False, True)
+        if not last:
+            mm(A("P5", 256, 512), A("BO32"), A("STA", 0, 256), True, False)
+            mm(A("P5", 256, 512), A("NBO32"), A("ST1"), False, True)
+            act(A("OWB"), A("P5", 256, 512))
+        cp(A("CODE"), A("P7", 0, 32))
+        ts(A("MSK"), A("JT"), C("P7", 64), OP.is_lt)
+        ts(A("RE"), pick(A("P4", 256, 512)), cRe, OP.add, 0.5, OP.mult)
+
+        def shifted():
+            for hf in range(2):
+                mm(HF("P5", hf), HF("STA" if last else "ST1", hf), A("SI"))
+            act(A("DLT"), A("P5", 0, 256))
+        if last:
+            shifted()
+        tt(A("RV"), A(MI, 0, 32), A("MSK"), OP.mult)
+        if not last:
+            for e in range(2):
+                mm(A("P6", e, 64, 2), UN7[e], A("RV"))
+        cp(A("RU"), A("RV"))
+        act(A("OWN"), G("X", 2049, "RU", 0, 32))
+        diffs(A("RV"), 32, "P4", "AB")
+        hs, un = heights(t), unique(A("RV"), 32, "AB", "JO")
+        between = []
+        if not last:
+            hs.pop(0)()
+            cp(A("R7", 0, 64), A("P6", 0, 64))
+            hs.pop(0)()
+            tt(A("TM"), G("R7", RW, "RE", 0, 16), A("OWB"), OP.add)
+            hs.pop(0)()
+            names_to_lists(A("TM"))
+            un.pop(0)()
+            hs.pop(0)()
+            for f in un:
+                f()
+            shifted()
+            own_vertex()
+            got_stacks()
+            diffs(A("V16"), 16, "P5", "AV")
+            act(A("NX"), G("NN", 16, *lst(EXP)), AF.Relu, bias=-1.0)
+            between = neighbour_tiles() + hs
+        else:
+            got_stacks()
+            for f in hs:
+                f()
+            mm(A("P7", 0, 256), A("I32"), A("STA", 0, 256), True, False)
+            mm(A("P7", 0, 256), A("I32"), A("RCV"), False, False)
+            for hf in range(2):
+                mm(HF("P7", hf), HF("PB", hf), A("I32"), False, hf == 1)
+            for hf in range(2):
+                mm(A("P6", 128 * hf, 128 * hf + 128, p=8), A("NN", 8 * hf, 8 * hf + 8), A("I32"))
+            act(A("YS"), A("P7", 0, 256), AF.Relu, bias=-1.0)
+            act(A("YC", p=8), A("P6", 0, 256, p=8))
+            dma("s", H(T.ystk[:, :]), A("YS"))
+            dma("s", H(T.ycnt[:, :]), A("YC", p=8))
+            for f in un:
+                f()
+        for c in range(32):
+            tt(G("X", XW, "JO", 2 * c, 2 * c + 1), A("OWN", 16 * c, 16 * c + 16), A(LI, 16 * c, 16 * c + 16), OP.max)
+            if between:
+                between.pop(0)()
+
+    for q in range(4):
+        o, a = A("DK", 512 * q, 512 * q + 512), A("X", 1 + 512 * q, 513 + 512 * q)
+        if q % 2 == 0:
+            ts(o, a, -1.0, OP.mult)
+            dma("s", H(T.ylab[:, 512 * q:512 * q + 512]), o)
+        else:
+            act(o, a, AF.Copy, scale=-1.0)
+            dma("a", H(T.ylab[:, 512 * q:512 * q + 512]), o)
+
+    emit(g, T, Q, ops, nsent[0])
+
+
+def emit(g, T, Q, ops, nsent):
+    touch = {}
+    know = {e: {} for e in Q}
+    for j, o in enumerate(ops):
+        e = o["e"]
+        o["id"] = e if o["k"] == "c" else ("u", j)
+        deps = set()
+        for acc, isw in ((o["r"], False), (o["w"], True)):
+            for (n, lo, hi, st) in acc:
+                for (i, w, l2, h2, s2) in touch.get(n, ()):
+                    p = ops[i]
+                    same = p["e"] == e and p["k"] == "c" and o["k"] == "c"
+                    over = lo < h2 and l2 < hi and not (st == s2 and (lo - l2) % st)
+                    if same:
+                        if e != "p" and over and (w or isw):
+                            deps.add(i)
+                    elif p["k"] == "r":
+                        continue
+                    elif (over and (w or isw)) or n in PSUM:
+                        deps.add(i)
+        for acc, isw in ((o["r"], False), (o["w"], True)):
+            for (n, lo, hi, st) in acc:
+                touch.setdefault(n, []).append((j, isw, lo, hi, st))
+        o["wait"] = []
+        if e == "x":
+            o["clock"] = {}
+            continue
+        kn = know[e]
+        for i in sorted(deps, reverse=True):
+            p = ops[i]
+            if kn.get(p["id"], -1) >= i:
+                continue
+            o["wait"].append(i)
+            p["need"] = True
+            kn[p["id"]] = i
+            for k, v in p["clock"].items():
+                if kn.get(k, -1) < v:
+                    kn[k] = v
+        o["clock"] = dict(kn)
+    cnt = {e: 0 for e in Q}
+    for o in ops:
+        if o["k"] == "c":
+            if o.get("need"):
+                cnt[o["e"]] += 1
+                o["tok"] = ("e" + o["e"], cnt[o["e"]])
+        elif o["k"] == "d":
+            o["tok"] = (o["sem"], 16)
+        elif o["k"] == "x":
+            o["tok"] = o["sem"]
+    for o in ops:
+        if o["k"] == "x":
+            continue
+        for i in o["wait"]:
+            s, v = ops[i]["tok"]
+            Q[o["e"]].wait_ge(T.sem[s], v)
+        ins = o["fn"]()
+        if o["k"] == "d" or (o["k"] == "c" and o.get("need")):
+            ins.then_inc(T.sem[o["tok"][0]], 16 if o["k"] == "d" else 1)
+    for e in "vapg":
+        if cnt[e]:
+            g.wait_ge(T.sem["e" + e], cnt[e])
+    g.wait_ge(T.sem.sent, nsent)
+    for o in ops:
+        if o["k"] == "d" or o["k"] == "x":
+            g.wait_ge(T.sem[o["tok"][0]], o["tok"][1])

@@ -3,7 +3,10 @@ from concourse.mybir import AluOpType, ActivationFunctionType
 NM = "float16"
 N1 = 13
 STEPS = 4
-XW = 2080
+XW = 2096
+GLDD = False
+ZG = (5, 1, 4, 0)
+PRE = 2
 RW = 328
 
 F, B, I, U = "float32", "bfloat16", "int32", "uint16"
@@ -12,13 +15,13 @@ _S = {
     "STI": (256, I), "STF": (256, F), "XK": (256 * N1, F), "XV": (256, F), "DK": (4096, F), "CMP": (4096, B),
     "PI": (8, I), "COL": (24, F), "IM": (256, F), "IS": (256, F), "LDD": (2048, NM), "FU": (768, NM),
     "M0": (144, B), "CT": (256, B), "ROW": (256, B), "DA": (32, F), "HOLD": (256, F),
-    "LST": (64, U), "SPI": (256, I), "SPJ": (256, I), "SPR": (256, F), "C4K": (512, F), "JB": (4, F), "JT": (32, F),
+    "LST": (64, U), "SPI": (16, I), "SPJ": (16, I), "KP": (16, F), "L1": (2048, NM), "L2": (2048, NM), "SPR": (256, F), "C4K": (512, F), "JB": (4, F), "JT": (32, F),
     "VB": (16, F), "V16": (16, NM), "VJ": (32, U), "VU": (16, U), "KJ": (512, F), "KJT": (512, F),
-    "KA": (256, F), "KT": (256, U), "WV": (256, F), "AB": (512, F), "AV": (256, F), "SC": (512, F), "SM": (48, F),
+    "KA": (256, F), "KT": (256, U), "WV": (256, F), "AB": (512, F), "AV": (256, F), "SC": (512, F), "SM": (64, F), "DIF": (16, NM), "T16": (128, NM),
     "ZO": (32, U), "JO": (64, U), "S0": (256, F), "S1": (256, F), "ZS": (256, F), "HIT": (256, B), "TI": (256, I),
     "TA": (256, I), "RH": (256, F), "E0": (128, F), "E1": (128, F), "KY": (256, F), "ST": (256, NM), "ST1": (256, F),
     "C2": (256, F), "TM": (256, F), "OWB": (256, F), "DLT": (256, F), "NP": (16, F), "NN": (16, F), "NX": (256, B),
-    "FL": (32, B), "CODE": (32, F), "GG": (32, F), "FS": (256, B), "FE": (256, B), "JK": (256, B), "SA": (4, F),
+    "FL": (32, B), "CODE": (32, F), "GG": (32, F), "FS": (256, B), "FE": (256, B), "JK": (1024, B), "SA": (4, F),
     "SL": (4, U), "STA": (264, F), "GA": (64, NM), "GU": (32, U), "RE": (16, U), "MSK": (32, F), "RV": (32, NM),
     "RU": (32, U), "R7": (RW, F), "RA": (RW, F), "RCV": (256, F), "OWN": (512, F), "PB": (256, F), "YS": (256, F),
     "YC": (256, F), "CNI": (256, I), "CNF": (256, F),
@@ -164,7 +167,6 @@ def rank_program(g, core, T, topo):
     ms(A("ONE32"), 1.0)
     ms(A("ONE"), 1.0)
     ms(A("NONE"), -1.0)
-    ms(A("C4K"), 4096.0)
     sel(A("I32"), A("ONE32"), OP.is_equal, 0.0)
     for k, m in enumerate((15, 112, 16, 8)):
         ts(C("PI", 1 + k), C("PI", 0), m, OP.bitwise_and)
@@ -185,13 +187,19 @@ def rank_program(g, core, T, topo):
     cp(A("LST", 0, 16), A("IM", 0, 16))
     ts(A("LST", 32, 48), A("IM", 0, 16), cPick, OP.add)
     ts(A("HOLD"), A("HOLD"), -4096.0, OP.add)
+    ts(A("DA", 0, 16), A("IM", 0, 16), cA, OP.is_equal)
+    cA4 = col(22, cA, -4096.0, 0.0)
+    if not GLDD:
+        ts(A("DA", 16, 32), A("IM", 0, 16), cA, OP.is_equal, -1.0, OP.add)
+    cBig = col(15, C("DA", 15), -1048576.0, -4096.0)
+    cCap = col(19, cA, -4096.0, cBig)
+    act(A("NBO32"), A("BO32"), scale=-1.0)
     sel(A("T2"), A("BO32"), OP.not_equal, -1.0)
     sel(A("IB"), A("ONE"), OP.is_equal, 0.0)
     sel(A("NIB"), A("NONE"), OP.is_equal, 0.0)
     iota(A("CT"), [[0, 16], [-1, 16]], 15)
     act(A("BO"), A("BO32"))
     act(A("NBO"), A("BO32"), scale=-1.0)
-    act(A("NBO32"), A("BO32"), scale=-1.0)
     act(A("NI32"), A("I32"), scale=-1.0)
     sel(A("BT"), A("BO"), OP.is_gt, 0.0)
     sel(A("NBT"), A("NBO"), OP.is_gt, 0.0)
@@ -202,6 +210,19 @@ def rank_program(g, core, T, topo):
     sel(A("TRX"), A("ONE"), OP.is_gt, 0.0)
     sel(A("TXM"), A("TRX"), OP.not_equal, -64.0)
     iota(A("ROW"), [[1, 256]], 1)
+    if GLDD:
+        for o, a, pat, cm, op, fill in (("L1", "LDD", [[-1, 16], [-16, 8], [0, 16]], 1, OP.is_equal, 0.0),
+                                        ("L2", "L1", [[0, 16], [-1, 128]], 1, OP.not_equal, -1.0),
+                                        ("LDD", "L2", [[-33, 16], [-512, 8], [1, 16]], 32, OP.not_equal, 0.0)):
+            if o == "L1":
+                ms(A("LDD"), 1.0)
+            (lambda o, a, pat, cm, op, fill: add("g", lambda: g.affine_select(o[0], a[0], pat, op, fill, 0, cm), [o], [a]))(
+                A(o), A(a), pat, cm, op, fill)
+    iota(A("C4K"), [[0, 512]], 4096)
+    iota(A("STA", 256, 264), [[0, 8]])
+    iota(A("R7", 64, RW), [[0, RW - 64]])
+    iota(A("RA", 64, RW), [[0, RW - 64]])
+    iota(A("X", 2049, XW), [[0, XW - 2049]])
 
     def lst(k):
         return ("LST", k, k + 16)
@@ -221,12 +242,12 @@ def rank_program(g, core, T, topo):
 
     def neighbour_tiles():
         def tr(q):
-            o, a = A("KJT", 128 * q, 128 * q + 128), A("KJ", 128 * q, 128 * q + 128)
+            o, a = A("KJT", 256 * q, 256 * q + 256), A("KJ", 256 * q, 256 * q + 256)
             add("v", lambda: g.vector.transpose(o[0], a[0]), [o], [a])
 
         def pk(q):
-            cp(A("KT", 64 * q, 64 * q + 64), G("KJT", 512, "LST", PICK + 4 * q, PICK + 4 * q + 4))
-        return [(lambda f, q: lambda: f(q))(f, q) for f in (tr, pk) for q in range(4)]
+            cp(A("KT", 128 * q, 128 * q + 128), G("KJT", 512, "LST", PICK + 8 * q, PICK + 8 * q + 8))
+        return [(lambda f, q: lambda: f(q))(f, q) for f in (tr, pk) for q in range(2)]
 
     def own_vertex():
         act(A("WV"), G("WB", 2049, "VU", 0, 16))
@@ -250,67 +271,69 @@ def rank_program(g, core, T, topo):
     mm(A("P5", 0, 256), A("E8", p=8), A("CNF", p=8))
     for hf in range(2):
         mm(A("P7", 8 * hf, 8 * hf + 8), A("CNF", 128 * hf, 128 * hf + 128, p=8), A("I32", 0, 8, p=8))
-    ts(A("TM"), A("P5", 0, 256), cA1, OP.is_equal)
-    ts(A("OWB"), A("P5", 0, 256), cA1, OP.is_gt)
-    tt(A("TM"), A("TM"), A("STF"), OP.mult)
-    mm(A("P5", 256, 512), A("BO32"), A("TM"))
+    act(A("P6", 0, 256), A("P5", 0, 256), AF.Relu, bias=cA4, scale=4096.0)
+    act(A("P4", 0, 256), A("P5", 0, 256), AF.Relu, bias=cCap, scale=4096.0)
+    tt(A("TM"), A("STF"), A("P6", 0, 256), OP.min)
+    tt(A("ST1"), A("STF"), A("P4", 0, 256), OP.min)
+    mm(A("P5", 256, 512), A("BO32"), A("TM"), True, False)
+    mm(A("P5", 256, 512), A("NBO32"), A("ST1"), False, True)
+    cp(A("NN"), A("P7", 0, 16))
     ms(A("NB", 0, 1), 0.0)
     ts(A("NB", 1, 1025), A("NBI", 0, 1024), 1.0, OP.add)
-    tt(A("ST1"), A("OWB"), A("STF"), OP.mult)
-    cp(A("NN"), A("P7", 0, 16))
     ts(A("NB", 1025, 2049), A("NBI", 1024, 2048), 1.0, OP.add)
     names_to_lists(A("P5", 256, 512))
     own_vertex()
     for q in range(4):
         act(A("W%d" % q), A("WB", 1 + 512 * q, 513 + 512 * q))
     ms(A("X", 0, 1), 0.0)
-    ms(A("X", 2049, XW), 0.0)
     ms(A("D", 0, 1), 1.0)
-    ts(A("DA", 0, 16), A("IM", 0, 16), cA, OP.is_equal)
-    ts(A("DA", 16, 32), A("IM", 0, 16), cA, OP.is_equal, -1.0, OP.add)
-    for a in range(16):
-        ts(A("LDD", 128 * a, 128 * a + 128), A("T2"), C("DA", 16 + a), OP.max, C("DA", a), OP.min)
-    for f in neighbour_tiles():
-        f()
-    for q in range(2):
-        ts(A("X", 1 + 1024 * q, 1025 + 1024 * q), A("LABI", 1024 * q, 1024 * q + 1024), -1.0, OP.mult)
+    if not GLDD:
+        cp(A("T16"), A("T2"))
+        for a in range(16):
+            ts(A("LDD", 128 * a, 128 * a + 128), A("T16"), C("DA", 16 + a), OP.max, C("DA", a), OP.min)
     cDum = C("COL", 7)
-    cCap = C("COL", 19)
     cRe = C("COL", 20)
+
+    def first_tables():
+        for f in neighbour_tiles():
+            f()
+        for q in range(2):
+            ts(A("X", 1 + 1024 * q, 1025 + 1024 * q), A("LABI", 1024 * q, 1024 * q + 1024), -1.0, OP.mult)
 
     def late_constants():
         col(7, cA, 1.0, 2049.0)
         cA16 = col(8, cA, 16.0, 0.0)
         cG15 = col(10, cG, 1.0, 15.0)
-        ts(A("SPI"), A("IS"), -1.0, OP.add, SPREAD, OP.mult)
+        ts(A("SPI"), A("IM", 0, 16), SPREAD, OP.mult)
+        ts(A("LST", 48, 64), A("IM", 0, 16), 0.0, OP.mult, cA, OP.add)
         ts(A("SPJ"), A("SPI"), BITS, OP.bitwise_and)
         ts(A("M0"), A("IM", 0, 144), cG15, OP.is_equal)
-        cp(A("SPR"), A("SPJ"))
+        cp(A("KP"), A("SPJ"))
+        act(A("SPR"), G("KP", 16, *lst(48)))
         ts(A("LST", 16, 32), A("IM", 0, 16), cA16, OP.add)
         cp(A("I16"), A("I32"))
-        ts(A("I7"), A("I32"), C("DA", 23), OP.mult, -1.0, OP.mult)
         cP8 = col(11, cP, 1.0, 8.0)
         cM8 = col(12, cP, 1.0, -8.0)
         cGe = col(13, c8, 0.125, 0.0)
         cLt = col(14, c8, -0.125, 1.0)
         cJ = col(16, cA, 2.0, 1.0)
         cJT = col(17, c8, 0.25, -256.0)
-        cBig = col(15, C("DA", 15), -1048576.0, -4096.0)
         col(20, cWin, 1.0, 63.0)
         im = A("IM", 0, 128)
         ts(A("FU", 0, 128), im, cP, OP.is_equal, cLt, OP.mult)
         ts(A("FU", 128, 256), im, cP8, OP.is_equal, cLt, OP.mult)
-        ts(A("FU", 256, 384), im, cM8, OP.is_equal, cGe, OP.mult)
-        col(19, cA, -4096.0, cBig)
-        for e in range(2):
-            ts(A("FU", 384 + 128 * e, 512 + 128 * e), A("BO32"), C("DA", 8 * e + 7), OP.mult)
-        tt(A("SI"), A("FU", 256, 384), A("I32"), OP.subtract)
         ts(A("JB"), A("IM", 0, 4), 32.0, OP.mult, cJ, OP.add)
-        ts(A("JT"), A("IM", 0, 32), 4.0, OP.mult, cJT, OP.add)
-        ms(A("STA", 256, 264), 0.0)
-        ms(A("R7", 64, RW), 0.0)
-        ms(A("RA", 64, RW), 0.0)
         tt(A("TT"), A("BT"), A("D2"), OP.add)
+
+        def last_constants():
+            ts(A("FU", 256, 384), im, cM8, OP.is_equal, cGe, OP.mult)
+            ts(A("JT"), A("IM", 0, 32), 4.0, OP.mult, cJT, OP.add)
+            tt(A("SI"), A("FU", 256, 384), A("I32"), OP.subtract)
+            for e in range(2):
+                ts(A("FU", 384 + 128 * e, 512 + 128 * e), A("BO32"), C("DA", 8 * e + 7), OP.mult)
+            ts(A("I7"), A("I32"), col(23, C("DA", 7), -1.0, 1.0), OP.mult)
+            col(21, cA, 1.0, 2065.0)
+        return last_constants
     FOLD = [A("FU", 0, 128), A("FU", 128, 256)]
     UNF = [A("FU", 0, 128), A("FU", 256, 384)]
     UN7 = [A("FU", 384, 512), A("FU", 512, 640)]
@@ -328,6 +351,7 @@ def rank_program(g, core, T, topo):
         act(A("RA", 0, 64), A("P7", 256, 320))
         act(A("RCV"), G("RA", RW, "RE", 0, 16))
 
+    first_tables()
     for t in range(STEPS):
         last = t == STEPS - 1
         peer = T.cores[rank ^ (1 << (t % 2))]
@@ -343,7 +367,7 @@ def rank_program(g, core, T, topo):
         for q in range(4):
             tt(A("D", 1 + 512 * q, 513 + 512 * q), A("X", 1 + 512 * q, 513 + 512 * q), A("W%d" % q), OP.add)
         if t == 0:
-            late_constants()
+            last_constants = late_constants()
             diffs(A("V16"), 16, "P5", "AV")
             act(A("NX"), G("NN", 16, *lst(EXP)), AF.Relu, bias=-1.0)
         mm(A("P7", 0, 256), A("NI32"), A("SPR"), True, False)
@@ -408,17 +432,18 @@ def rank_program(g, core, T, topo):
             mm(HF("P5", hf, 256), HF("HIT", hf), A("BO"), False, hf == 1)
         act(A("RH"), A("P7", 0, 256), AF.Relu, bias=-61440.0, scale=4096.0)
         act(A("FS"), A("P5", 256, 512), AF.Sign, bias=-8.5)
-        zscat(6)
+        zscat(ZG[0])
         ts(A("TI"), A("P6", 0, 256), SPREAD, OP.mult)
-        tt(A("P6", 256, 512), A("RH"), A("P6", 256, 512), OP.min)
+        zscat(ZG[1])
         ts(A("TA"), A("TI"), BITS, OP.bitwise_and)
+        tt(A("P6", 256, 512), A("RH"), A("P6", 256, 512), OP.min)
         mm(A("P4", 0, 256), A("IB"), A("ROW"), True, False)
         mm(A("P4", 0, 128), HF("FS", 0), A("TRI"), False, False)
         mm(A("P4", 128, 256), HF("FS", 0), A("ONE"), False, False)
         mm(A("P4", 128, 256), HF("FS", 1), A("TRI"), False, True)
         ts(A("NP"), A("P5", 256, 512, 16), 16.0, OP.min)
         for c in range(4):
-            act(A("JK"), A("P4", 0, 256), AF.Sign, bias=C("JB", c), scale=-1.0, acc=C("SA", c))
+            act(A("JK", 256 * c, 256 * c + 256), A("P4", 0, 256), AF.Sign, bias=C("JB", c), scale=-1.0, acc=C("SA", c))
         act(A("FE"), A("P5", 256, 512), AF.Sign, bias=0.5, scale=-1.0)
         tt(A("E0"), A("TA", 0, 256, 2), A("P6", 256, 512, 2), OP.add)
         tt(A("P6", 0, 128), A("TA", 1, 256, 2), A("P6", 257, 512, 2), OP.add)
@@ -448,8 +473,6 @@ def rank_program(g, core, T, topo):
                     tt(HF("KY", k), A(e), A("P6", o, o + 128), op)
             if s == 1:
                 ts(A(MO, 32, 64), A("P7", 32, 64), 64.0, OP.min, -64.0, OP.add)
-            elif s == 2:
-                zscat(1)
             elif s == 3:
                 ts(A("SL"), A("SA"), 0.5, OP.mult, 128.0, OP.add)
             else:
@@ -458,7 +481,7 @@ def rank_program(g, core, T, topo):
         for hf in range(2):
             mm(HF("P4", hf), HF("ST", hf), A("I16"))
         act(A("STA", 0, 256), A("P4", 0, 256))
-        zscat(6)
+        zscat(ZG[2])
         cp(A("GA"), G("STA", 264, "SL", 0, 4))
         mm(A("P7", 128, 160), FOLD[0], A("GA", 0, 64, 2), True, False)
         mm(A("P7", 128, 160), FOLD[1], A("GA", 1, 64, 2), False, True)
@@ -481,20 +504,20 @@ def rank_program(g, core, T, topo):
         mm(A("P4", 256, 384), HF("FE", 0), A("TXM"), False, False)
         mm(A("P4", 384, 512), HF("FE", 0), A("ONE"), False, False)
         mm(A("P4", 384, 512), HF("FE", 1), A("TXM"), False, True)
+        if t == 0:
+            cp(A("T16"), A("BO32"))
         if not last:
-            mm(A("P5", 256, 512), A("BO32"), A("STA", 0, 256), True, False)
-            mm(A("P5", 256, 512), A("NBO32"), A("ST1"), False, True)
+            tt(A("ST"), A("STA", 0, 256), A("ST1"), OP.subtract)
+            mm(A("P5", 256, 512), A("T16"), A("ST"))
             act(A("OWB"), A("P5", 256, 512))
+        if t == 0:
+            last_constants()
         cp(A("CODE"), A("P7", 0, 32))
         ts(A("MSK"), A("JT"), C("P7", 64), OP.is_lt)
         ts(A("RE"), pick(A("P4", 256, 512)), cRe, OP.add, 0.5, OP.mult)
-
-        def shifted():
-            for hf in range(2):
-                mm(HF("P5", hf), HF("STA" if last else "ST1", hf), A("SI"))
-            act(A("DLT"), A("P5", 0, 256))
-        if last:
-            shifted()
+        for hf in range(2):
+            mm(HF("P5", hf), HF("STA" if last else "ST1", hf), A("SI"))
+        act(A("DLT"), A("P5", 0, 256))
         tt(A("RV"), A(MI, 0, 32), A("MSK"), OP.mult)
         if not last:
             for e in range(2):
@@ -502,7 +525,17 @@ def rank_program(g, core, T, topo):
         cp(A("RU"), A("RV"))
         act(A("OWN"), G("X", 2049, "RU", 0, 32))
         diffs(A("RV"), 32, "P4", "AB")
-        hs, un = heights(t), unique(A("RV"), 32, "AB", "JO")
+        tt(A("DIF"), A("RV", 1, 32, 2), A("RV", 0, 32, 2), OP.subtract)
+        for a in range(16):
+            mm(A("P5", a, 256, 16), A("LDD", 128 * a, 128 * a + 128), A("RV", 1, 32, 2), True, False)
+            mm(A("P5", a, 256, 16), A("I16"), A("DIF"), False, True)
+        hs = heights(t)
+        un = unique(A("RV"), 32, "AB", "JO")[0:2] + [
+            lambda: ts(A("JO", 1, 32, 2), A("SM", 1, 32, 2), cWin, OP.add, C("COL", 21), OP.min),
+            lambda: scan(A("S0"), A("C4K", 0, 256), A("AV"), 0.0, OP.add, OP.min),
+            lambda: ts(A("SM", 48, 64), A("S0", 15, 256, 16), 65536.0, OP.is_lt, 8192.0, OP.mult),
+            lambda: tt(A("SM", 48, 64), A("SM", 48, 64), A("SM", 0, 32, 2), OP.add),
+            lambda: ts(A("JO", 0, 32, 2), A("SM", 48, 64), cWin, OP.add, cDum, OP.min)]
         between = []
         if not last:
             hs.pop(0)()
@@ -511,17 +544,21 @@ def rank_program(g, core, T, topo):
             tt(A("TM"), G("R7", RW, "RE", 0, 16), A("OWB"), OP.add)
             hs.pop(0)()
             names_to_lists(A("TM"))
-            un.pop(0)()
-            hs.pop(0)()
-            for f in un:
+            act(A("AV"), A("P5", 0, 256), AF.Abs, scale=131072.0)
+            nt = neighbour_tiles()
+            for f in (un[0], hs[0], un[1], hs[1], un[2]):
                 f()
-            shifted()
+            for k in range(4):
+                if k < PRE:
+                    nt[k]()
+                un[3 + k]()
             own_vertex()
             got_stacks()
             diffs(A("V16"), 16, "P5", "AV")
             act(A("NX"), G("NN", 16, *lst(EXP)), AF.Relu, bias=-1.0)
-            between = neighbour_tiles() + hs
+            between = nt[PRE:]
         else:
+            act(A("AV"), A("P5", 0, 256), AF.Abs, scale=131072.0)
             got_stacks()
             for f in hs:
                 f()
@@ -537,8 +574,8 @@ def rank_program(g, core, T, topo):
             dma("s", H(T.ycnt[:, :]), A("YC", p=8))
             for f in un:
                 f()
-        for c in range(32):
-            tt(G("X", XW, "JO", 2 * c, 2 * c + 1), A("OWN", 16 * c, 16 * c + 16), A(LI, 16 * c, 16 * c + 16), OP.max)
+        for c in range(16):
+            tt(G("X", XW, "JO", 2 * c, 2 * c + 2), A("OWN", 32 * c, 32 * c + 32), A(LI, 32 * c, 32 * c + 32), OP.max)
             if between:
                 between.pop(0)()
 

@@ -1,11 +1,12 @@
 from concourse.mybir import AluOpType, ActivationFunctionType
 
 NM = "float16"
-N1 = 13
+N1 = 11
+DQ = 1
 STEPS = 4
 XW = 2096
-GLDD = False
-ZG = (5, 1, 4, 0)
+EARLY = True
+ZG = (3, 1, 2, 0)
 PRE = 2
 RW = 328
 
@@ -15,9 +16,9 @@ _S = {
     "STI": (256, I), "STF": (256, F), "XK": (256 * N1, F), "XV": (256, F), "DK": (4096, F), "CMP": (4096, B),
     "PI": (8, I), "COL": (24, F), "IM": (256, F), "IS": (256, F), "LDD": (2048, NM), "FU": (768, NM),
     "M0": (144, B), "CT": (256, B), "ROW": (256, B), "DA": (32, F), "HOLD": (256, F),
-    "LST": (64, U), "SPI": (16, I), "SPJ": (16, I), "KP": (16, F), "L1": (2048, NM), "L2": (2048, NM), "SPR": (256, F), "C4K": (512, F), "JB": (4, F), "JT": (32, F),
+    "LST": (64, U), "SPI": (16, I), "SPJ": (16, I), "KP": (16, F), "SPR": (256, F), "C4K": (512, B), "JB": (4, F), "JT": (32, F),
     "VB": (16, F), "V16": (16, NM), "VJ": (32, U), "VU": (16, U), "KJ": (512, F), "KJT": (512, F),
-    "KA": (256, F), "KT": (256, U), "WV": (256, F), "AB": (512, F), "AV": (256, F), "SC": (512, F), "SM": (64, F), "DIF": (16, NM), "T16": (128, NM),
+    "KA": (256, F), "KT": (256, U), "WV": (256, F), "AB": (512, B), "AV": (256, B), "SC": (256, F), "SB": (768, B), "SM": (64, F), "DIF": (16, F), "T16": (128, NM),
     "ZO": (32, U), "JO": (64, U), "S0": (256, F), "S1": (256, F), "ZS": (256, F), "HIT": (256, B), "TI": (256, I),
     "TA": (256, I), "RH": (256, F), "E0": (128, F), "E1": (128, F), "KY": (256, F), "ST": (256, NM), "ST1": (256, F),
     "C2": (256, F), "TM": (256, F), "OWB": (256, F), "DLT": (256, F), "NP": (16, F), "NN": (16, F), "NX": (256, B),
@@ -189,8 +190,7 @@ def rank_program(g, core, T, topo):
     ts(A("HOLD"), A("HOLD"), -4096.0, OP.add)
     ts(A("DA", 0, 16), A("IM", 0, 16), cA, OP.is_equal)
     cA4 = col(22, cA, -4096.0, 0.0)
-    if not GLDD:
-        ts(A("DA", 16, 32), A("IM", 0, 16), cA, OP.is_equal, -1.0, OP.add)
+    ts(A("DA", 16, 32), A("IM", 0, 16), cA, OP.is_equal, -1.0, OP.add)
     cBig = col(15, C("DA", 15), -1048576.0, -4096.0)
     cCap = col(19, cA, -4096.0, cBig)
     act(A("NBO32"), A("BO32"), scale=-1.0)
@@ -210,14 +210,6 @@ def rank_program(g, core, T, topo):
     sel(A("TRX"), A("ONE"), OP.is_gt, 0.0)
     sel(A("TXM"), A("TRX"), OP.not_equal, -64.0)
     iota(A("ROW"), [[1, 256]], 1)
-    if GLDD:
-        for o, a, pat, cm, op, fill in (("L1", "LDD", [[-1, 16], [-16, 8], [0, 16]], 1, OP.is_equal, 0.0),
-                                        ("L2", "L1", [[0, 16], [-1, 128]], 1, OP.not_equal, -1.0),
-                                        ("LDD", "L2", [[-33, 16], [-512, 8], [1, 16]], 32, OP.not_equal, 0.0)):
-            if o == "L1":
-                ms(A("LDD"), 1.0)
-            (lambda o, a, pat, cm, op, fill: add("g", lambda: g.affine_select(o[0], a[0], pat, op, fill, 0, cm), [o], [a]))(
-                A(o), A(a), pat, cm, op, fill)
     iota(A("C4K"), [[0, 512]], 4096)
     iota(A("STA", 256, 264), [[0, 8]])
     iota(A("R7", 64, RW), [[0, RW - 64]])
@@ -231,8 +223,9 @@ def rank_program(g, core, T, topo):
         scan(A("SC", 0, 256), A("HOLD"), src, 0.0, OP.add, OP.min)
         return A("SC", 15, 256, 16)
 
-    def names_to_lists(src):
+    def names_to_lists(src, meanwhile=lambda: None):
         picked = pick(src)
+        meanwhile()
         for f in range(2):
             ts(A("VJ", f, 32, 2), picked, cWin, OP.add)
         act(A("KJ"), G("NB", 2049, "VJ", 0, 32))
@@ -240,14 +233,16 @@ def rank_program(g, core, T, topo):
         ts(A("V16"), picked, cWin, OP.add)
         ts(A("VB"), picked, cWin, OP.add)
 
-    def neighbour_tiles():
+    def neighbour_tiles(n):
         def tr(q):
-            o, a = A("KJT", 256 * q, 256 * q + 256), A("KJ", 256 * q, 256 * q + 256)
+            w = 512 // n
+            o, a = A("KJT", w * q, w * q + w), A("KJ", w * q, w * q + w)
             add("v", lambda: g.vector.transpose(o[0], a[0]), [o], [a])
 
         def pk(q):
-            cp(A("KT", 128 * q, 128 * q + 128), G("KJT", 512, "LST", PICK + 8 * q, PICK + 8 * q + 8))
-        return [(lambda f, q: lambda: f(q))(f, q) for f in (tr, pk) for q in range(2)]
+            w = 16 // n
+            cp(A("KT", 16 * w * q, 16 * w * (q + 1)), G("KJT", 512, "LST", PICK + w * q, PICK + w * q + w))
+        return [(lambda f, q: lambda: f(q))(f, q) for f in (tr, pk) for q in range(n)]
 
     def own_vertex():
         act(A("WV"), G("WB", 2049, "VU", 0, 16))
@@ -262,9 +257,25 @@ def rank_program(g, core, T, topo):
         act(A(out, 0, 16 * n), A(bank, 0, 16 * n), AF.Abs, scale=131072.0)
 
     def unique(src, n, ab, out):
-        return [lambda: scan(A("SC", 0, 16 * n), A("C4K", 0, 16 * n), A(ab, 0, 16 * n), 0.0, OP.add, OP.min),
-                lambda: tt(A("SM", 0, n), src, A("SC", 15, 16 * n, 16), OP.subtract),
+        return [lambda: scan(A("SB", 0, 16 * n), A("C4K", 0, 16 * n), A(ab, 0, 16 * n), 0.0, OP.add, OP.min),
+                lambda: tt(A("SM", 0, n), src, A("SB", 15, 16 * n, 16), OP.subtract),
                 lambda: ts(A(out, 0, 2 * n, 2), A("SM", 0, n), cWin, OP.add, cDum, OP.min)]
+
+    def vertex_pairs():
+        tt(A("DIF", 0, 8), A("VB", 1, 16, 2), A("VB", 0, 16, 2), OP.subtract)
+        cp(A("ST", 0, 128), G("DIF", 16, "LST", EXP, EXP + 8))
+        mm(A("P5", 256, 384), A("I16"), A("ST", 0, 128), True, False)
+        for a in range(16):
+            mm(A("P5", 256 + a, 384, 16), A("LDD", 128 * a, 128 * a + 128), A("V16", 1, 16, 2), False, a == 15)
+        act(A("AB", 0, 128), A("P5", 256, 384), AF.Abs, scale=131072.0)
+
+    def unique_vertices():
+        return unique(A("VB"), 16, "AV", "ZO")[0:2] + [
+            lambda: scan(A("SB", 512, 640), A("C4K", 0, 128), A("AB", 0, 128), 0.0, OP.add, OP.min),
+            lambda: ts(A("ZO", 1, 16, 2), A("SM", 1, 16, 2), cWin, OP.add, C("COL", 21), OP.min),
+            lambda: ts(A("SM", 48, 56), A("SB", 527, 640, 16), 65536.0, OP.is_lt, 8192.0, OP.mult),
+            lambda: tt(A("SM", 48, 56), A("SM", 48, 56), A("SM", 0, 16, 2), OP.add),
+            lambda: ts(A("ZO", 0, 16, 2), A("SM", 48, 56), cWin, OP.add, cDum, OP.min)]
 
     cp(A("CNF", p=8), A("CNI", p=8))
     ts(A("STF"), A("STI"), 1.0, OP.add)
@@ -273,6 +284,11 @@ def rank_program(g, core, T, topo):
         mm(A("P7", 8 * hf, 8 * hf + 8), A("CNF", 128 * hf, 128 * hf + 128, p=8), A("I32", 0, 8, p=8))
     act(A("P6", 0, 256), A("P5", 0, 256), AF.Relu, bias=cA4, scale=4096.0)
     act(A("P4", 0, 256), A("P5", 0, 256), AF.Relu, bias=cCap, scale=4096.0)
+    cp(A("T16"), A("T2"))
+    ms(A("X", 0, 1), 0.0)
+    ms(A("D", 0, 1), 1.0)
+    for a in range(16):
+        ts(A("LDD", 128 * a, 128 * a + 128), A("T16"), C("DA", 16 + a), OP.max, C("DA", a), OP.min)
     tt(A("TM"), A("STF"), A("P6", 0, 256), OP.min)
     tt(A("ST1"), A("STF"), A("P4", 0, 256), OP.min)
     mm(A("P5", 256, 512), A("BO32"), A("TM"), True, False)
@@ -283,25 +299,21 @@ def rank_program(g, core, T, topo):
     ts(A("NB", 1025, 2049), A("NBI", 1024, 2048), 1.0, OP.add)
     names_to_lists(A("P5", 256, 512))
     own_vertex()
-    for q in range(4):
+    for q in range(4 - DQ):
         act(A("W%d" % q), A("WB", 1 + 512 * q, 513 + 512 * q))
-    ms(A("X", 0, 1), 0.0)
-    ms(A("D", 0, 1), 1.0)
-    if not GLDD:
-        cp(A("T16"), A("T2"))
-        for a in range(16):
-            ts(A("LDD", 128 * a, 128 * a + 128), A("T16"), C("DA", 16 + a), OP.max, C("DA", a), OP.min)
     cDum = C("COL", 7)
     cRe = C("COL", 20)
 
     def first_tables():
-        for f in neighbour_tiles():
+        for f in neighbour_tiles(1):
             f()
         for q in range(2):
             ts(A("X", 1 + 1024 * q, 1025 + 1024 * q), A("LABI", 1024 * q, 1024 * q + 1024), -1.0, OP.mult)
 
     def late_constants():
         col(7, cA, 1.0, 2049.0)
+        col(21, cA, 1.0, 2065.0)
+        ms(A("DIF", 8, 16), 0.0)
         cA16 = col(8, cA, 16.0, 0.0)
         cG15 = col(10, cG, 1.0, 15.0)
         ts(A("SPI"), A("IM", 0, 16), SPREAD, OP.mult)
@@ -332,7 +344,6 @@ def rank_program(g, core, T, topo):
             for e in range(2):
                 ts(A("FU", 384 + 128 * e, 512 + 128 * e), A("BO32"), C("DA", 8 * e + 7), OP.mult)
             ts(A("I7"), A("I32"), col(23, C("DA", 7), -1.0, 1.0), OP.mult)
-            col(21, cA, 1.0, 2065.0)
         return last_constants
     FOLD = [A("FU", 0, 128), A("FU", 128, 256)]
     UNF = [A("FU", 0, 128), A("FU", 256, 384)]
@@ -351,6 +362,8 @@ def rank_program(g, core, T, topo):
         act(A("RA", 0, 64), A("P7", 256, 320))
         act(A("RCV"), G("RA", RW, "RE", 0, 16))
 
+    if EARLY:
+        last_constants = late_constants()
     first_tables()
     for t in range(STEPS):
         last = t == STEPS - 1
@@ -359,16 +372,24 @@ def rank_program(g, core, T, topo):
 
         act(A("XV"), G("X", 2049, "VU", 0, 16))
         c0 = 0
-        for n in (2, 3, 3, 4, 4):
+        for n in (3, 3, 4, 3, 3):
             n = min(n, N1 - c0)
             if n > 0:
                 act(A("XK", 256 * c0, 256 * (c0 + n)), G("X", 2049, "KT", 16 * c0, 16 * (c0 + n)))
             c0 += n
         for q in range(4):
-            tt(A("D", 1 + 512 * q, 513 + 512 * q), A("X", 1 + 512 * q, 513 + 512 * q), A("W%d" % q), OP.add)
+            lo, hi = 1 + 512 * q, 513 + 512 * q
+            if q < 4 - DQ:
+                tt(A("D", lo, hi), A("X", lo, hi), A("W%d" % q), OP.add)
+            else:
+                mm(A("W%d" % q), A("IB"), A("WB", lo, hi), True, False)
+                mm(A("W%d" % q), A("I32"), A("X", lo, hi), False, True)
+                act(A("D", lo, hi), A("W%d" % q))
         if t == 0:
-            last_constants = late_constants()
+            if not EARLY:
+                last_constants = late_constants()
             diffs(A("V16"), 16, "P5", "AV")
+            vertex_pairs()
             act(A("NX"), G("NN", 16, *lst(EXP)), AF.Relu, bias=-1.0)
         mm(A("P7", 0, 256), A("NI32"), A("SPR"), True, False)
         if t > 0:
@@ -378,7 +399,7 @@ def rank_program(g, core, T, topo):
         for hf in range(2):
             mm(HF("P7", hf), HF("ST1", hf), A("I32"), False, hf == 1)
         c0 = 0
-        for n in (2, 2, 4, 4, 2, 2):
+        for n in (4, 4, 4, 2, 1, 1):
             act(A("DK", 256 * c0, 256 * (c0 + n)), G("D", 2049, "KT", 16 * c0, 16 * (c0 + n)))
             c0 += n
         act(A("C2"), A("P7", 0, 256), scale=-1.0)
@@ -392,7 +413,7 @@ def rank_program(g, core, T, topo):
         prev = XK(0)
         own = list(range(N1, 16))
         for i in range(3, N1):
-            if own and i % 2 == 1:
+            if own and (i % 2 == 1 or 2 * len(own) > N1 - i):
                 k = own.pop(0)
                 cur = A("S%d" % (k % 2))
                 tt(cur, G("X", 2049, "KT", 16 * k, 16 * k + 16), prev, OP.max)
@@ -400,33 +421,42 @@ def rank_program(g, core, T, topo):
             c = P if (N1 - i) % 2 == 1 else Z
             tt(c, XK(i), c, OP.max)
         assert not own
-        later = unique(A("VB"), 16, "AV", "ZO")
-        tt(A("ZS"), prev, Z, OP.max)
+        uv = unique_vertices()
+        if t == 0:
+            for f in uv[:4]:
+                f()
+        later = uv[4:]
+        pn = prev[1][0][0]
+        for hf in range(2):
+            tt(HF("ZS", hf), HF(pn, hf), HF("P4", hf, 256), OP.max)
         later.pop(0)()
-        tt(P, A("ZS"), P, OP.max)
+        for hf in range(2):
+            tt(HF("P4", hf), HF("ZS", hf), HF("P4", hf), OP.max)
         later.pop(0)()
-        tt(Z, P, A("WV"), OP.subtract)
+        for hf in range(2):
+            tt(HF("P4", hf, 256), HF("P4", hf), HF("WV", hf), OP.subtract)
         later.pop(0)()
+        cp(HF("ZS", 0), HF("P4", 0, 256))
         mm(A("P6", 0, 256), A("IB"), A("NX"), True, False)
         mm(A("P6", 0, 256), A("IB"), A("CT"), False, False)
         for i in range(16):
             tt(A("CMP", 256 * i, 256 * i + 256), A("DK", 256 * i, 256 * i + 256), Z, OP.is_lt)
             mm(A("P5", 0, 256), A("M0", 15 - i, 143 - i), A("CMP", 256 * i, 256 * i + 256), i == 0, i == 15)
         mm(A("P7", 0, 256), A("NIB"), A("NX"), True, False)
-        cp(A("ZS"), Z)
+        cp(HF("ZS", 1), HF("P4", 1, 256))
         zs = [0]
 
         def zscat(n):
             for _ in range(n):
                 b = zs[0]
-                if b < 16:
-                    cp(G("X", XW, "ZO", 2 * b, 2 * b + 1), A("ZS", 16 * b, 16 * b + 16))
+                if b < 8:
+                    cp(G("X", XW, "ZO", 2 * b, 2 * b + 2), A("ZS", 32 * b, 32 * b + 32))
                     zs[0] += 1
-        act(A("HIT"), A("P5", 0, 256), AF.Sign)
         for hf in range(2):
-            mm(HF("P6", hf), HF("HIT", hf), A("TT"), False, hf == 1)
+            act(HF("HIT", hf), HF("P5", hf), AF.Sign)
         for hf in range(2):
             mm(HF("P7", hf), HF("HIT", hf), A("TH"), False, hf == 1)
+            mm(HF("P6", hf), HF("HIT", hf), A("TT"), False, hf == 1)
         mm(A("P5", 256, 512), A("IB"), A("NX"), True, False)
         for hf in range(2):
             mm(HF("P5", hf, 256), HF("HIT", hf), A("BO"), False, hf == 1)
@@ -522,58 +552,66 @@ def rank_program(g, core, T, topo):
         if not last:
             for e in range(2):
                 mm(A("P6", e, 64, 2), UN7[e], A("RV"))
+        hs = heights(t)
+        hs.pop(0)()
         cp(A("RU"), A("RV"))
         act(A("OWN"), G("X", 2049, "RU", 0, 32))
         diffs(A("RV"), 32, "P4", "AB")
         tt(A("DIF"), A("RV", 1, 32, 2), A("RV", 0, 32, 2), OP.subtract)
+        if not last:
+            cp(A("R7", 0, 64), A("P6", 0, 64))
+        cp(A("ST"), G("DIF", 16, *lst(EXP)))
+        mm(A("P5", 0, 256), A("I16"), A("ST"), True, False)
         for a in range(16):
-            mm(A("P5", a, 256, 16), A("LDD", 128 * a, 128 * a + 128), A("RV", 1, 32, 2), True, False)
-            mm(A("P5", a, 256, 16), A("I16"), A("DIF"), False, True)
-        hs = heights(t)
+            mm(A("P5", a, 256, 16), A("LDD", 128 * a, 128 * a + 128), A("RV", 1, 32, 2), False, a == 15)
         un = unique(A("RV"), 32, "AB", "JO")[0:2] + [
             lambda: ts(A("JO", 1, 32, 2), A("SM", 1, 32, 2), cWin, OP.add, C("COL", 21), OP.min),
-            lambda: scan(A("S0"), A("C4K", 0, 256), A("AV"), 0.0, OP.add, OP.min),
-            lambda: ts(A("SM", 48, 64), A("S0", 15, 256, 16), 65536.0, OP.is_lt, 8192.0, OP.mult),
+            lambda: scan(A("SB", 512, 768), A("C4K", 0, 256), A("AV"), 0.0, OP.add, OP.min),
+            lambda: ts(A("SM", 48, 64), A("SB", 527, 768, 16), 65536.0, OP.is_lt, 8192.0, OP.mult),
             lambda: tt(A("SM", 48, 64), A("SM", 48, 64), A("SM", 0, 32, 2), OP.add),
             lambda: ts(A("JO", 0, 32, 2), A("SM", 48, 64), cWin, OP.add, cDum, OP.min)]
         between = []
         if not last:
-            hs.pop(0)()
-            cp(A("R7", 0, 64), A("P6", 0, 64))
-            hs.pop(0)()
             tt(A("TM"), G("R7", RW, "RE", 0, 16), A("OWB"), OP.add)
             hs.pop(0)()
-            names_to_lists(A("TM"))
+            names_to_lists(A("TM"), hs.pop(0))
+            hs.pop(0)()
             act(A("AV"), A("P5", 0, 256), AF.Abs, scale=131072.0)
-            nt = neighbour_tiles()
-            for f in (un[0], hs[0], un[1], hs[1], un[2]):
+            nt = neighbour_tiles(4)[:4] + neighbour_tiles(8)[8:]
+            for f in (un[0], hs[0], un[1], un[3], un[2], un[4]):
                 f()
-            for k in range(4):
+            for k in range(2):
                 if k < PRE:
                     nt[k]()
-                un[3 + k]()
+                un[5 + k]()
             own_vertex()
             got_stacks()
             diffs(A("V16"), 16, "P5", "AV")
+            vertex_pairs()
             act(A("NX"), G("NN", 16, *lst(EXP)), AF.Relu, bias=-1.0)
-            between = nt[PRE:]
+            between = nt[PRE:] + unique_vertices()[:4]
         else:
             act(A("AV"), A("P5", 0, 256), AF.Abs, scale=131072.0)
             got_stacks()
-            for f in hs:
-                f()
             mm(A("P7", 0, 256), A("I32"), A("STA", 0, 256), True, False)
             mm(A("P7", 0, 256), A("I32"), A("RCV"), False, False)
-            for hf in range(2):
-                mm(HF("P7", hf), HF("PB", hf), A("I32"), False, hf == 1)
-            for hf in range(2):
-                mm(A("P6", 128 * hf, 128 * hf + 128, p=8), A("NN", 8 * hf, 8 * hf + 8), A("I32"))
-            act(A("YS"), A("P7", 0, 256), AF.Relu, bias=-1.0)
-            act(A("YC", p=8), A("P6", 0, 256, p=8))
-            dma("s", H(T.ystk[:, :]), A("YS"))
-            dma("s", H(T.ycnt[:, :]), A("YC", p=8))
-            for f in un:
+            given = hs.pop()
+
+            def stacks_out():
+                given()
+                for hf in range(2):
+                    mm(HF("P7", hf), HF("PB", hf), A("I32"), False, hf == 1)
+                act(A("YS"), A("P7", 0, 256), AF.Relu, bias=-1.0)
+                dma("s", H(T.ystk[:, :]), A("YS"))
+
+            def counts_out():
+                for hf in range(2):
+                    mm(A("P6", 128 * hf, 128 * hf + 128, p=8), A("NN", 8 * hf, 8 * hf + 8), A("I32"))
+                act(A("YC", p=8), A("P6", 0, 256, p=8))
+                dma("s", H(T.ycnt[:, :]), A("YC", p=8))
+            for f in (un[0], hs[0], un[1], un[3], un[2], un[4], hs[1], un[5], hs[2], un[6]):
                 f()
+            between = [stacks_out, counts_out]
         for c in range(16):
             tt(G("X", XW, "JO", 2 * c, 2 * c + 2), A("OWN", 32 * c, 32 * c + 32), A(LI, 32 * c, 32 * c + 32), OP.max)
             if between:

@@ -1,51 +1,51 @@
-from concourse.mybir import AluOpType, ActivationFunctionType
+from concourse.mybir import AluOpType, ActivationFunctionType, AxisListType
 
-NM = "float16"
-N1 = 11
-DQ = 1
 STEPS = 4
 XW = 2096
-EARLY = True
-ZG = (3, 1, 2, 0)
-PRE = 2
-RW = 328
+ZWAIT = 3
+ZEARLY = 1
+OWN_LANES = 192
+LAST = 192
+BARE = 4
+PIECES = 2
+MW = 72
 
-F, B, I, U = "float32", "bfloat16", "int32", "uint16"
+F, B, I, U, NM = "float32", "bfloat16", "int32", "uint16", "float16"
 _S = {
-    "X": (XW, F), "D": (2064, F), "NB": (2064, F), "WB": (2064, B), "LABI": (2048, I), "NBI": (2048, I),
-    "STI": (256, I), "STF": (256, F), "XK": (256 * N1, F), "XV": (256, F), "DK": (4096, F), "CMP": (4096, B),
-    "PI": (8, I), "COL": (24, F), "IM": (256, F), "IS": (256, F), "LDD": (2048, NM), "FU": (768, NM),
-    "M0": (144, B), "CT": (256, B), "ROW": (256, B), "DA": (32, F), "HOLD": (256, F),
-    "LST": (64, U), "SPI": (16, I), "SPJ": (16, I), "KP": (16, F), "SPR": (256, F), "C4K": (512, B), "JB": (4, F), "JT": (32, F),
-    "VB": (16, F), "V16": (16, NM), "VJ": (32, U), "VU": (16, U), "KJ": (512, F), "KJT": (512, F),
-    "KA": (256, F), "KT": (256, U), "WV": (256, F), "AB": (512, B), "AV": (256, B), "SC": (256, F), "SB": (768, B), "SM": (64, F), "DIF": (16, F), "T16": (128, NM),
-    "ZO": (32, U), "JO": (64, U), "S0": (256, F), "S1": (256, F), "ZS": (256, F), "HIT": (256, B), "TI": (256, I),
-    "TA": (256, I), "RH": (256, F), "E0": (128, F), "E1": (128, F), "KY": (256, F), "ST": (256, NM), "ST1": (256, F),
-    "C2": (256, F), "TM": (256, F), "OWB": (256, F), "DLT": (256, F), "NP": (16, F), "NN": (16, F), "NX": (256, B),
-    "FL": (32, B), "CODE": (32, F), "GG": (32, F), "FS": (256, B), "FE": (256, B), "JK": (1024, B), "SA": (4, F),
-    "SL": (4, U), "STA": (264, F), "GA": (64, NM), "GU": (32, U), "RE": (16, U), "MSK": (32, F), "RV": (32, NM),
-    "RU": (32, U), "R7": (RW, F), "RA": (RW, F), "RCV": (256, F), "OWN": (512, F), "PB": (256, F), "YS": (256, F),
-    "YC": (256, F), "CNI": (256, I), "CNF": (256, F),
+    "X": (XW, F), "D": (2064, F), "WB": (2064, B), "LABI": (2048, I), "NBI": (2064, I),
+    "STI": (256, I), "CNI": (256, I), "CNF": (256, B), "XK": (4096, F), "XV": (256, F), "DK": (4096, F),
+    "CMP": (4096, B), "PI": (8, I), "COL": (32, F), "IM": (256, F), "IS": (256, F),
+    "M0": (144, B), "M7": (144, B), "IW": (4 * 144, F), "TL": (4 * 144, B), "FO": (144, B), "SR": (1024, B),
+    "RV8": (8, F), "RV16": (16, F), "NI": (256, F), "GI": (256, F), "IP": (512, B), "TT": (512, B), "BH": (512, B),
+    "CT": (256, B), "ONES": (256, B), "DA": (48, F), "HOLD": (256, F), "LST": (48, U),
+    "C4K": (512, B), "JB": (4, F), "JT": (64, F), "E8T": (8, B),
+    "VF": (16, F), "VU": (16, U), "KA": (256, NM), "KT": (256, U), "WV": (256, B),
+    "SC": (256, F), "SB": (768, B), "SM": (64, F), "EX": (512, NM), "ZO": (16, U), "JO": (32, U),
+    "NE": (768, B), "OVR": (256, B), "INS": (256, B), "INE": (256, B), "GA": (64, NM),
+    "ZS": (256, F), "HIT": (256, B), "TI": (256, I), "TA": (256, I), "E0": (128, F), "E1": (128, F), "KY": (256, NM), "SPR": (128, F),
+    "HV": (256, F), "STA": (264, F), "ST1": (256, NM), "TOP": (256, NM), "A1": (256, NM), "OLD": (256, NM),
+    "OCC": (256, B), "FS": (256, B), "FE": (256, B), "JK": (1024, B), "SA": (8, F), "SL": (4, U), "GU": (32, U),
+    "RE": (16, U), "MSK": (64, F), "RM": (64, NM), "RV": (32, F), "RU": (32, U), "RCV": (256, NM), "OWN": (512, F),
+    "YS": (256, F), "YC": (256, F),
 }
 POOL = {}
-for _n, _d, _l in (("CB", B, "ONE NONE IB NIB TRI TRX TXM BO NBO BT NBT TT TH D1 D2"),
-                   ("CF", F, "IG ONE32 I32 NI32 I7 BO32 NBO32 T2 SI E8")):
+for _n, _d, _l in (("CB", B, "IB BO E8 DG DN DHF N4 T2 PERM SH ISH I7 I8"),
+                   ("CF", F, "IG")):
     for _k, _c in enumerate(_l.split()):
         POOL[_c] = (_n, 128 * _k)
     _S[_n] = (128 * len(_l.split()), _d)
-POOL["I16"] = ("FU", 640)
 for _t in range(STEPS):
-    _S["MO%d" % _t] = (64, F)
-    _S["MI%d" % _t] = (64, F)
+    _S["MO%d" % _t] = (MW, F)
+    _S["MI%d" % _t] = (MW + 8, F)
     _S["LO%d" % _t] = (512, F)
     _S["LI%d" % _t] = (512, F)
 SCRATCH = {k: ("sbuf", [128, w], d) for k, (w, d) in _S.items()}
 PSUM = ["W0", "W1", "W2", "W3", "P4", "P5", "P6", "P7"]
 for _k in PSUM:
     SCRATCH[_k] = ("psum", [128, 512], F)
-NDMA = 16
+NDMA = 20
 SEMAPHORES = ["ev", "ea", "ep", "eg", "sent"] + ["d%d" % k for k in range(NDMA)] + \
-    [k + str(t) for t in range(STEPS) for k in ("nm", "la", "lb")]
+    ["nm%d" % t for t in range(STEPS)] + ["lb%d_%d" % (t, k) for t in range(STEPS) for k in range(PIECES)]
 
 OP = AluOpType
 AF = ActivationFunctionType
@@ -73,11 +73,17 @@ def rank_program(g, core, T, topo):
     def HF(n, hf, base=0):
         return A(n, base + 128 * hf, base + 128 * hf + 128)
 
+    def LO_(n):
+        return A(n, 0, 256)
+
+    def HI_(n):
+        return A(n, 256, 512)
+
     def C(n, c):
         return A(n, c, c + 1)
 
-    def G(n, hi, on, c, d):
-        return (T[n][:, 0:hi].indirect(T[on][:, c:d]), [(n, 0, hi, 1)], [(on, c, d, 1)])
+    def G(n, hi, on, c, d, lo=0):
+        return (T[n][:, lo:hi].indirect(T[on][:, c:d]), [(n, lo, hi, 1)], [(on, c, d, 1)])
 
     def val(x):
         return x[0] if isinstance(x, tuple) else x
@@ -123,14 +129,18 @@ def rank_program(g, core, T, topo):
     def mm(o, l, r, st=True, sp=True):
         add("p", lambda: g.tensor.matmul(o[0], l[0], r[0], st, sp), [o], [l, r])
 
+    def mms(o, pairs, st=True, sp=True):
+        for k, q in enumerate(pairs):
+            mm(q[2] if len(q) > 2 else o, q[0], q[1], st and k == 0, sp and k == len(pairs) - 1)
+
     def iota(o, pat, base=0, cm=0, isint=False):
         if isint:
             add("g", lambda: g.iota(o[0], pat, base, cm), [o], [])
         else:
             add("g", lambda: g.iota(o[0], pat, base, cm, allow_small_or_imprecise_dtypes=True), [o], [])
 
-    def sel(o, a, cmpop, fill):
-        add("g", lambda: g.affine_select(o[0], a[0], [[1, 128]], cmpop, fill, 0, -1), [o], [a])
+    def sel(o, a, cmpop, fill, sg=1):
+        add("g", lambda: g.affine_select(o[0], a[0], [[sg, 128]], cmpop, fill, 0, -sg), [o], [a])
 
     nd = [0]
 
@@ -144,7 +154,7 @@ def rank_program(g, core, T, topo):
 
     nsent = [0]
 
-    def send(src, dst, sem, peer, lo=0, hi=None):
+    def send(src, dst, sem, peer, lo, hi):
         rid, pid, _ = topo.addr(peer)
         m = topo.mask(core, peer)
         nsent[0] += len(topo.engines(core, peer))
@@ -152,470 +162,377 @@ def rank_program(g, core, T, topo):
         add("g", lambda: g.remote_dma(o[0], a[0], T.sem[sem], T.sem.sent, pid, rid, m), [], [a], kind="r")
         ops.append({"e": "x", "fn": None, "r": [], "w": o[1], "k": "x", "sem": (sem, len(topo.engines(peer, core)))})
 
-    ms(A("WB", 0, 16), 1.0)
+    def weave(*lists):
+        lists = [list(l) for l in lists]
+        while any(lists):
+            for l in lists:
+                if l:
+                    l.pop(0)()
+
+    ms(A("NBI", 0, 4), -1)
+    ms(A("WB", 0, 8), 1.0)
     dma("s", A("CNI", p=8), H(T.cnt[:, :]))
     dma("s", A("STI"), H(T.stk[:, :]))
-    dma("a", A("NBI", 0, 1024), H(T.nb[:, 0:1024]))
-    dma("s", A("NBI", 1024, 2048), H(T.nb[:, 1024:2048]))
-    dma("a", (T.WB[:, 1:2049], [("WB", 0, 2064, 1)], []), H(T.ln[:, :]))
-    dma("s", A("LABI", 0, 1024), H(T.lab[:, 0:1024]))
-    dma("a", A("LABI", 1024, 2048), H(T.lab[:, 1024:2048]))
+    for q, e in enumerate("as"):
+        dma(e, (T.NBI[:, 1 + 1024 * q:1025 + 1024 * q], [("NBI", 0 if q == 0 else 1025, 1025 + 1024 * q, 1)], []),
+            H(T.nb[:, 1024 * q:1024 * q + 1024]))
+    for q, e in enumerate("asas"):
+        dma(e, A("LABI", 512 * q, 512 * q + 512), H(T.lab[:, 512 * q:512 * q + 512]))
+    dma("s", (T.WB[:, 1:2049], [("WB", 0, 2064, 1)], []), H(T.ln[:, :]))
 
     iota(C("PI", 0), [[0, 1]], 0, 1, True)
-    iota(A("IG"), [[16, 8], [0, 16]])
-    iota(A("IS"), [[0, 16], [1, 16]], 1)
+    iota(A("RV8"), [[1, 2], [2, 2], [4, 2]])
     iota(A("IM"), [[1, 256]])
-    ms(A("ONE32"), 1.0)
-    ms(A("ONE"), 1.0)
-    ms(A("NONE"), -1.0)
-    sel(A("I32"), A("ONE32"), OP.is_equal, 0.0)
-    for k, m in enumerate((15, 112, 16, 8)):
+    iota(A("IG"), [[16, 8], [0, 16]])
+    iota(A("IW"), [[1, 576]])
+    iota(A("GI"), [[0, 16], [16, 16]])
+    ms(A("ONES"), 1.0)
+    for k, m in enumerate((15, 112, 1, 3, 12)):
         ts(C("PI", 1 + k), C("PI", 0), m, OP.bitwise_and)
-    cp(A("COL", 0, 5), A("PI", 0, 5))
-    cP, cA, cG, c16, c8 = C("COL", 0), C("COL", 1), C("COL", 2), C("COL", 3), C("COL", 4)
+    cp(A("COL", 0, 6), A("PI", 0, 6))
+    cP, cA, cG, cOdd, cR, cQ = [C("COL", k) for k in range(6)]
+    ncol = [6]
 
-    def col(k, src, m, a):
-        ts(C("COL", k), src, m, OP.mult, a, OP.add)
-        return C("COL", k)
-    cA1 = col(5, cA, 1.0, 1.0)
-    cWin = col(6, cA, -4096.0, 61440.0)
-    cP16 = col(18, cP, 16.0, 0.0)
-    cPick = col(9, cA, 32.0, c16)
-    ts(A("E8"), A("IG"), cP16, OP.is_equal)
-    ts(A("BO32"), A("IG"), cG, OP.is_equal)
-    EXP, PERM, PICK = 0, 16, 32
-    ts(A("HOLD"), A("IS"), cA1, OP.is_le, 1052672.0, OP.mult)
-    cp(A("LST", 0, 16), A("IM", 0, 16))
-    ts(A("LST", 32, 48), A("IM", 0, 16), cPick, OP.add)
-    ts(A("HOLD"), A("HOLD"), -4096.0, OP.add)
-    ts(A("DA", 0, 16), A("IM", 0, 16), cA, OP.is_equal)
-    cA4 = col(22, cA, -4096.0, 0.0)
-    ts(A("DA", 16, 32), A("IM", 0, 16), cA, OP.is_equal, -1.0, OP.add)
-    cBig = col(15, C("DA", 15), -1048576.0, -4096.0)
-    cCap = col(19, cA, -4096.0, cBig)
-    act(A("NBO32"), A("BO32"), scale=-1.0)
-    sel(A("T2"), A("BO32"), OP.not_equal, -1.0)
-    sel(A("IB"), A("ONE"), OP.is_equal, 0.0)
-    sel(A("NIB"), A("NONE"), OP.is_equal, 0.0)
-    iota(A("CT"), [[0, 16], [-1, 16]], 15)
-    act(A("BO"), A("BO32"))
-    act(A("NBO"), A("BO32"), scale=-1.0)
-    act(A("NI32"), A("I32"), scale=-1.0)
-    sel(A("BT"), A("BO"), OP.is_gt, 0.0)
-    sel(A("NBT"), A("NBO"), OP.is_gt, 0.0)
-    sel(A("TH"), A("NBT"), OP.not_equal, 31.0)
-    iota(A("D1"), [[0, 8], [1, 16]], -15)
-    sel(A("D2"), A("D1"), OP.is_equal, 0.0)
-    sel(A("TRI"), A("ONE"), OP.is_ge, 0.0)
-    sel(A("TRX"), A("ONE"), OP.is_gt, 0.0)
-    sel(A("TXM"), A("TRX"), OP.not_equal, -64.0)
-    iota(A("ROW"), [[1, 256]], 1)
-    iota(A("C4K"), [[0, 512]], 4096)
-    iota(A("STA", 256, 264), [[0, 8]])
-    iota(A("R7", 64, RW), [[0, RW - 64]])
-    iota(A("RA", 64, RW), [[0, RW - 64]])
-    iota(A("X", 2049, XW), [[0, XW - 2049]])
+    def col(src, m, a, op=OP.add):
+        c = C("COL", ncol[0])
+        ncol[0] += 1
+        ts(c, src, m, OP.mult, a, op)
+        return c
 
-    def lst(k):
-        return ("LST", k, k + 16)
+    def cola(src, m, a):
+        c = C("COL", ncol[0])
+        ncol[0] += 1
+        act(c, src, AF.Identity, bias=a, scale=m)
+        return c
 
-    def pick(src):
-        scan(A("SC", 0, 256), A("HOLD"), src, 0.0, OP.add, OP.min)
-        return A("SC", 15, 256, 16)
+    def fill(o, c):
+        iota(o, [[0, len(range(*o[1][0][1:]))]], c)
+    im, im16, im144 = A("IM", 0, 128), A("IM", 0, 16), A("IM", 0, 144)
+    for e in range(2):
+        ts(A("RV16", e, 16, 2), A("RV8"), 8.0 * e, OP.add)
+    ts(A("DA", 0, 16), im16, cA, OP.is_equal)
+    ts(A("E8"), A("IG"), col(cP, 16.0, 0.0), OP.is_equal)
+    tt(A("DA", 32, 48), A("DA", 0, 16), A("RV16"), OP.mult)
+    ts(A("IB"), im, cP, OP.is_equal)
+    cS = C("COL", 31)
+    add("v", lambda: g.vector.tensor_reduce(cS[0], A("DA", 32, 48)[0], AxisListType.X, OP.add), [cS], [A("DA", 32, 48)])
+    cp(A("LST", 0, 32), A("IM", 0, 32))
+    cS4 = col(cS, -4096.0, 0.0)
+    cCap = col(C("DA", 15), -1048576.0, col(cS, -4096.0, -4096.0))
+    ts(A("PERM"), im, col(cS, 1.0, cG), OP.is_equal)
+    cG15 = col(cG, 1.0, 15.0)
+    ts(A("M0"), im144, cG15, OP.is_equal)
+    EXP = ("LST", 0, 16)
 
-    def names_to_lists(src, meanwhile=lambda: None):
-        picked = pick(src)
-        meanwhile()
-        for f in range(2):
-            ts(A("VJ", f, 32, 2), picked, cWin, OP.add)
-        act(A("KJ"), G("NB", 2049, "VJ", 0, 32))
-        ts(A("VU"), picked, cWin, OP.add)
-        ts(A("V16"), picked, cWin, OP.add)
-        ts(A("VB"), picked, cWin, OP.add)
+    act(A("CNF", p=8), A("CNI", p=8))
+    act(A("TOP"), A("STI"))
+    mm(LO_("P4"), A("E8", p=8), A("CNF", p=8))
+    mms(LO_("P7"), [(A("PERM"), A("TOP")), (A("IB"), A("ONES"))])
+    act(A("HV"), LO_("P4"), AF.Relu, bias=cS4, scale=4096.0)
+    act(LO_("P4"), LO_("P4"), AF.Relu, bias=cCap, scale=4096.0)
+    cTl = col(cQ, 36.0, col(cR, 1.0, col(cG, 1.0, 12.0)))
+    ts(A("BO"), A("IG"), cG, OP.is_equal)
+    tt(LO_("STA"), LO_("P7"), A("HV"), OP.min)
 
-    def neighbour_tiles(n):
-        def tr(q):
-            w = 512 // n
-            o, a = A("KJT", w * q, w * q + w), A("KJ", w * q, w * q + w)
-            add("v", lambda: g.vector.transpose(o[0], a[0]), [o], [a])
+    def pop():
+        return [lambda: tt(A("ST1"), LO_("STA"), LO_("P4"), OP.min),
+                lambda: tt(A("TOP"), LO_("STA"), A("ST1"), OP.subtract)]
 
-        def pk(q):
-            w = 16 // n
-            cp(A("KT", 16 * w * q, 16 * w * (q + 1)), G("KJT", 512, "LST", PICK + w * q, PICK + w * q + w))
-        return [(lambda f, q: lambda: f(q))(f, q) for f in (tr, pk) for q in range(n)]
+    def pick(src, by, st, sp):
+        mms(A("P6", 0, 16), [(A(by, 15 - a, 143 - a), A(src, a, 256, 16)) for a in range(16)], st, sp)
 
-    def own_vertex():
+    def lists_of_names():
+        return [lambda: cp(A("VU"), A("P6", 0, 16)), lambda: cp(A("VF"), A("P6", 0, 16))]
+
+    def neighbours():
+        act(A("KA"), G("NBI", 2049, "VU", 0, 16), AF.Identity, bias=1.0)
+        for q in range(4):
+            mms(A("P6", 256 + 64 * q, 320 + 64 * q),
+                [(A("TL", 144 * q + 12 - 4 * e, 144 * q + 140 - 4 * e), A("KA", e, 256, 4)) for e in range(4)])
+
+    def names_by_lane():
+        mms(LO_("P6"), [(HF("KA", hf), A("IP", 256 * hf, 256 * hf + 256)) for hf in range(2)])
+
+    def lengths():
         act(A("WV"), G("WB", 2049, "VU", 0, 16))
-        act(A("KA"), G("NB", 2049, "VU", 0, 16))
-        act(A("P4", 0, 256), A("WV"))
-        for hf in range(2):
-            mm(HF("P6", hf, 256), HF("KA", hf), A("I32"))
+        mm(HI_("P4"), A("IB"), A("WV"))
 
-    def diffs(src, n, bank, out):
-        for a in range(16):
-            mm(A(bank, a, 16 * n, 16), A("LDD", 128 * a, 128 * a + 128), src)
-        act(A(out, 0, 16 * n), A(bank, 0, 16 * n), AF.Abs, scale=131072.0)
+    def repeated_names():
+        act(LO_("EX"), G("VF", 16, "LST", 0, 16))
+        act(HI_("EX"), G("VF", 16, "LST", 32, 48))
 
-    def unique(src, n, ab, out):
-        return [lambda: scan(A("SB", 0, 16 * n), A("C4K", 0, 16 * n), A(ab, 0, 16 * n), 0.0, OP.add, OP.min),
-                lambda: tt(A("SM", 0, n), src, A("SB", 15, 16 * n, 16), OP.subtract),
-                lambda: ts(A(out, 0, 2 * n, 2), A("SM", 0, n), cWin, OP.add, cDum, OP.min)]
+    def unique():
+        return [lambda: tt(LO_("NE"), LO_("EX"), LO_("P5"), OP.not_equal),
+                lambda: tt(HI_("NE"), HI_("EX"), LO_("P5"), OP.not_equal),
+                lambda: scan(A("SB", 0, 512), A("C4K"), A("NE", 0, 512), 0.0, OP.add, OP.mult),
+                lambda: tt(A("SM", 0, 16), A("VF"), A("SB", 15, 256, 16), OP.subtract),
+                lambda: ts(A("SM", 48, 56), A("SB", 287, 512, 32), 65536.0, OP.is_lt, 8192.0, OP.mult),
+                lambda: ts(A("ZO", 1, 16, 2), A("SM", 1, 16, 2), cWin, OP.add, cDum[1], OP.min),
+                lambda: tt(A("SM", 48, 56), A("SM", 48, 56), A("SM", 0, 16, 2), OP.add),
+                lambda: ts(A("ZO", 0, 16, 2), A("SM", 48, 56), cWin, OP.add, cDum[0], OP.min)]
 
-    def vertex_pairs():
-        tt(A("DIF", 0, 8), A("VB", 1, 16, 2), A("VB", 0, 16, 2), OP.subtract)
-        cp(A("ST", 0, 128), G("DIF", 16, "LST", EXP, EXP + 8))
-        mm(A("P5", 256, 384), A("I16"), A("ST", 0, 128), True, False)
-        for a in range(16):
-            mm(A("P5", 256 + a, 384, 16), A("LDD", 128 * a, 128 * a + 128), A("V16", 1, 16, 2), False, a == 15)
-        act(A("AB", 0, 128), A("P5", 256, 384), AF.Abs, scale=131072.0)
+    def old_stacks(src):
+        act(A("OLD"), src)
+        act(A("OCC"), src, AF.Sign)
 
-    def unique_vertices():
-        return unique(A("VB"), 16, "AV", "ZO")[0:2] + [
-            lambda: scan(A("SB", 512, 640), A("C4K", 0, 128), A("AB", 0, 128), 0.0, OP.add, OP.min),
-            lambda: ts(A("ZO", 1, 16, 2), A("SM", 1, 16, 2), cWin, OP.add, C("COL", 21), OP.min),
-            lambda: ts(A("SM", 48, 56), A("SB", 527, 640, 16), 65536.0, OP.is_lt, 8192.0, OP.mult),
-            lambda: tt(A("SM", 48, 56), A("SM", 48, 56), A("SM", 0, 16, 2), OP.add),
-            lambda: ts(A("ZO", 0, 16, 2), A("SM", 48, 56), cWin, OP.add, cDum, OP.min)]
+    def scaled(o, a, c):
+        act(o, a, AF.Identity, scale=val(c))
+        ops[-1]["r"] += c[1] if isinstance(c, tuple) else []
 
-    cp(A("CNF", p=8), A("CNI", p=8))
-    ts(A("STF"), A("STI"), 1.0, OP.add)
-    mm(A("P5", 0, 256), A("E8", p=8), A("CNF", p=8))
+    weave(pop(), [lambda: ts(A("TL"), A("IW"), cTl, OP.is_equal)])
+    pick("TOP", "M0", True, True)
+    mm(LO_("P5"), A("BO"), A("TOP"))
+    sel(A("T2"), A("BO"), OP.is_gt, 0.0, -1)
+    fill(A("X", 0, 1), 0)
+    fill(A("D", 0, 1), 1)
+    fill(A("C4K"), 4096)
+    iota(A("IS"), [[0, 16], [1, 16]], 1)
+    fill(A("STA", 256, 264), 0)
+    for t in range(STEPS):
+        fill(A("MO%d" % t, 0, 8), 0)
+        fill(A("MI%d" % t, MW, MW + 8), 0)
+    for e in range(2):
+        cp(A("LST", 32 + e, 48, 2), A("IM", 1 - e, 16, 2))
+    tt(A("NI"), G("RV16", 16, *EXP), A("GI"), OP.add)
+    weave(lists_of_names())
+    old_stacks(A("ST1"))
+    act(A("CT"), G("RV16", 16, *EXP), AF.Identity, bias=15.0, scale=-1.0)
+    scaled(A("DG"), A("IB"), cola(cA, 1.0, -15.0))
+    cP1 = cola(cP, 1.0, 128.0)
+    cWin = cola(cA, -4096.0, 61440.0)
+    cDum = [cola(cA, 1.0, 2049.0), cola(cA, 1.0, 2065.0)]
+    neighbours()
+    repeated_names()
     for hf in range(2):
-        mm(A("P7", 8 * hf, 8 * hf + 8), A("CNF", 128 * hf, 128 * hf + 128, p=8), A("I32", 0, 8, p=8))
-    act(A("P6", 0, 256), A("P5", 0, 256), AF.Relu, bias=cA4, scale=4096.0)
-    act(A("P4", 0, 256), A("P5", 0, 256), AF.Relu, bias=cCap, scale=4096.0)
-    cp(A("T16"), A("T2"))
-    ms(A("X", 0, 1), 0.0)
-    ms(A("D", 0, 1), 1.0)
-    for a in range(16):
-        ts(A("LDD", 128 * a, 128 * a + 128), A("T16"), C("DA", 16 + a), OP.max, C("DA", a), OP.min)
-    tt(A("TM"), A("STF"), A("P6", 0, 256), OP.min)
-    tt(A("ST1"), A("STF"), A("P4", 0, 256), OP.min)
-    mm(A("P5", 256, 512), A("BO32"), A("TM"), True, False)
-    mm(A("P5", 256, 512), A("NBO32"), A("ST1"), False, True)
-    cp(A("NN"), A("P7", 0, 16))
-    ms(A("NB", 0, 1), 0.0)
-    ts(A("NB", 1, 1025), A("NBI", 0, 1024), 1.0, OP.add)
-    ts(A("NB", 1025, 2049), A("NBI", 1024, 2048), 1.0, OP.add)
-    names_to_lists(A("P5", 256, 512))
-    own_vertex()
-    for q in range(4 - DQ):
-        act(A("W%d" % q), A("WB", 1 + 512 * q, 513 + 512 * q))
-    cDum = C("COL", 7)
-    cRe = C("COL", 20)
+        ts(A("IP", 256 * hf, 256 * hf + 256), A("NI"), (cP, cP1)[hf], OP.is_equal)
+    act(A("KT"), HI_("P6"))
+    mms(A("P7"), [(A("T2"), A("IP")), (A("DG"), A("IP"))])
+    mm(A("P4"), A("BO"), A("IP"))
+    ts(A("TI", 0, 16), A("RV16"), SPREAD, OP.mult)
+    cFo = col(cA, 0.5, col(cG, 1.0, 8.0))
+    ts(A("TA", 0, 16), A("TI", 0, 16), BITS, OP.bitwise_and)
+    ts(A("N4"), A("IB"), -4096.0, OP.mult)
+    ts(A("FO"), im144, cFo, OP.is_equal)
+    for q in range(8):
+        cp(A("SPR", 16 * q, 16 * q + 16), A("TA", 0, 16))
+    cp(A("BH"), A("P4"))
+    cp(A("TT"), A("P7"))
+    for q in range(4):
+        o, a = A("X", 1 + 512 * q, 513 + 512 * q), A("LABI", 512 * q, 512 * q + 512)
+        if q % 2 == 0:
+            act(o, a, scale=-1.0)
+        else:
+            ts(o, a, -1.0, OP.mult)
+    cRe, cS1 = C("COL", 28), C("COL", 27)
 
-    def first_tables():
-        for f in neighbour_tiles(1):
-            f()
-        for q in range(2):
-            ts(A("X", 1 + 1024 * q, 1025 + 1024 * q), A("LABI", 1024 * q, 1024 * q + 1024), -1.0, OP.mult)
+    def push_constants():
+        return [lambda: ts(cS1, cS, 1.0, OP.add),
+                lambda: ts(A("JB"), A("IM", 0, 4), 32.0, OP.mult, col(cA, 2.0, -191.0), OP.add),
+                lambda: ts(A("JT"), A("IM", 0, 64), -8192.0, OP.mult, 1048576.0, OP.add)]
 
-    def late_constants():
-        col(7, cA, 1.0, 2049.0)
-        col(21, cA, 1.0, 2065.0)
-        ms(A("DIF", 8, 16), 0.0)
-        cA16 = col(8, cA, 16.0, 0.0)
-        cG15 = col(10, cG, 1.0, 15.0)
-        ts(A("SPI"), A("IM", 0, 16), SPREAD, OP.mult)
-        ts(A("LST", 48, 64), A("IM", 0, 16), 0.0, OP.mult, cA, OP.add)
-        ts(A("SPJ"), A("SPI"), BITS, OP.bitwise_and)
-        ts(A("M0"), A("IM", 0, 144), cG15, OP.is_equal)
-        cp(A("KP"), A("SPJ"))
-        act(A("SPR"), G("KP", 16, *lst(48)))
-        ts(A("LST", 16, 32), A("IM", 0, 16), cA16, OP.add)
-        cp(A("I16"), A("I32"))
-        cP8 = col(11, cP, 1.0, 8.0)
-        cM8 = col(12, cP, 1.0, -8.0)
-        cGe = col(13, c8, 0.125, 0.0)
-        cLt = col(14, c8, -0.125, 1.0)
-        cJ = col(16, cA, 2.0, 1.0)
-        cJT = col(17, c8, 0.25, -256.0)
-        col(20, cWin, 1.0, 63.0)
-        im = A("IM", 0, 128)
-        ts(A("FU", 0, 128), im, cP, OP.is_equal, cLt, OP.mult)
-        ts(A("FU", 128, 256), im, cP8, OP.is_equal, cLt, OP.mult)
-        ts(A("JB"), A("IM", 0, 4), 32.0, OP.mult, cJ, OP.add)
-        tt(A("TT"), A("BT"), A("D2"), OP.add)
+    def meeting_constants():
+        scaled(A("DN"), A("IB"), -32.5)
+        scaled(A("DHF"), A("IB"), 0.5)
+        cEven = col(cOdd, -1.0, 1.0)
+        ts(A("HOLD"), A("IS"), col(cA, 1.0, 1.0), OP.is_le, 1052672.0, OP.mult)
+        ts(cRe, cWin, 31.5, OP.add)
+        ts(A("HOLD"), A("HOLD"), -4096.0, OP.add)
 
-        def last_constants():
-            ts(A("FU", 256, 384), im, cM8, OP.is_equal, cGe, OP.mult)
-            ts(A("JT"), A("IM", 0, 32), 4.0, OP.mult, cJT, OP.add)
-            tt(A("SI"), A("FU", 256, 384), A("I32"), OP.subtract)
-            for e in range(2):
-                ts(A("FU", 384 + 128 * e, 512 + 128 * e), A("BO32"), C("DA", 8 * e + 7), OP.mult)
-            ts(A("I7"), A("I32"), col(23, C("DA", 7), -1.0, 1.0), OP.mult)
-        return last_constants
-    FOLD = [A("FU", 0, 128), A("FU", 128, 256)]
-    UNF = [A("FU", 0, 128), A("FU", 256, 384)]
-    UN7 = [A("FU", 384, 512), A("FU", 512, 640)]
+        def later():
+            for r in range(8):
+                ts(A("SR", 128 * r, 128 * r + 128), A("BO"), C("DA", 2 * r), OP.mult)
+            scaled(A("M7"), A("M0"), C("DA", 14))
+            ts(A("SH"), im, col(cP, 1.0, -1.0), OP.is_equal, cOdd, OP.mult)
+            scaled(A("I8"), A("IB"), cEven)
+            scaled(A("I7"), A("IB"), col(C("DA", 14), -1.0, cEven))
+            tt(A("ISH"), A("IB"), A("SH"), OP.subtract)
+            ts(A("E8T"), A("IM", 0, 8), 16.0, OP.mult, cG, OP.is_equal)
+        return later
 
-    def heights(t):
-        return [lambda: tt(A("GG"), A("CODE"), A("MI%d" % t, 32, 64), OP.is_lt),
-                lambda: tt(A("SM", 32, 48), A("GG", 16, 32), A("GG", 0, 16), OP.subtract),
-                lambda: ts(A("SM", 32, 48), A("SM", 32, 48), 8.0, OP.mult),
-                lambda: tt(A("NN"), A("SM", 32, 48), A("NP"), OP.add),
-                lambda: tt(A("PB"), G("GG", 16, *lst(EXP)), A("DLT"), OP.mult)]
+    def fold(o, src):
+        mms(o, [(A("FO", 8 - 8 * e, 136 - 8 * e), A(src, e, 64, 2)) for e in range(2)])
 
-    def got_stacks():
-        for e in range(2):
-            mm(A("P7", 256 + e, 320, 2), UNF[e], A("RV"))
-        act(A("RA", 0, 64), A("P7", 256, 320))
-        act(A("RCV"), G("RA", RW, "RE", 0, 16))
-
-    if EARLY:
-        last_constants = late_constants()
-    first_tables()
+    P, Z = LO_("P4"), HI_("P4")
     for t in range(STEPS):
         last = t == STEPS - 1
         peer = T.cores[rank ^ (1 << (t % 2))]
         MO, MI, LO, LI = "MO%d" % t, "MI%d" % t, "LO%d" % t, "LI%d" % t
 
+        def gather(o, win, q, lo=0, hi=256):
+            act(A(o, 1024 * q + 4 * lo, 1024 * q + 4 * hi), G(win, 2049, "KT", 64 * q + lo // 4, 64 * q + hi // 4))
+
+        def nbr(n, q, r, lo=0, hi=256):
+            return A(n, 1024 * q + 4 * lo + r, 1024 * q + 4 * hi, 4)
+        n = OWN_LANES
+        gather("XK", "X", 1)
+        gather("XK", "X", 0, n)
         act(A("XV"), G("X", 2049, "VU", 0, 16))
-        c0 = 0
-        for n in (3, 3, 4, 3, 3):
-            n = min(n, N1 - c0)
-            if n > 0:
-                act(A("XK", 256 * c0, 256 * (c0 + n)), G("X", 2049, "KT", 16 * c0, 16 * (c0 + n)))
-            c0 += n
-        for q in range(4):
-            lo, hi = 1 + 512 * q, 513 + 512 * q
-            if q < 4 - DQ:
-                tt(A("D", lo, hi), A("X", lo, hi), A("W%d" % q), OP.add)
-            else:
-                mm(A("W%d" % q), A("IB"), A("WB", lo, hi), True, False)
-                mm(A("W%d" % q), A("I32"), A("X", lo, hi), False, True)
-                act(A("D", lo, hi), A("W%d" % q))
         if t == 0:
-            if not EARLY:
-                last_constants = late_constants()
-            diffs(A("V16"), 16, "P5", "AV")
-            vertex_pairs()
-            act(A("NX"), G("NN", 16, *lst(EXP)), AF.Relu, bias=-1.0)
-        mm(A("P7", 0, 256), A("NI32"), A("SPR"), True, False)
-        if t > 0:
-            mm(A("P7", 0, 256), A("I32"), A("PB"), False, False)
-            for hf in range(2):
-                mm(HF("P7", hf), HF("RCV", hf), A("I7"), False, False)
-        for hf in range(2):
-            mm(HF("P7", hf), HF("ST1", hf), A("I32"), False, hf == 1)
-        c0 = 0
-        for n in (4, 4, 4, 2, 1, 1):
-            act(A("DK", 256 * c0, 256 * (c0 + n)), G("D", 2049, "KT", 16 * c0, 16 * (c0 + n)))
-            c0 += n
-        act(A("C2"), A("P7", 0, 256), scale=-1.0)
-        P = A("P4", 0, 256)
-        Z = A("P4", 256, 512)
+            for q in range(4):
+                mm(A("W%d" % q), A("IB"), A("WB", 1 + 512 * q, 513 + 512 * q))
+            lengths()
+        gather("XK", "X", 2)
+        gather("XK", "X", 3)
+        names_by_lane()
+        dd = [(lambda q: lambda: tt(A("D", 1 + 256 * q, 257 + 256 * q), A("X", 1 + 256 * q, 257 + 256 * q),
+                                    A("W%d" % (q // 2), 256 * (q % 2), 256 * (q % 2) + 256), OP.add))(q) for q in range(8)]
 
-        def XK(i):
-            return A("XK", 256 * i, 256 * i + 256)
-        tt(P, A("XV"), P, OP.add)
-        tt(Z, XK(1), XK(2), OP.max)
-        prev = XK(0)
-        own = list(range(N1, 16))
-        for i in range(3, N1):
-            if own and (i % 2 == 1 or 2 * len(own) > N1 - i):
-                k = own.pop(0)
-                cur = A("S%d" % (k % 2))
-                tt(cur, G("X", 2049, "KT", 16 * k, 16 * k + 16), prev, OP.max)
-                prev = cur
-            c = P if (N1 - i) % 2 == 1 else Z
-            tt(c, XK(i), c, OP.max)
-        assert not own
-        uv = unique_vertices()
+        def fold_in(i):
+            lo = n if i // 4 == 1 else 0
+            c = A("P4", 256 * (1 - i % 2) + lo, 256 * (2 - i % 2))
+            tt(A("ZS") if i == 14 else c, nbr("XK", i // 4, i % 4, lo), c, OP.max)
+        own = [lambda: tt(A("XK", 0, 4 * n), G("X", 2049, "KT", 0, n // 4), A("XK", 1024, 1024 + 4 * n), OP.max),
+               lambda: tt(Z, A("XV"), Z, OP.add),
+               lambda: tt(P, nbr("XK", 0, 0), nbr("XK", 0, 1), OP.max)]
+        un = unique()
         if t == 0:
-            for f in uv[:4]:
-                f()
-        later = uv[4:]
-        pn = prev[1][0][0]
-        for hf in range(2):
-            tt(HF("ZS", hf), HF(pn, hf), HF("P4", hf, 256), OP.max)
-        later.pop(0)()
-        for hf in range(2):
-            tt(HF("P4", hf), HF("ZS", hf), HF("P4", hf), OP.max)
-        later.pop(0)()
-        for hf in range(2):
-            tt(HF("P4", hf, 256), HF("P4", hf), HF("WV", hf), OP.subtract)
-        later.pop(0)()
-        cp(HF("ZS", 0), HF("P4", 0, 256))
-        mm(A("P6", 0, 256), A("IB"), A("NX"), True, False)
-        mm(A("P6", 0, 256), A("IB"), A("CT"), False, False)
-        for i in range(16):
-            tt(A("CMP", 256 * i, 256 * i + 256), A("DK", 256 * i, 256 * i + 256), Z, OP.is_lt)
-            mm(A("P5", 0, 256), A("M0", 15 - i, 143 - i), A("CMP", 256 * i, 256 * i + 256), i == 0, i == 15)
-        mm(A("P7", 0, 256), A("NIB"), A("NX"), True, False)
-        cp(HF("ZS", 1), HF("P4", 1, 256))
-        zs = [0]
+            weave(push_constants(), un[:5])
+            weave([own[0]] + dd[:3] + [own[2]] + dd[3:6] + [own[1]] + dd[6:])
+        else:
+            weave(dd[:7] + own + dd[7:])
+        for i in range(2, 16):
+            fold_in(i)
+        for q in range(3):
+            gather("DK", "D", q)
+        gather("DK", "D", 3, 0, LAST)
+        gather("DK", "D", 3, LAST)
+        weave(un[5:], [lambda: tt(P, A("ZS"), P, OP.max),
+                       lambda: tt(Z, P, A("WV"), OP.subtract),
+                       lambda: tt(A("ZS"), P, A("WV"), OP.subtract)])
+        mms(HI_("P6"), [(HF("OCC", hf), A("BH", 256 * hf, 256 * hf + 256)) for hf in range(2)] + [(A("IB"), A("CT"))], True, False)
+        R = HI_("P7")
+        mm(R, A("BO"), A("OCC"), True, False)
 
-        def zscat(n):
-            for _ in range(n):
-                b = zs[0]
-                if b < 8:
-                    cp(G("X", XW, "ZO", 2 * b, 2 * b + 2), A("ZS", 32 * b, 32 * b + 32))
-                    zs[0] += 1
+        def compare(q, r, lo, hi):
+            i = 4 * q + r
+            c = A("CMP", 256 * i + lo, 256 * i + hi)
+            tt(c, nbr("DK", q, r, lo, hi), A("P4", 256 + lo, 256 + hi), OP.is_lt)
+            mm(A("P5", lo, hi), A("M0", 15 - i, 143 - i), c, i == 0, i == 15 and hi == 256)
+        cmps = [(lambda *a: lambda: compare(*a))(q, r, lo, hi)
+                for q, lo, hi in ((0, 0, 256), (1, 0, 256), (2, 0, 256), (3, 0, LAST), (3, LAST, 256)) for r in range(4)]
+        zs = [(lambda b: lambda: cp(G("X", XW, "ZO", 2 * b, 2 * b + 2), A("ZS", 32 * b, 32 * b + 32)))(b) for b in range(8)]
+        weave(cmps, zs[:ZEARLY])
+        weave(zs[ZEARLY:ZEARLY + ZWAIT])
+        zs = zs[ZEARLY + ZWAIT:]
         for hf in range(2):
             act(HF("HIT", hf), HF("P5", hf), AF.Sign)
-        for hf in range(2):
-            mm(HF("P7", hf), HF("HIT", hf), A("TH"), False, hf == 1)
-            mm(HF("P6", hf), HF("HIT", hf), A("TT"), False, hf == 1)
-        mm(A("P5", 256, 512), A("IB"), A("NX"), True, False)
-        for hf in range(2):
-            mm(HF("P5", hf, 256), HF("HIT", hf), A("BO"), False, hf == 1)
-        act(A("RH"), A("P7", 0, 256), AF.Relu, bias=-61440.0, scale=4096.0)
-        act(A("FS"), A("P5", 256, 512), AF.Sign, bias=-8.5)
-        zscat(ZG[0])
-        ts(A("TI"), A("P6", 0, 256), SPREAD, OP.mult)
-        zscat(ZG[1])
-        ts(A("TA"), A("TI"), BITS, OP.bitwise_and)
-        tt(A("P6", 256, 512), A("RH"), A("P6", 256, 512), OP.min)
-        mm(A("P4", 0, 256), A("IB"), A("ROW"), True, False)
-        mm(A("P4", 0, 128), HF("FS", 0), A("TRI"), False, False)
-        mm(A("P4", 128, 256), HF("FS", 0), A("ONE"), False, False)
-        mm(A("P4", 128, 256), HF("FS", 1), A("TRI"), False, True)
-        ts(A("NP"), A("P5", 256, 512, 16), 16.0, OP.min)
+        mms(HI_("P6"), [(HF("HIT", hf), A("TT", 256 * hf, 256 * hf + 256)) for hf in range(2)], False, True)
+        mm(R, A("BO"), A("HIT"), False, True)
+        act(A("FS"), R, AF.Sign, bias=-8.5)
+        act(A("OVR"), R, AF.Relu, bias=cS1, scale=-1.0)
+        mms(LO_("P5"), [(A("N4"), A("OCC")), (A("N4"), A("OVR"))], True, False)
+        for k in range(2):
+            ts(HF("TI", k), HF("P6", k, 256), SPREAD, OP.mult)
+        for k in range(2):
+            ts(HF("TA", k), HF("TI", k), BITS, OP.bitwise_and)
+        tt(A("E0"), HF("TA", 0), HF("P6", 0), OP.add)
+        tt(HF("P6", 1), HF("TA", 1), HF("P6", 1), OP.add)
+        scan(A("INS"), A("FS"), A("ONES"), -192.0, OP.add, OP.add)
         for c in range(4):
-            act(A("JK", 256 * c, 256 * c + 256), A("P4", 0, 256), AF.Sign, bias=C("JB", c), scale=-1.0, acc=C("SA", c))
-        act(A("FE"), A("P5", 256, 512), AF.Sign, bias=0.5, scale=-1.0)
-        tt(A("E0"), A("TA", 0, 256, 2), A("P6", 256, 512, 2), OP.add)
-        tt(A("P6", 0, 128), A("TA", 1, 256, 2), A("P6", 257, 512, 2), OP.add)
-        ts(A("FL", 0, 16), A("NP"), 8.5, OP.is_gt)
-        ts(A("FL", 16, 32), A("NP"), 0.5, OP.is_lt)
-        mm(A("P7", 0, 32), A("TXM"), A("FL"), True, False)
-        mm(A("P7", 8, 16), A("ONE"), A("FL", 0, 8), False, False)
-        mm(A("P7", 24, 32), A("ONE"), A("FL", 16, 24), False, True)
-        for k in range(4):
-            s = 16 - 16 * (k // 2)
-            mm(A("P7", 32 + 8 * k, 40 + 8 * k), A("ONE"), A("FL", s, s + 8), True, False)
-            mm(A("P7", 32 + 8 * k, 40 + 8 * k), A("ONE"), A("FL", s + 8, s + 16), False, True)
+            act(A("JK", 256 * c, 256 * c + 256), A("INS"), AF.Sign, bias=C("JB", c), scale=-1.0, acc=C("SA", c))
+        act(A("FE"), R, AF.Sign, bias=0.5, scale=-1.0, acc=C("SA", 4))
         if not last:
-            mm(A("P5", 0, 256), A("BO"), A("HIT"), True, False)
-            for hf in range(2):
-                mm(HF("P5", hf), HF("NX", hf), A("IB"), False, hf == 1)
-            act(A("P5", 0, 256), A("P5", 0, 256), AF.Relu, bias=cCap, scale=4096.0)
+            act(LO_("P4"), R, AF.Relu, bias=cCap, scale=4096.0)
         for s in range(4):
-            e, o = "E%d" % (s % 2), 128 * (s % 2)
-            if s < 3:
-                e2, o2 = "E%d" % (1 - s % 2), 128 - o
-                for k, op in enumerate((OP.min, OP.max)):
-                    tt(A(e2, 64 * k, 64 * k + 64), A(e, 0, 128, 2), A("P6", o, o + 128, 2), op)
-                    tt(A("P6", o2 + 64 * k, o2 + 64 * k + 64), A(e, 1, 128, 2), A("P6", o + 1, o + 128, 2), op)
-            else:
-                for k, op in enumerate((OP.min, OP.max)):
-                    tt(HF("KY", k), A(e), A("P6", o, o + 128), op)
-            if s == 1:
-                ts(A(MO, 32, 64), A("P7", 32, 64), 64.0, OP.min, -64.0, OP.add)
-            elif s == 3:
-                ts(A("SL"), A("SA"), 0.5, OP.mult, 128.0, OP.add)
-            else:
-                zscat(1)
-        tt(A("ST"), G("KY", 256, *lst(PERM)), A("C2"), OP.subtract)
-        for hf in range(2):
-            mm(HF("P4", hf), HF("ST", hf), A("I16"))
-        act(A("STA", 0, 256), A("P4", 0, 256))
-        zscat(ZG[2])
-        cp(A("GA"), G("STA", 264, "SL", 0, 4))
-        mm(A("P7", 128, 160), FOLD[0], A("GA", 0, 64, 2), True, False)
-        mm(A("P7", 128, 160), FOLD[1], A("GA", 1, 64, 2), False, True)
-        if not last:
-            tt(A("ST1"), A("STA", 0, 256), A("P5", 0, 256), OP.min)
-        else:
-            zscat(2)
-        cp(A(MO, 0, 32), A("P7", 128, 160))
-        send(MO, MI, "nm%d" % t, peer)
-        zscat(1)
-        cp(A("GU"), A("P7", 128, 160))
-        zscat(16)
-        act(A(LO, 256, 512), G("X", 2049, "GU", 16, 32))
-        cp(A(LO, 0, 256), G("X", 2049, "GU", 0, 16))
-        send(LO, LI, "la%d" % t, peer, 0, 256)
-        send(LO, LI, "lb%d" % t, peer, 256, 512)
-        for hf in range(2):
-            mm(A("P7", 64, 66), HF("FE", hf), A("ONE", 0, 2), hf == 0, hf == 1)
-        mm(A("P4", 256, 512), A("IB"), A("ROW"), True, False)
-        mm(A("P4", 256, 384), HF("FE", 0), A("TXM"), False, False)
-        mm(A("P4", 384, 512), HF("FE", 0), A("ONE"), False, False)
-        mm(A("P4", 384, 512), HF("FE", 1), A("TXM"), False, True)
-        if t == 0:
-            cp(A("T16"), A("BO32"))
-        if not last:
-            tt(A("ST"), A("STA", 0, 256), A("ST1"), OP.subtract)
-            mm(A("P5", 256, 512), A("T16"), A("ST"))
-            act(A("OWB"), A("P5", 256, 512))
-        if t == 0:
-            last_constants()
-        cp(A("CODE"), A("P7", 0, 32))
-        ts(A("MSK"), A("JT"), C("P7", 64), OP.is_lt)
-        ts(A("RE"), pick(A("P4", 256, 512)), cRe, OP.add, 0.5, OP.mult)
-        for hf in range(2):
-            mm(HF("P5", hf), HF("STA" if last else "ST1", hf), A("SI"))
-        act(A("DLT"), A("P5", 0, 256))
-        tt(A("RV"), A(MI, 0, 32), A("MSK"), OP.mult)
-        if not last:
-            for e in range(2):
-                mm(A("P6", e, 64, 2), UN7[e], A("RV"))
-        hs = heights(t)
-        hs.pop(0)()
-        cp(A("RU"), A("RV"))
-        act(A("OWN"), G("X", 2049, "RU", 0, 32))
-        diffs(A("RV"), 32, "P4", "AB")
-        tt(A("DIF"), A("RV", 1, 32, 2), A("RV", 0, 32, 2), OP.subtract)
-        if not last:
-            cp(A("R7", 0, 64), A("P6", 0, 64))
-        cp(A("ST"), G("DIF", 16, *lst(EXP)))
-        mm(A("P5", 0, 256), A("I16"), A("ST"), True, False)
-        for a in range(16):
-            mm(A("P5", a, 256, 16), A("LDD", 128 * a, 128 * a + 128), A("RV", 1, 32, 2), False, a == 15)
-        un = unique(A("RV"), 32, "AB", "JO")[0:2] + [
-            lambda: ts(A("JO", 1, 32, 2), A("SM", 1, 32, 2), cWin, OP.add, C("COL", 21), OP.min),
-            lambda: scan(A("SB", 512, 768), A("C4K", 0, 256), A("AV"), 0.0, OP.add, OP.min),
-            lambda: ts(A("SM", 48, 64), A("SB", 527, 768, 16), 65536.0, OP.is_lt, 8192.0, OP.mult),
-            lambda: tt(A("SM", 48, 64), A("SM", 48, 64), A("SM", 0, 32, 2), OP.add),
-            lambda: ts(A("JO", 0, 32, 2), A("SM", 48, 64), cWin, OP.add, cDum, OP.min)]
-        between = []
-        if not last:
-            tt(A("TM"), G("R7", RW, "RE", 0, 16), A("OWB"), OP.add)
-            hs.pop(0)()
-            names_to_lists(A("TM"), hs.pop(0))
-            hs.pop(0)()
-            act(A("AV"), A("P5", 0, 256), AF.Abs, scale=131072.0)
-            nt = neighbour_tiles(4)[:4] + neighbour_tiles(8)[8:]
-            for f in (un[0], hs[0], un[1], un[3], un[2], un[4]):
-                f()
+            e, o = "E%d" % (s % 2), 128 + 128 * (s % 2)
+            e2, o2 = "E%d" % (1 - s % 2), 256 - 128 * (s % 2)
             for k in range(2):
-                if k < PRE:
-                    nt[k]()
-                un[5 + k]()
-            own_vertex()
-            got_stacks()
-            diffs(A("V16"), 16, "P5", "AV")
-            vertex_pairs()
-            act(A("NX"), G("NN", 16, *lst(EXP)), AF.Relu, bias=-1.0)
-            between = nt[PRE:] + unique_vertices()[:4]
+                for b, op in enumerate((OP.min, OP.max)):
+                    if s == 3:
+                        out = A("P6", 128 * k + b, 128 * k + 128, 2)
+                    else:
+                        out = A(e2, b, 128, 2) if k == 0 else A("P6", o2 + b, o2 + 128, 2)
+                    tt(out, A(e, 64 * k, 64 * k + 64), A("P6", o + 64 * k, o + 64 * k + 64), op)
+            weave(zs[s:s + 1])
+        for k in range(2):
+            tt(HF("KY", k), HF("P6", k), A("SPR"), OP.subtract)
+            mm(HF("P5", k), HF("KY", k), A("IB"), False, k == 1)
+        ts(A("SL"), A("SA", 0, 4), 0.5, OP.mult, 128.0, OP.add)
+        ts(C(MO, 0), C("SA", 4), -128.0, OP.min, -4096.0, OP.mult)
+        tt(LO_("STA"), LO_("P5"), A("OLD"), OP.max)
+        cp(A(MO, 8, MW), G("STA", 264, "SL", 0, 4))
+        send(MO, MI, "nm%d" % t, peer, 0, MW)
+        act(A("GA"), G("STA", 264, "SL", 0, 4))
+        fold(A("P6", 256, 288), "GA")
+        ts(A("MSK"), A("JT"), C(MO, 0), OP.is_gt)
+        scan(A("INE"), A("FE"), A("ONES"), 0.0, OP.add, OP.add)
+        for e in range(2):
+            cp(A("GU", e, 32, 2), A("P6", 256 + 16 * e, 272 + 16 * e))
+        w = 512 // PIECES
+        for k in range(PIECES):
+            h = w // 2
+            cp(A(LO, w * k, w * k + h), G("X", 2049, "GU", w * k // 16, (w * k + h) // 16))
+            act(A(LO, w * k + h, w * k + w), G("X", 2049, "GU", (w * k + h) // 16, (w * k + w) // 16))
+            send(LO, LI, "lb%d_%d" % (t, k), peer, w * k, w * k + w)
+        if t == 0:
+            later_constants = meeting_constants()
+        mms(HI_("P5"), [(A("DN"), A("FE")), (A("DHF"), A("INE"))])
+        place = [lambda: scan(A("SC"), A("HOLD"), HI_("P5"), 0.0, OP.add, OP.min),
+                 lambda: ts(A("RE"), A("SC", 15, 256, 16), cRe, OP.add, 64.0, OP.min)]
+        if not last:
+            weave(pop())
+            mms(HI_("P7"), [(A("DN"), A("FS")), (A("DHF"), A("INS"))])
+            pick("TOP", "M0", True, False)
         else:
-            act(A("AV"), A("P5", 0, 256), AF.Abs, scale=131072.0)
-            got_stacks()
-            mm(A("P7", 0, 256), A("I32"), A("STA", 0, 256), True, False)
-            mm(A("P7", 0, 256), A("I32"), A("RCV"), False, False)
-            given = hs.pop()
+            mms(HI_("P7"), [(A("DN"), A("FS")), (A("DHF"), A("INS"))])
+            act(A("ST1"), LO_("STA"))
+        weave(place)
+        if t == 0:
+            later_constants()
+        tt(A("RM"), A(MI, 8, MW), A("MSK"), OP.mult)
+        act(A("RCV"), G(MI, MW + 8, "RE", 0, 16, 8))
+        fold(A("P5", 0, 32), "RM")
+        for r in range(8):
+            mm(A("P4", r, 512, 8), A("SR", 128 * r, 128 * r + 128), A("RM"))
+        cp(A("RV"), A("P5", 0, 32))
+        for e in range(2):
+            cp(A("RU", e, 32, 2), A("P5", 16 * e, 16 * e + 16))
+        act(LO_("EX"), G("RV", 32, "LST", 0, 16))
+        cp(HI_("EX"), G("RV", 32, "LST", 16, 32))
+        act(A("OWN"), G("X", 2049, "RU", 0, 32))
+        if not last:
+            pick("RCV", "M7", False, True)
+            mms(LO_("P5"), [(A("BO"), A("TOP")), (A("SR", 896, 1024), A("RCV"))])
+        act(HI_("P7"), HI_("P7"), AF.Relu, bias=C(MI, 0), scale=8192.0)
+        names = [lambda: None] * 2 if last else lists_of_names()
+        tt(HI_("NE"), HI_("EX"), HI_("P4"), OP.not_equal)
+        tt(A("NE", 512, 768), LO_("EX"), HI_("P4"), OP.not_equal)
+        tt(LO_("NE"), LO_("EX"), LO_("P4"), OP.not_equal)
+        scan(A("SB", 512, 768), A("C4K", 0, 256), A("NE", 512, 768), 0.0, OP.add, OP.mult)
+        scan(A("SB", 0, 512), A("C4K"), A("NE", 0, 512), 0.0, OP.add, OP.mult)
+        ts(A("SM", 48, 64), A("SB", 527, 768, 16), 65536.0, OP.is_lt, 8192.0, OP.mult)
+        names[0]()
+        tt(A("SM", 0, 32), A("RV"), A("SB", 15, 512, 16), OP.subtract)
+        names[1]()
+        tt(A("SM", 48, 64), A("SM", 48, 64), A("SM", 0, 16), OP.add)
+        ts(A("JO", 1, 32, 2), A("SM", 16, 32), cWin, OP.add, cDum[1], OP.min)
+        ts(A("JO", 0, 32, 2), A("SM", 48, 64), cWin, OP.add, cDum[0], OP.min)
+        if not last:
+            neighbours()
+            repeated_names()
+            lengths()
 
-            def stacks_out():
-                given()
-                for hf in range(2):
-                    mm(HF("P7", hf), HF("PB", hf), A("I32"), False, hf == 1)
-                act(A("YS"), A("P7", 0, 256), AF.Relu, bias=-1.0)
-                dma("s", H(T.ystk[:, :]), A("YS"))
+        def stacks():
+            tt(A("A1"), A("ST1"), HI_("P7"), OP.min)
+            mms(LO_("P7"), [(A("SH"), A("ST1")), (A("I8" if last else "I7"), A("RCV")), (A("ISH"), A("A1"))])
+            old_stacks(LO_("P7"))
 
-            def counts_out():
-                for hf in range(2):
-                    mm(A("P6", 128 * hf, 128 * hf + 128, p=8), A("NN", 8 * hf, 8 * hf + 8), A("I32"))
-                act(A("YC", p=8), A("P6", 0, 256, p=8))
-                dma("s", H(T.ycnt[:, :]), A("YC", p=8))
-            for f in (un[0], hs[0], un[1], un[3], un[2], un[4], hs[1], un[5], hs[2], un[6]):
-                f()
-            between = [stacks_out, counts_out]
-        for c in range(16):
-            tt(G("X", XW, "JO", 2 * c, 2 * c + 2), A("OWN", 32 * c, 32 * c + 32), A(LI, 32 * c, 32 * c + 32), OP.max)
-            if between:
-                between.pop(0)()
+        def stacks_out():
+            mm(LO_("P5"), A("PERM"), A("OLD"))
+            act(A("YS"), LO_("P5"), AF.Relu, bias=-1.0)
+            dma("s", H(T.ystk[:, :]), A("YS"))
+            mm(A("P6", 0, 256, p=8), A("E8T"), A("OCC"))
+            act(A("YC", p=8), A("P6", 0, 256, p=8))
+            dma("s", H(T.ycnt[:, :]), A("YC", p=8))
+        join = [(lambda c: lambda: tt(G("X", XW, "JO", 2 * c, 2 * c + 2), A("OWN", 32 * c, 32 * c + 32),
+                                      A(LI, 32 * c, 32 * c + 32), OP.max))(c) for c in range(16)]
+        if last:
+            weave(join, [stacks, stacks_out])
+        else:
+            stacks()
+            weave(join[:BARE])
+            un = unique()
+            weave(join[BARE:], un[:2] + [(lambda k: lambda: cp(HF("KT", k), HF("P6", k, 256)))(k) for k in range(2)] + un[2:5])
 
     for q in range(4):
         o, a = A("DK", 512 * q, 512 * q + 512), A("X", 1 + 512 * q, 513 + 512 * q)
@@ -630,7 +547,7 @@ def rank_program(g, core, T, topo):
 
 
 def emit(g, T, Q, ops, nsent):
-    touch = {}
+    touch, bank = {}, {}
     know = {e: {} for e in Q}
     for j, o in enumerate(ops):
         e = o["e"]
@@ -638,20 +555,20 @@ def emit(g, T, Q, ops, nsent):
         deps = set()
         for acc, isw in ((o["r"], False), (o["w"], True)):
             for (n, lo, hi, st) in acc:
-                for (i, w, l2, h2, s2) in touch.get(n, ()):
-                    p = ops[i]
-                    same = p["e"] == e and p["k"] == "c" and o["k"] == "c"
-                    over = lo < h2 and l2 < hi and not (st == s2 and (lo - l2) % st)
-                    if same:
-                        if e != "p" and over and (w or isw):
-                            deps.add(i)
-                    elif p["k"] == "r":
-                        continue
-                    elif (over and (w or isw)) or n in PSUM:
-                        deps.add(i)
+                deps.update(i for q, i in bank.get(n, {}).items() if q != e)
+                for w in ((True, False) if isw else (True,)):
+                    for (i, l2, h2, s2) in touch.get((n, w), ()):
+                        if lo < h2 and l2 < hi and not (st == s2 and (lo - l2) % st):
+                            if not (e == "p" and ops[i]["e"] == "p") and ops[i]["k"] != "r":
+                                deps.add(i)
         for acc, isw in ((o["r"], False), (o["w"], True)):
             for (n, lo, hi, st) in acc:
-                touch.setdefault(n, []).append((j, isw, lo, hi, st))
+                if n in PSUM:
+                    bank.setdefault(n, {})[e] = j
+                if isw and st == 1:
+                    for w in (True, False):
+                        touch[(n, w)] = [x for x in touch.get((n, w), ()) if x[1] < lo or hi < x[2] or x[0] == j]
+                touch.setdefault((n, isw), []).append((j, lo, hi, st))
         o["wait"] = []
         if e == "x":
             o["clock"] = {}

@@ -1,12 +1,13 @@
 from concourse.mybir import AluOpType, ActivationFunctionType, AxisListType
 
 STEPS = 4
-XW = 2096
-ZWAIT = 3
-ZEARLY = 1
-OWN_LANES = 192
-LAST = 192
-BARE = 4
+XW = 2120
+ZPART = (0, 0, 0, 0, 1, 4)
+OWN_LANES = 256
+PARTS = ((0, 0, 256), (1, 0, 256), (2, 0, 128), (2, 128, 256), (3, 0, 128), (3, 128, 256))
+BARE = 3
+NPRE = 2
+DPRE = 7
 PIECES = 2
 MW = 72
 
@@ -14,18 +15,18 @@ F, B, I, U, NM = "float32", "bfloat16", "int32", "uint16", "float16"
 _S = {
     "X": (XW, F), "D": (2064, F), "WB": (2064, B), "LABI": (2048, I), "NBI": (2064, I),
     "STI": (256, I), "CNI": (256, I), "CNF": (256, B), "XK": (4096, F), "XV": (256, F), "DK": (4096, F),
-    "CMP": (4096, B), "PI": (8, I), "COL": (32, F), "IM": (256, F), "IS": (256, F),
-    "M0": (144, B), "M7": (144, B), "IW": (4 * 144, F), "TL": (4 * 144, B), "FO": (144, B), "SR": (1024, B),
+    "CMP": (4096, B), "PI": (8, I), "COL": (40, F), "IM": (256, F), "IS": (256, F),
+    "M0": (144, B), "IW": (4 * 144, F), "TL": (4 * 144, B), "FO": (144, B), "SR": (1024, B),
     "RV8": (8, F), "RV16": (16, F), "NI": (256, F), "GI": (256, F), "IP": (512, B), "TT": (512, B), "BH": (512, B),
     "CT": (256, B), "ONES": (256, B), "DA": (48, F), "HOLD": (256, F), "LST": (48, U),
-    "C4K": (512, B), "JB": (4, F), "JT": (64, F), "E8T": (8, B),
-    "VF": (16, F), "VU": (16, U), "KA": (256, NM), "KT": (256, U), "WV": (256, B),
-    "SC": (256, F), "SB": (768, B), "SM": (64, F), "EX": (512, NM), "ZO": (16, U), "JO": (32, U),
-    "NE": (768, B), "OVR": (256, B), "INS": (256, B), "INE": (256, B), "GA": (64, NM),
+    "C4K": (512, B), "N4K": (512, B), "RST": (768, B), "JB": (4, F), "JT": (32, F), "E8T": (8, B), "FO32": (144, F),
+    "VF": (16, F), "VU": (16, U), "KA": (256, NM), "KT": (256, U), "WV": (256, B), "RVM": (32, NM),
+    "SC": (256, F), "SB": (1280, B), "SM": (64, F), "EX": (512, NM), "ZO": (16, U), "JO": (32, U),
+    "NE": (1280, B), "OVR": (256, B), "INS": (256, B), "INE": (256, B), "GA": (64, NM),
     "ZS": (256, F), "HIT": (256, B), "TI": (256, I), "TA": (256, I), "E0": (128, F), "E1": (128, F), "KY": (256, NM), "SPR": (128, F),
     "HV": (256, F), "STA": (264, F), "ST1": (256, NM), "TOP": (256, NM), "A1": (256, NM), "OLD": (256, NM),
     "OCC": (256, B), "FS": (256, B), "FE": (256, B), "JK": (1024, B), "SA": (8, F), "SL": (4, U), "GU": (32, U),
-    "RE": (16, U), "MSK": (64, F), "RM": (64, NM), "RV": (32, F), "RU": (32, U), "RCV": (256, NM), "OWN": (512, F),
+    "RE": (16, U), "MSK": (32, F), "RM": (64, NM), "RV": (32, F), "RU": (32, U), "RCV": (256, NM), "OWN": (512, F),
     "YS": (256, F), "YC": (256, F),
 }
 POOL = {}
@@ -36,7 +37,7 @@ for _n, _d, _l in (("CB", B, "IB BO E8 DG DN DHF N4 T2 PERM SH ISH I7 I8"),
     _S[_n] = (128 * len(_l.split()), _d)
 for _t in range(STEPS):
     _S["MO%d" % _t] = (MW, F)
-    _S["MI%d" % _t] = (MW + 8, F)
+    _S["MI%d" % _t] = (MW, F)
     _S["LO%d" % _t] = (512, F)
     _S["LI%d" % _t] = (512, F)
 SCRATCH = {k: ("sbuf", [128, w], d) for k, (w, d) in _S.items()}
@@ -184,14 +185,15 @@ def rank_program(g, core, T, topo):
     iota(A("RV8"), [[1, 2], [2, 2], [4, 2]])
     iota(A("IM"), [[1, 256]])
     iota(A("IG"), [[16, 8], [0, 16]])
+    iota(A("IS"), [[0, 16], [1, 16]])
     iota(A("IW"), [[1, 576]])
     iota(A("GI"), [[0, 16], [16, 16]])
     ms(A("ONES"), 1.0)
-    for k, m in enumerate((15, 112, 1, 3, 12)):
+    for k, m in enumerate((15, 112, 1, 3, 12, 8)):
         ts(C("PI", 1 + k), C("PI", 0), m, OP.bitwise_and)
-    cp(A("COL", 0, 6), A("PI", 0, 6))
-    cP, cA, cG, cOdd, cR, cQ = [C("COL", k) for k in range(6)]
-    ncol = [6]
+    cp(A("COL", 0, 7), A("PI", 0, 7))
+    cP, cA, cG, cOdd, cR, cQ, c8 = [C("COL", k) for k in range(7)]
+    ncol = [7]
 
     def col(src, m, a, op=OP.add):
         c = C("COL", ncol[0])
@@ -214,7 +216,7 @@ def rank_program(g, core, T, topo):
     ts(A("E8"), A("IG"), col(cP, 16.0, 0.0), OP.is_equal)
     tt(A("DA", 32, 48), A("DA", 0, 16), A("RV16"), OP.mult)
     ts(A("IB"), im, cP, OP.is_equal)
-    cS = C("COL", 31)
+    cS = C("COL", 39)
     add("v", lambda: g.vector.tensor_reduce(cS[0], A("DA", 32, 48)[0], AxisListType.X, OP.add), [cS], [A("DA", 32, 48)])
     cp(A("LST", 0, 32), A("IM", 0, 32))
     cS4 = col(cS, -4096.0, 0.0)
@@ -232,22 +234,26 @@ def rank_program(g, core, T, topo):
     act(LO_("P4"), LO_("P4"), AF.Relu, bias=cCap, scale=4096.0)
     cTl = col(cQ, 36.0, col(cR, 1.0, col(cG, 1.0, 12.0)))
     ts(A("BO"), A("IG"), cG, OP.is_equal)
+    cWin = cola(cA, -4096.0, 61440.0)
+    ts(A("HOLD"), A("IS"), cA, OP.is_le, 1052672.0, OP.mult)
     tt(LO_("STA"), LO_("P7"), A("HV"), OP.min)
 
     def pop():
         return [lambda: tt(A("ST1"), LO_("STA"), LO_("P4"), OP.min),
                 lambda: tt(A("TOP"), LO_("STA"), A("ST1"), OP.subtract)]
 
-    def pick(src, by, st, sp):
-        mms(A("P6", 0, 16), [(A(by, 15 - a, 143 - a), A(src, a, 256, 16)) for a in range(16)], st, sp)
+    def pick(src):
+        scan(A("SC"), A("HOLD"), src, 0.0, OP.add, OP.min)
 
     def lists_of_names():
-        return [lambda: cp(A("VU"), A("P6", 0, 16)), lambda: cp(A("VF"), A("P6", 0, 16))]
+        return [lambda: pick(LO_("P6")),
+                lambda: ts(A("VU"), A("SC", 15, 256, 16), cWin, OP.add),
+                lambda: ts(A("VF"), A("SC", 15, 256, 16), cWin, OP.add)]
 
     def neighbours():
         act(A("KA"), G("NBI", 2049, "VU", 0, 16), AF.Identity, bias=1.0)
         for q in range(4):
-            mms(A("P6", 256 + 64 * q, 320 + 64 * q),
+            mms(A("P5", 256 + 64 * q, 320 + 64 * q),
                 [(A("TL", 144 * q + 12 - 4 * e, 144 * q + 140 - 4 * e), A("KA", e, 256, 4)) for e in range(4)])
 
     def names_by_lane():
@@ -262,8 +268,8 @@ def rank_program(g, core, T, topo):
         act(HI_("EX"), G("VF", 16, "LST", 32, 48))
 
     def unique():
-        return [lambda: tt(LO_("NE"), LO_("EX"), LO_("P5"), OP.not_equal),
-                lambda: tt(HI_("NE"), HI_("EX"), LO_("P5"), OP.not_equal),
+        return [lambda: tt(LO_("NE"), LO_("EX"), LO_("P6"), OP.not_equal),
+                lambda: tt(HI_("NE"), HI_("EX"), LO_("P6"), OP.not_equal),
                 lambda: scan(A("SB", 0, 512), A("C4K"), A("NE", 0, 512), 0.0, OP.add, OP.mult),
                 lambda: tt(A("SM", 0, 16), A("VF"), A("SB", 15, 256, 16), OP.subtract),
                 lambda: ts(A("SM", 48, 56), A("SB", 287, 512, 32), 65536.0, OP.is_lt, 8192.0, OP.mult),
@@ -279,35 +285,34 @@ def rank_program(g, core, T, topo):
         act(o, a, AF.Identity, scale=val(c))
         ops[-1]["r"] += c[1] if isinstance(c, tuple) else []
 
-    weave(pop(), [lambda: ts(A("TL"), A("IW"), cTl, OP.is_equal)])
-    pick("TOP", "M0", True, True)
-    mm(LO_("P5"), A("BO"), A("TOP"))
+    weave(pop(), [lambda: ts(A("HOLD"), A("HOLD"), -4096.0, OP.add)])
+    mm(LO_("P6"), A("BO"), A("TOP"))
+    ts(A("TL"), A("IW"), cTl, OP.is_equal)
     sel(A("T2"), A("BO"), OP.is_gt, 0.0, -1)
     fill(A("X", 0, 1), 0)
     fill(A("D", 0, 1), 1)
     fill(A("C4K"), 4096)
-    iota(A("IS"), [[0, 16], [1, 16]], 1)
     fill(A("STA", 256, 264), 0)
     for t in range(STEPS):
         fill(A("MO%d" % t, 0, 8), 0)
-        fill(A("MI%d" % t, MW, MW + 8), 0)
+    fill(A("N4K"), -4096)
+    iota(A("RST"), [[0, 48], [-16, 16]])
     for e in range(2):
         cp(A("LST", 32 + e, 48, 2), A("IM", 1 - e, 16, 2))
-    tt(A("NI"), G("RV16", 16, *EXP), A("GI"), OP.add)
-    weave(lists_of_names())
+    weave(lists_of_names(), [lambda: tt(A("NI"), G("RV16", 16, *EXP), A("GI"), OP.add)])
+    cP1 = cola(cP, 1.0, 128.0)
+    scaled(A("DG"), A("IB"), cola(cA, 1.0, -15.0))
     old_stacks(A("ST1"))
     act(A("CT"), G("RV16", 16, *EXP), AF.Identity, bias=15.0, scale=-1.0)
-    scaled(A("DG"), A("IB"), cola(cA, 1.0, -15.0))
-    cP1 = cola(cP, 1.0, 128.0)
-    cWin = cola(cA, -4096.0, 61440.0)
-    cDum = [cola(cA, 1.0, 2049.0), cola(cA, 1.0, 2065.0)]
-    neighbours()
-    repeated_names()
+    cDum = [cola(cA, 1.0, 2049.0 + 16 * k) for k in range(4)]
+    cJb, cJt = cola(cA, -2.0, -65.0), cola(c8, 1024.0, 532480.0)
     for hf in range(2):
         ts(A("IP", 256 * hf, 256 * hf + 256), A("NI"), (cP, cP1)[hf], OP.is_equal)
-    act(A("KT"), HI_("P6"))
     mms(A("P7"), [(A("T2"), A("IP")), (A("DG"), A("IP"))])
+    neighbours()
     mm(A("P4"), A("BO"), A("IP"))
+    repeated_names()
+    act(A("KT"), HI_("P5"))
     ts(A("TI", 0, 16), A("RV16"), SPREAD, OP.mult)
     cFo = col(cA, 0.5, col(cG, 1.0, 8.0))
     ts(A("TA", 0, 16), A("TI", 0, 16), BITS, OP.bitwise_and)
@@ -315,7 +320,6 @@ def rank_program(g, core, T, topo):
     ts(A("FO"), im144, cFo, OP.is_equal)
     for q in range(8):
         cp(A("SPR", 16 * q, 16 * q + 16), A("TA", 0, 16))
-    cp(A("BH"), A("P4"))
     cp(A("TT"), A("P7"))
     for q in range(4):
         o, a = A("X", 1 + 512 * q, 513 + 512 * q), A("LABI", 512 * q, 512 * q + 512)
@@ -323,25 +327,24 @@ def rank_program(g, core, T, topo):
             act(o, a, scale=-1.0)
         else:
             ts(o, a, -1.0, OP.mult)
-    cRe, cS1 = C("COL", 28), C("COL", 27)
+    cp(A("BH"), A("P4"))
+    cRe, cS1 = C("COL", 38), C("COL", 37)
 
     def push_constants():
         return [lambda: ts(cS1, cS, 1.0, OP.add),
-                lambda: ts(A("JB"), A("IM", 0, 4), 32.0, OP.mult, col(cA, 2.0, -191.0), OP.add),
-                lambda: ts(A("JT"), A("IM", 0, 64), -8192.0, OP.mult, 1048576.0, OP.add)]
+                lambda: ts(A("JB"), A("IM", 0, 4), -32.0, OP.mult, cJb, OP.add),
+                lambda: ts(A("JT"), A("IM", 0, 32), 16384.0, OP.mult, cJt, OP.add)]
 
     def meeting_constants():
-        scaled(A("DN"), A("IB"), -32.5)
-        scaled(A("DHF"), A("IB"), 0.5)
+        scaled(A("DN"), A("IB"), 32.5)
+        scaled(A("DHF"), A("IB"), -0.5)
         cEven = col(cOdd, -1.0, 1.0)
-        ts(A("HOLD"), A("IS"), col(cA, 1.0, 1.0), OP.is_le, 1052672.0, OP.mult)
-        ts(cRe, cWin, 31.5, OP.add)
-        ts(A("HOLD"), A("HOLD"), -4096.0, OP.add)
+        ts(cRe, cWin, 39.5, OP.add)
 
         def later():
+            act(A("FO32"), A("FO"))
             for r in range(8):
                 ts(A("SR", 128 * r, 128 * r + 128), A("BO"), C("DA", 2 * r), OP.mult)
-            scaled(A("M7"), A("M0"), C("DA", 14))
             ts(A("SH"), im, col(cP, 1.0, -1.0), OP.is_equal, cOdd, OP.mult)
             scaled(A("I8"), A("IB"), cEven)
             scaled(A("I7"), A("IB"), col(C("DA", 14), -1.0, cEven))
@@ -349,8 +352,8 @@ def rank_program(g, core, T, topo):
             ts(A("E8T"), A("IM", 0, 8), 16.0, OP.mult, cG, OP.is_equal)
         return later
 
-    def fold(o, src):
-        mms(o, [(A("FO", 8 - 8 * e, 136 - 8 * e), A(src, e, 64, 2)) for e in range(2)])
+    def fold(o, by, src, lo):
+        mms(o, [(A(by, 8 - 8 * e, 136 - 8 * e), A(src, lo + e, lo + 64, 2)) for e in range(2)])
 
     P, Z = LO_("P4"), HI_("P4")
     for t in range(STEPS):
@@ -364,8 +367,10 @@ def rank_program(g, core, T, topo):
         def nbr(n, q, r, lo=0, hi=256):
             return A(n, 1024 * q + 4 * lo + r, 1024 * q + 4 * hi, 4)
         n = OWN_LANES
-        gather("XK", "X", 1)
-        gather("XK", "X", 0, n)
+        gather("XK", "X", 1, 0, n)
+        if n < 256:
+            gather("XK", "X", 0, n)
+            gather("XK", "X", 1, n)
         act(A("XV"), G("X", 2049, "VU", 0, 16))
         if t == 0:
             for q in range(4):
@@ -373,7 +378,6 @@ def rank_program(g, core, T, topo):
             lengths()
         gather("XK", "X", 2)
         gather("XK", "X", 3)
-        names_by_lane()
         dd = [(lambda q: lambda: tt(A("D", 1 + 256 * q, 257 + 256 * q), A("X", 1 + 256 * q, 257 + 256 * q),
                                     A("W%d" % (q // 2), 256 * (q % 2), 256 * (q % 2) + 256), OP.add))(q) for q in range(8)]
 
@@ -387,18 +391,20 @@ def rank_program(g, core, T, topo):
         un = unique()
         if t == 0:
             weave(push_constants(), un[:5])
-            weave([own[0]] + dd[:3] + [own[2]] + dd[3:6] + [own[1]] + dd[6:])
+            weave([own[0]] + dd[:3] + [own[2]] + dd[3:DPRE] + [own[1]])
         else:
-            weave(dd[:7] + own + dd[7:])
+            weave(dd[:DPRE] + own)
         for i in range(2, 16):
-            fold_in(i)
-        for q in range(3):
-            gather("DK", "D", q)
-        gather("DK", "D", 3, 0, LAST)
-        gather("DK", "D", 3, LAST)
+            if n < 256 or i // 4 != 1:
+                fold_in(i)
+            if i in (3, 5, 7):
+                weave(dd[DPRE + i // 2 - 1:DPRE + i // 2] if i < 7 else dd[DPRE + 2:])
+        for q, lo, hi in PARTS:
+            gather("DK", "D", q, lo, hi)
         weave(un[5:], [lambda: tt(P, A("ZS"), P, OP.max),
                        lambda: tt(Z, P, A("WV"), OP.subtract),
                        lambda: tt(A("ZS"), P, A("WV"), OP.subtract)])
+        names_by_lane()
         mms(HI_("P6"), [(HF("OCC", hf), A("BH", 256 * hf, 256 * hf + 256)) for hf in range(2)] + [(A("IB"), A("CT"))], True, False)
         R = HI_("P7")
         mm(R, A("BO"), A("OCC"), True, False)
@@ -408,12 +414,12 @@ def rank_program(g, core, T, topo):
             c = A("CMP", 256 * i + lo, 256 * i + hi)
             tt(c, nbr("DK", q, r, lo, hi), A("P4", 256 + lo, 256 + hi), OP.is_lt)
             mm(A("P5", lo, hi), A("M0", 15 - i, 143 - i), c, i == 0, i == 15 and hi == 256)
-        cmps = [(lambda *a: lambda: compare(*a))(q, r, lo, hi)
-                for q, lo, hi in ((0, 0, 256), (1, 0, 256), (2, 0, 256), (3, 0, LAST), (3, LAST, 256)) for r in range(4)]
+        cmps = [(lambda *a: lambda: compare(*a))(q, r, lo, hi) for q, lo, hi in PARTS for r in range(4)]
         zs = [(lambda b: lambda: cp(G("X", XW, "ZO", 2 * b, 2 * b + 2), A("ZS", 32 * b, 32 * b + 32)))(b) for b in range(8)]
-        weave(cmps, zs[:ZEARLY])
-        weave(zs[ZEARLY:ZEARLY + ZWAIT])
-        zs = zs[ZEARLY + ZWAIT:]
+        for k, nz in enumerate(ZPART):
+            weave(cmps[4 * k:4 * k + 4])
+            weave(zs[:nz])
+            zs = zs[nz:]
         for hf in range(2):
             act(HF("HIT", hf), HF("P5", hf), AF.Sign)
         mms(HI_("P6"), [(HF("HIT", hf), A("TT", 256 * hf, 256 * hf + 256)) for hf in range(2)], False, True)
@@ -449,15 +455,17 @@ def rank_program(g, core, T, topo):
             mm(HF("P5", k), HF("KY", k), A("IB"), False, k == 1)
         ts(A("SL"), A("SA", 0, 4), 0.5, OP.mult, 128.0, OP.add)
         ts(C(MO, 0), C("SA", 4), -128.0, OP.min, -4096.0, OP.mult)
+        scan(A("INE"), A("FE"), A("ONES"), 0.0, OP.add, OP.add)
         tt(LO_("STA"), LO_("P5"), A("OLD"), OP.max)
+        ts(A("MSK"), A("JT"), C(MO, 0), OP.is_le, 4096.0, OP.mult)
         cp(A(MO, 8, MW), G("STA", 264, "SL", 0, 4))
         send(MO, MI, "nm%d" % t, peer, 0, MW)
         act(A("GA"), G("STA", 264, "SL", 0, 4))
-        fold(A("P6", 256, 288), "GA")
-        ts(A("MSK"), A("JT"), C(MO, 0), OP.is_gt)
-        scan(A("INE"), A("FE"), A("ONES"), 0.0, OP.add, OP.add)
-        for e in range(2):
-            cp(A("GU", e, 32, 2), A("P6", 256 + 16 * e, 272 + 16 * e))
+        fold(A("P6", 256, 288), "FO", "GA", 0)
+        tops = [] if last else pop()
+        weave(tops[:1])
+        for k in range(4):
+            cp(A("GU", k, 32, 4), A("P6", 256 + 8 * k, 264 + 8 * k))
         w = 512 // PIECES
         for k in range(PIECES):
             h = w // 2
@@ -467,81 +475,83 @@ def rank_program(g, core, T, topo):
         if t == 0:
             later_constants = meeting_constants()
         mms(HI_("P5"), [(A("DN"), A("FE")), (A("DHF"), A("INE"))])
-        place = [lambda: scan(A("SC"), A("HOLD"), HI_("P5"), 0.0, OP.add, OP.min),
-                 lambda: ts(A("RE"), A("SC", 15, 256, 16), cRe, OP.add, 64.0, OP.min)]
+        place = [lambda: pick(HI_("P5")),
+                 lambda: ts(A("RE"), A("SC", 15, 256, 16), cRe, OP.add, 7.0, OP.max)]
+        mms(HI_("P7"), [(A("DN"), A("FS")), (A("DHF"), A("INS"))])
         if not last:
-            weave(pop())
-            mms(HI_("P7"), [(A("DN"), A("FS")), (A("DHF"), A("INS"))])
-            pick("TOP", "M0", True, False)
+            weave(place, tops[1:])
+            mm(LO_("P6"), A("BO"), A("TOP"), True, False)
         else:
-            mms(HI_("P7"), [(A("DN"), A("FS")), (A("DHF"), A("INS"))])
             act(A("ST1"), LO_("STA"))
-        weave(place)
+            weave(place)
+            act(A("DK", 1, 1025), A("X", 1, 1025), scale=-1.0)
+            ts(A("DK", 1025, 2049), A("X", 1025, 2049), -1.0, OP.mult)
         if t == 0:
             later_constants()
-        tt(A("RM"), A(MI, 8, MW), A("MSK"), OP.mult)
-        act(A("RCV"), G(MI, MW + 8, "RE", 0, 16, 8))
-        fold(A("P5", 0, 32), "RM")
+        cp(A("RM"), A(MI, 8, MW))
+        act(A("RCV"), G(MI, MW, "RE", 0, 16))
+        fold(A("P5", 0, 32), "FO32", MI, 8)
         for r in range(8):
             mm(A("P4", r, 512, 8), A("SR", 128 * r, 128 * r + 128), A("RM"))
         cp(A("RV"), A("P5", 0, 32))
-        for e in range(2):
-            cp(A("RU", e, 32, 2), A("P5", 16 * e, 16 * e + 16))
         act(LO_("EX"), G("RV", 32, "LST", 0, 16))
+        tt(A("RVM"), A("P5", 0, 32), A("MSK"), OP.add)
         cp(HI_("EX"), G("RV", 32, "LST", 16, 32))
+        for k in range(4):
+            act(A("RU", k, 32, 4), A("RV", 8 * k, 8 * k + 8))
         act(A("OWN"), G("X", 2049, "RU", 0, 32))
         if not last:
-            pick("RCV", "M7", False, True)
-            mms(LO_("P5"), [(A("BO"), A("TOP")), (A("SR", 896, 1024), A("RCV"))])
-        act(HI_("P7"), HI_("P7"), AF.Relu, bias=C(MI, 0), scale=8192.0)
-        names = [lambda: None] * 2 if last else lists_of_names()
+            mm(LO_("P6"), A("SR", 896, 1024), A("RCV"), False, True)
+        act(HI_("P7"), HI_("P7"), AF.Relu, bias=C(MI, 0), scale=-8192.0)
+        names = [] if last else lists_of_names()
         tt(HI_("NE"), HI_("EX"), HI_("P4"), OP.not_equal)
-        tt(A("NE", 512, 768), LO_("EX"), HI_("P4"), OP.not_equal)
         tt(LO_("NE"), LO_("EX"), LO_("P4"), OP.not_equal)
-        scan(A("SB", 512, 768), A("C4K", 0, 256), A("NE", 512, 768), 0.0, OP.add, OP.mult)
-        scan(A("SB", 0, 512), A("C4K"), A("NE", 0, 512), 0.0, OP.add, OP.mult)
-        ts(A("SM", 48, 64), A("SB", 527, 768, 16), 65536.0, OP.is_lt, 8192.0, OP.mult)
-        names[0]()
-        tt(A("SM", 0, 32), A("RV"), A("SB", 15, 512, 16), OP.subtract)
-        names[1]()
-        tt(A("SM", 48, 64), A("SM", 48, 64), A("SM", 0, 16), OP.add)
-        ts(A("JO", 1, 32, 2), A("SM", 16, 32), cWin, OP.add, cDum[1], OP.min)
-        ts(A("JO", 0, 32, 2), A("SM", 48, 64), cWin, OP.add, cDum[0], OP.min)
-        if not last:
-            neighbours()
-            repeated_names()
-            lengths()
+        sets = ((512, 384), (896, 256), (1152, 128))
+        for o, w in sets:
+            tt(A("NE", o, o + w), A("EX", 0, w), A("P4", 512 - w, 512), OP.is_equal)
+        scan(A("SB", 0, 512), A("N4K"), A("NE", 0, 512), 0.0, OP.add, OP.mult)
+        scan(A("SB", 512, 1280), A("RST"), A("NE", 512, 1280), 0.0, OP.max, OP.subtract)
+        mms(A("P5", 64, 96), [(A("IB"), A("RVM")), (A("IB"), A("SB", 15, 512, 16))]
+            + [(A("N4"), A("SB", o + 15, o + w, 16), A("P5", 64, 64 + w // 16)) for o, w in sets])
+        weave(names[:NPRE])
+        names = names[NPRE:]
+        for k in range(4):
+            ts(A("JO", k, 32, 4), A("P5", 64 + 8 * k, 72 + 8 * k), cWin, OP.add, cDum[k], OP.min)
 
         def stacks():
             tt(A("A1"), A("ST1"), HI_("P7"), OP.min)
             mms(LO_("P7"), [(A("SH"), A("ST1")), (A("I8" if last else "I7"), A("RCV")), (A("ISH"), A("A1"))])
-            old_stacks(LO_("P7"))
 
         def stacks_out():
+            old_stacks(LO_("P7"))
             mm(LO_("P5"), A("PERM"), A("OLD"))
             act(A("YS"), LO_("P5"), AF.Relu, bias=-1.0)
             dma("s", H(T.ystk[:, :]), A("YS"))
             mm(A("P6", 0, 256, p=8), A("E8T"), A("OCC"))
             act(A("YC", p=8), A("P6", 0, 256, p=8))
             dma("s", H(T.ycnt[:, :]), A("YC", p=8))
-        join = [(lambda c: lambda: tt(G("X", XW, "JO", 2 * c, 2 * c + 2), A("OWN", 32 * c, 32 * c + 32),
-                                      A(LI, 32 * c, 32 * c + 32), OP.max))(c) for c in range(16)]
+        def part(n, c):
+            return A(n, 64 * c, 64 * c + 64)
+        join = [(lambda c: lambda: tt(G("X", XW, "JO", 4 * c, 4 * c + 4), part("OWN", c), part(LI, c), OP.max))(c) for c in range(8)]
         if last:
-            weave(join, [stacks, stacks_out])
+            best = [(lambda c: lambda: tt(part("OWN", c), part("OWN", c), part(LI, c), OP.max))(c) for c in range(8)]
+            join = [(lambda c: lambda: ts(G("DK", XW, "JO", 4 * c, 4 * c + 4), part("OWN", c), -1.0, OP.mult, 0.0, OP.add))(c)
+                    for c in range(8)]
+            weave(best[:2])
+            weave(join, best[2:4] + [stacks] + best[4:])
+            stacks_out()
         else:
-            stacks()
-            weave(join[:BARE])
-            un = unique()
-            weave(join[BARE:], un[:2] + [(lambda k: lambda: cp(HF("KT", k), HF("P6", k, 256)))(k) for k in range(2)] + un[2:5])
+            weave(names)
+            neighbours()
+            repeated_names()
+            weave(join[:BARE], [stacks])
+            lengths()
+            act(A("KT"), HI_("P5"))
+            old_stacks(LO_("P7"))
+            weave(join[BARE:], unique()[:5])
 
-    for q in range(4):
-        o, a = A("DK", 512 * q, 512 * q + 512), A("X", 1 + 512 * q, 513 + 512 * q)
-        if q % 2 == 0:
-            ts(o, a, -1.0, OP.mult)
-            dma("s", H(T.ylab[:, 512 * q:512 * q + 512]), o)
-        else:
-            act(o, a, AF.Copy, scale=-1.0)
-            dma("a", H(T.ylab[:, 512 * q:512 * q + 512]), o)
+    for q, e in enumerate("sasa"):
+        dma(e, H(T.ylab[:, 512 * q:512 * q + 512]), A("DK", 1 + 512 * q, 513 + 512 * q))
 
     emit(g, T, Q, ops, nsent[0])
 

@@ -2,12 +2,18 @@ from concourse.mybir import AluOpType, ActivationFunctionType, AxisListType
 
 STEPS = 4
 XW = 2120
-ZPART = (0, 0, 0, 0, 1, 4)
-OWN_LANES = 256
-PARTS = ((0, 0, 256), (1, 0, 256), (2, 0, 128), (2, 128, 256), (3, 0, 128), (3, 128, 256))
+ZPART = (0, 0, 0, 0, 1, 0, 3)
+TPOS = 0
+RPOS = 4
+XVV = 0
+DQ0 = 2
+OWN0 = 128
+OWN_LANES = 64
+DQ = 2
+PARTS = ((0, 0, 256), (2, 0, 256), (3, 0, 96), (3, 96, 192), (3, 192, 256))
 BARE = 3
 NPRE = 2
-DPRE = 7
+DPRE = 4
 PIECES = 2
 MW = 72
 
@@ -15,23 +21,23 @@ F, B, I, U, NM = "float32", "bfloat16", "int32", "uint16", "float16"
 _S = {
     "X": (XW, F), "D": (2064, F), "WB": (2064, B), "LABI": (2048, I), "NBI": (2064, I),
     "STI": (256, I), "CNI": (256, I), "CNF": (256, B), "XK": (4096, F), "XV": (256, F), "DK": (4096, F),
-    "CMP": (4096, B), "PI": (8, I), "COL": (40, F), "IM": (256, F), "IS": (256, F),
+    "CMP": (4096, B), "PI": (8, I), "COL": (48, F), "IM": (256, F), "IS": (256, F),
     "M0": (144, B), "IW": (4 * 144, F), "TL": (4 * 144, B), "FO": (144, B), "SR": (1024, B),
     "RV8": (8, F), "RV16": (16, F), "NI": (256, F), "GI": (256, F), "IP": (512, B), "TT": (512, B), "BH": (512, B),
-    "CT": (256, B), "ONES": (256, B), "DA": (48, F), "HOLD": (256, F), "LST": (48, U),
-    "C4K": (512, B), "N4K": (512, B), "RST": (768, B), "JB": (4, F), "JT": (32, F), "E8T": (8, B), "FO32": (144, F),
-    "VF": (16, F), "VU": (16, U), "KA": (256, NM), "KT": (256, U), "WV": (256, B), "RVM": (32, NM),
-    "SC": (256, F), "SB": (1280, B), "SM": (64, F), "EX": (512, NM), "ZO": (16, U), "JO": (32, U),
+    "CT": (256, B), "ONES": (256, B), "DA": (48, F), "HOLD": (256, F), "LST": (84, U),
+    "C4K": (512, B), "N4K": (256, B), "RST": (384, B), "SETS": (36, F), "JB": (4, F), "JT": (32, F), "E8T": (8, B), "FO32": (144, F),
+    "VF": (16, F), "VU": (16, U), "KA": (256, NM), "KT": (256, U), "WV": (256, B), "WK": (1024, B), "RVM": (32, NM),
+    "SC": (256, F), "SB": (1280, B), "SM": (64, F), "EX": (512, NM), "EY": (256, NM), "ZO": (16, U), "JO": (32, U),
     "NE": (1280, B), "OVR": (256, B), "INS": (256, B), "INE": (256, B), "GA": (64, NM),
     "ZS": (256, F), "HIT": (256, B), "TI": (256, I), "TA": (256, I), "E0": (128, F), "E1": (128, F), "KY": (256, NM), "SPR": (128, F),
     "HV": (256, F), "STA": (264, F), "ST1": (256, NM), "TOP": (256, NM), "A1": (256, NM), "OLD": (256, NM),
     "OCC": (256, B), "FS": (256, B), "FE": (256, B), "JK": (1024, B), "SA": (8, F), "SL": (4, U), "GU": (32, U),
-    "RE": (16, U), "MSK": (32, F), "RM": (64, NM), "RV": (32, F), "RU": (32, U), "RCV": (256, NM), "OWN": (512, F),
+    "RE": (16, U), "MSK": (32, B), "RM": (64, NM), "RV": (32, F), "RU": (32, U), "RCV": (256, NM), "OWN": (512, F),
     "YS": (256, F), "YC": (256, F),
 }
 POOL = {}
-for _n, _d, _l in (("CB", B, "IB BO E8 DG DN DHF N4 T2 PERM SH ISH I7 I8"),
-                   ("CF", F, "IG")):
+for _n, _d, _l in (("CB", B, "IB BO NBO E8 DG DN DHF N4 T2 PERM SH ISH I7 I8"),
+                   ("CF", F, "IG I32")):
     for _k, _c in enumerate(_l.split()):
         POOL[_c] = (_n, 128 * _k)
     _S[_n] = (128 * len(_l.split()), _d)
@@ -173,12 +179,11 @@ def rank_program(g, core, T, topo):
     ms(A("NBI", 0, 4), -1)
     ms(A("WB", 0, 8), 1.0)
     dma("s", A("CNI", p=8), H(T.cnt[:, :]))
-    dma("s", A("STI"), H(T.stk[:, :]))
-    for q, e in enumerate("as"):
-        dma(e, (T.NBI[:, 1 + 1024 * q:1025 + 1024 * q], [("NBI", 0 if q == 0 else 1025, 1025 + 1024 * q, 1)], []),
-            H(T.nb[:, 1024 * q:1024 * q + 1024]))
-    for q, e in enumerate("asas"):
-        dma(e, A("LABI", 512 * q, 512 * q + 512), H(T.lab[:, 512 * q:512 * q + 512]))
+    dma("a", A("STI"), H(T.stk[:, :]))
+    dma("a", A("NBI", 1025, 2049), H(T.nb[:, 1024:2048]))
+    dma("s", (T.NBI[:, 1:1025], [("NBI", 0, 1025, 1)], []), H(T.nb[:, 0:1024]))
+    for q, e in enumerate("sa"):
+        dma(e, A("LABI", 1024 * q, 1024 * q + 1024), H(T.lab[:, 1024 * q:1024 * q + 1024]))
     dma("s", (T.WB[:, 1:2049], [("WB", 0, 2064, 1)], []), H(T.ln[:, :]))
 
     iota(C("PI", 0), [[0, 1]], 0, 1, True)
@@ -188,6 +193,8 @@ def rank_program(g, core, T, topo):
     iota(A("IS"), [[0, 16], [1, 16]])
     iota(A("IW"), [[1, 576]])
     iota(A("GI"), [[0, 16], [16, 16]])
+    iota(A("SETS", 0, 32), [[16, 2], [1, 4], [4, 4]])
+    iota(A("SETS", 32, 36), [[32, 2], [4, 2]])
     ms(A("ONES"), 1.0)
     for k, m in enumerate((15, 112, 1, 3, 12, 8)):
         ts(C("PI", 1 + k), C("PI", 0), m, OP.bitwise_and)
@@ -212,18 +219,22 @@ def rank_program(g, core, T, topo):
     im, im16, im144 = A("IM", 0, 128), A("IM", 0, 16), A("IM", 0, 144)
     for e in range(2):
         ts(A("RV16", e, 16, 2), A("RV8"), 8.0 * e, OP.add)
+    c16, cG15, cG12, cG8 = cola(cP, 16.0, 0.0), cola(cG, 1.0, 15.0), cola(cG, 1.0, 12.0), cola(cG, 1.0, 8.0)
+    cWin, cP1 = cola(cA, -4096.0, 61440.0), cola(cP, 1.0, 128.0)
+    cTl, cFo = cola(cR, 1.0, cG12), cola(cA, 0.5, cG8)
+    act(A("LST", 0, 32), A("IM", 0, 32))
+    cTl = cola(cQ, 36.0, cTl)
     ts(A("DA", 0, 16), im16, cA, OP.is_equal)
-    ts(A("E8"), A("IG"), col(cP, 16.0, 0.0), OP.is_equal)
-    tt(A("DA", 32, 48), A("DA", 0, 16), A("RV16"), OP.mult)
     ts(A("IB"), im, cP, OP.is_equal)
-    cS = C("COL", 39)
+    tt(A("DA", 32, 48), A("DA", 0, 16), A("RV16"), OP.mult)
+    ts(A("E8"), A("IG"), c16, OP.is_equal)
+    cS = C("COL", 47)
     add("v", lambda: g.vector.tensor_reduce(cS[0], A("DA", 32, 48)[0], AxisListType.X, OP.add), [cS], [A("DA", 32, 48)])
-    cp(A("LST", 0, 32), A("IM", 0, 32))
-    cS4 = col(cS, -4096.0, 0.0)
-    cCap = col(C("DA", 15), -1048576.0, col(cS, -4096.0, -4096.0))
-    ts(A("PERM"), im, col(cS, 1.0, cG), OP.is_equal)
-    cG15 = col(cG, 1.0, 15.0)
-    ts(A("M0"), im144, cG15, OP.is_equal)
+    ts(A("BO"), A("IG"), cG, OP.is_equal)
+    cPerm, cS4, cCap = col(cS, 1.0, cG), col(cS, -4096.0, 0.0), col(cS, -4096.0, -4096.0)
+    ts(A("PERM"), im, cPerm, OP.is_equal)
+    cCap = col(C("DA", 15), -1048576.0, cCap)
+    ts(A("HOLD"), A("IS"), cA, OP.is_le, 1052672.0, OP.mult)
     EXP = ("LST", 0, 16)
 
     act(A("CNF", p=8), A("CNI", p=8))
@@ -232,11 +243,12 @@ def rank_program(g, core, T, topo):
     mms(LO_("P7"), [(A("PERM"), A("TOP")), (A("IB"), A("ONES"))])
     act(A("HV"), LO_("P4"), AF.Relu, bias=cS4, scale=4096.0)
     act(LO_("P4"), LO_("P4"), AF.Relu, bias=cCap, scale=4096.0)
-    cTl = col(cQ, 36.0, col(cR, 1.0, col(cG, 1.0, 12.0)))
-    ts(A("BO"), A("IG"), cG, OP.is_equal)
-    cWin = cola(cA, -4096.0, 61440.0)
-    ts(A("HOLD"), A("IS"), cA, OP.is_le, 1052672.0, OP.mult)
+    ts(A("M0"), im144, cG15, OP.is_equal)
+    ts(A("TI", 0, 16), A("RV16"), SPREAD, OP.mult)
+    ts(A("FO"), im144, cFo, OP.is_equal)
+    ts(A("TA", 0, 16), A("TI", 0, 16), BITS, OP.bitwise_and)
     tt(LO_("STA"), LO_("P7"), A("HV"), OP.min)
+    ts(A("HOLD"), A("HOLD"), -4096.0, OP.add)
 
     def pop():
         return [lambda: tt(A("ST1"), LO_("STA"), LO_("P4"), OP.min),
@@ -250,29 +262,31 @@ def rank_program(g, core, T, topo):
                 lambda: ts(A("VU"), A("SC", 15, 256, 16), cWin, OP.add),
                 lambda: ts(A("VF"), A("SC", 15, 256, 16), cWin, OP.add)]
 
-    def neighbours():
+    def neighbours(bank, lo):
         act(A("KA"), G("NBI", 2049, "VU", 0, 16), AF.Identity, bias=1.0)
         for q in range(4):
-            mms(A("P5", 256 + 64 * q, 320 + 64 * q),
+            mms(A(bank, lo + 64 * q, lo + 64 * q + 64),
                 [(A("TL", 144 * q + 12 - 4 * e, 144 * q + 140 - 4 * e), A("KA", e, 256, 4)) for e in range(4)])
 
     def names_by_lane():
-        mms(LO_("P6"), [(HF("KA", hf), A("IP", 256 * hf, 256 * hf + 256)) for hf in range(2)])
+        mms(LO_("W3"), [(HF("KA", hf), A("IP", 256 * hf, 256 * hf + 256)) for hf in range(2)])
 
     def lengths():
         act(A("WV"), G("WB", 2049, "VU", 0, 16))
         mm(HI_("P4"), A("IB"), A("WV"))
 
+    def tile_lengths():
+        act(A("WK"), G("WB", 2049, "KT", 64, 128))
+
     def repeated_names():
-        act(LO_("EX"), G("VF", 16, "LST", 0, 16))
-        act(HI_("EX"), G("VF", 16, "LST", 32, 48))
+        act(A("EY"), G("VF", 16, "LST", 0, 16))
 
     def unique():
-        return [lambda: tt(LO_("NE"), LO_("EX"), LO_("P6"), OP.not_equal),
-                lambda: tt(HI_("NE"), HI_("EX"), LO_("P6"), OP.not_equal),
-                lambda: scan(A("SB", 0, 512), A("C4K"), A("NE", 0, 512), 0.0, OP.add, OP.mult),
+        return [lambda: tt(LO_("NE"), A("EY"), LO_("P6"), OP.not_equal),
+                lambda: tt(A("NE", 256, 496), A("EY", 0, 240), A("P6", 16, 256), OP.not_equal),
+                lambda: scan(A("SB", 0, 496), A("C4K", 0, 496), A("NE", 0, 496), 0.0, OP.add, OP.mult),
                 lambda: tt(A("SM", 0, 16), A("VF"), A("SB", 15, 256, 16), OP.subtract),
-                lambda: ts(A("SM", 48, 56), A("SB", 287, 512, 32), 65536.0, OP.is_lt, 8192.0, OP.mult),
+                lambda: ts(A("SM", 48, 56), A("SB", 271, 496, 32), 65536.0, OP.is_lt, 8192.0, OP.mult),
                 lambda: ts(A("ZO", 1, 16, 2), A("SM", 1, 16, 2), cWin, OP.add, cDum[1], OP.min),
                 lambda: tt(A("SM", 48, 56), A("SM", 48, 56), A("SM", 0, 16, 2), OP.add),
                 lambda: ts(A("ZO", 0, 16, 2), A("SM", 48, 56), cWin, OP.add, cDum[0], OP.min)]
@@ -285,9 +299,10 @@ def rank_program(g, core, T, topo):
         act(o, a, AF.Identity, scale=val(c))
         ops[-1]["r"] += c[1] if isinstance(c, tuple) else []
 
-    weave(pop(), [lambda: ts(A("HOLD"), A("HOLD"), -4096.0, OP.add)])
+    weave(pop(), [lambda: tt(A("NI"), G("RV16", 16, *EXP), A("GI"), OP.add)])
     mm(LO_("P6"), A("BO"), A("TOP"))
-    ts(A("TL"), A("IW"), cTl, OP.is_equal)
+    for hf in range(2):
+        ts(A("IP", 256 * hf, 256 * hf + 256), A("NI"), (cP, cP1)[hf], OP.is_equal)
     sel(A("T2"), A("BO"), OP.is_gt, 0.0, -1)
     fill(A("X", 0, 1), 0)
     fill(A("D", 0, 1), 1)
@@ -296,61 +311,51 @@ def rank_program(g, core, T, topo):
     for t in range(STEPS):
         fill(A("MO%d" % t, 0, 8), 0)
     fill(A("N4K"), -4096)
-    iota(A("RST"), [[0, 48], [-16, 16]])
-    for e in range(2):
-        cp(A("LST", 32 + e, 48, 2), A("IM", 1 - e, 16, 2))
-    weave(lists_of_names(), [lambda: tt(A("NI"), G("RV16", 16, *EXP), A("GI"), OP.add)])
-    cP1 = cola(cP, 1.0, 128.0)
-    scaled(A("DG"), A("IB"), cola(cA, 1.0, -15.0))
-    old_stacks(A("ST1"))
-    act(A("CT"), G("RV16", 16, *EXP), AF.Identity, bias=15.0, scale=-1.0)
-    cDum = [cola(cA, 1.0, 2049.0 + 16 * k) for k in range(4)]
+    iota(A("RST"), [[0, 24], [-16, 16]])
+    weave(lists_of_names(), [lambda: ts(A("TL"), A("IW"), cTl, OP.is_equal)])
+    cDg, cS1 = cola(cA, 1.0, -15.0), cola(cS, 1.0, 1.0)
     cJb, cJt = cola(cA, -2.0, -65.0), cola(c8, 1024.0, 532480.0)
-    for hf in range(2):
-        ts(A("IP", 256 * hf, 256 * hf + 256), A("NI"), (cP, cP1)[hf], OP.is_equal)
+    scaled(A("DG"), A("IB"), cDg)
+    cDum = [cola(cA, 1.0, 2049.0 + 16 * k) for k in range(4)]
+    act(A("JB"), A("IM", 0, 4), AF.Identity, bias=cJb, scale=-32.0)
+    act(A("JT"), A("SETS", 0, 32), AF.Identity, bias=cJt, scale=16384.0)
+    act(A("LST", 48, 80), A("SETS", 0, 32))
+    cSet = cola(cQ, 4.0, 8.0)
+    old_stacks(A("ST1"))
+    cSet = cola(c8, -3.75, cSet)
+    act(A("CT"), G("RV16", 16, *EXP), AF.Identity, bias=15.0, scale=-1.0)
+    cSet = cola(cR, 4.0, cSet)
+    act(A("I32"), A("IB"))
+    scaled(A("N4"), A("IB"), -4096.0)
+    cSet = cola(cOdd, -3.0, cSet)
     mms(A("P7"), [(A("T2"), A("IP")), (A("DG"), A("IP"))])
-    neighbours()
     mm(A("P4"), A("BO"), A("IP"))
+    act(A("TT"), A("P7"))
+    neighbours("P5", 256)
     repeated_names()
-    act(A("KT"), HI_("P5"))
-    ts(A("TI", 0, 16), A("RV16"), SPREAD, OP.mult)
-    cFo = col(cA, 0.5, col(cG, 1.0, 8.0))
-    ts(A("TA", 0, 16), A("TI", 0, 16), BITS, OP.bitwise_and)
-    ts(A("N4"), A("IB"), -4096.0, OP.mult)
-    ts(A("FO"), im144, cFo, OP.is_equal)
     for q in range(8):
         cp(A("SPR", 16 * q, 16 * q + 16), A("TA", 0, 16))
-    cp(A("TT"), A("P7"))
-    for q in range(4):
-        o, a = A("X", 1 + 512 * q, 513 + 512 * q), A("LABI", 512 * q, 512 * q + 512)
-        if q % 2 == 0:
-            act(o, a, scale=-1.0)
-        else:
-            ts(o, a, -1.0, OP.mult)
     cp(A("BH"), A("P4"))
-    cRe, cS1 = C("COL", 38), C("COL", 37)
 
-    def push_constants():
-        return [lambda: ts(cS1, cS, 1.0, OP.add),
-                lambda: ts(A("JB"), A("IM", 0, 4), -32.0, OP.mult, cJb, OP.add),
-                lambda: ts(A("JT"), A("IM", 0, 32), 16384.0, OP.mult, cJt, OP.add)]
+    def labels(q, f):
+        f(A("X", 1 + 512 * q, 513 + 512 * q), A("LABI", 512 * q, 512 * q + 512))
+    un = unique()
+    act(A("KT"), HI_("P5"))
+    for q in (2, 3, 0):
+        labels(q, lambda o, a: ts(o, a, -1.0, OP.mult))
+    labels(1, lambda o, a: act(o, a, scale=-1.0))
+    weave(un[:3])
+    cM1, cEven, cRe = col(cP, 1.0, -1.0), col(cOdd, -1.0, 1.0), col(cWin, 1.0, 39.5)
+    ts(A("E8T"), A("IM", 0, 8), 16.0, OP.mult, cG, OP.is_equal)
+    ts(A("SH"), im, cM1, OP.is_equal, cOdd, OP.mult)
+    c7 = col(C("DA", 14), -1.0, cEven)
 
     def meeting_constants():
-        scaled(A("DN"), A("IB"), 32.5)
-        scaled(A("DHF"), A("IB"), -0.5)
-        cEven = col(cOdd, -1.0, 1.0)
-        ts(cRe, cWin, 39.5, OP.add)
-
-        def later():
-            act(A("FO32"), A("FO"))
-            for r in range(8):
-                ts(A("SR", 128 * r, 128 * r + 128), A("BO"), C("DA", 2 * r), OP.mult)
-            ts(A("SH"), im, col(cP, 1.0, -1.0), OP.is_equal, cOdd, OP.mult)
-            scaled(A("I8"), A("IB"), cEven)
-            scaled(A("I7"), A("IB"), col(C("DA", 14), -1.0, cEven))
-            tt(A("ISH"), A("IB"), A("SH"), OP.subtract)
-            ts(A("E8T"), A("IM", 0, 8), 16.0, OP.mult, cG, OP.is_equal)
-        return later
+        first = [lambda: scaled(A("DN"), A("IB"), 32.5), lambda: scaled(A("DHF"), A("IB"), -0.5),
+                 lambda: scaled(A("NBO"), A("BO"), -1.0), lambda: act(A("FO32"), A("FO")),
+                 lambda: act(A("LST", 80, 84), A("SETS", 32, 36), AF.Identity, bias=cSet),
+                 lambda: scaled(A("I8"), A("IB"), cEven), lambda: scaled(A("I7"), A("IB"), c7)]
+        return first, [(lambda r: lambda: scaled(A("SR", 128 * r, 128 * r + 128), A("BO"), C("DA", 2 * r)))(r) for r in range(8)]
 
     def fold(o, by, src, lo):
         mms(o, [(A(by, 8 - 8 * e, 136 - 8 * e), A(src, lo + e, lo + 64, 2)) for e in range(2)])
@@ -366,95 +371,125 @@ def rank_program(g, core, T, topo):
 
         def nbr(n, q, r, lo=0, hi=256):
             return A(n, 1024 * q + 4 * lo + r, 1024 * q + 4 * hi, 4)
-        n = OWN_LANES
-        gather("XK", "X", 1, 0, n)
-        if n < 256:
-            gather("XK", "X", 0, n)
-            gather("XK", "X", 1, n)
-        act(A("XV"), G("X", 2049, "VU", 0, 16))
+        n = OWN_LANES if t else OWN0
+        gather("XK", "X", 1, 0, 128)
+        gather("XK", "X", 1, 128, 256)
+        if not XVV:
+            act(A("XV"), G("X", 2049, "VU", 0, 16))
+        dq = DQ if t else DQ0
+        for q in range(4):
+            if t == 0 or q == 3:
+                mm(A("W%d" % q), A("IB"), A("WB", 1 + 512 * q, 513 + 512 * q), True, q < 3 or dq == 0)
+        if dq:
+            mm(A("W3", 512 - 256 * dq, 512), A("I32"), A("X", 2049 - 256 * dq, 2049), False, True)
         if t == 0:
-            for q in range(4):
-                mm(A("W%d" % q), A("IB"), A("WB", 1 + 512 * q, 513 + 512 * q))
             lengths()
         gather("XK", "X", 2)
-        gather("XK", "X", 3)
+        if n < 256:
+            gather("XK", "X", 3, n)
+        if dq:
+            act(A("D", 2049 - 256 * dq, 2049), A("W3", 512 - 256 * dq, 512))
+        parts = PARTS if t else PARTS[:TPOS] + ((1, 0, 128), (1, 128, 256)) + PARTS[TPOS:]
+        for hf in range(2 if t else 0):
+            mms(A("P%d" % (6 + hf)), [(A("IB"), A("WK", 512 * hf, 512 * hf + 512)),
+                                      (A("I32"), A("XK", 1024 + 512 * hf, 1536 + 512 * hf))])
         dd = [(lambda q: lambda: tt(A("D", 1 + 256 * q, 257 + 256 * q), A("X", 1 + 256 * q, 257 + 256 * q),
-                                    A("W%d" % (q // 2), 256 * (q % 2), 256 * (q % 2) + 256), OP.add))(q) for q in range(8)]
+                                    A("W%d" % (q // 2), 256 * (q % 2), 256 * (q % 2) + 256), OP.add))(q) for q in range(8 - dq)]
 
         def fold_in(i):
-            lo = n if i // 4 == 1 else 0
+            lo = n if i // 4 == 2 else 0
             c = A("P4", 256 * (1 - i % 2) + lo, 256 * (2 - i % 2))
             tt(A("ZS") if i == 14 else c, nbr("XK", i // 4, i % 4, lo), c, OP.max)
-        own = [lambda: tt(A("XK", 0, 4 * n), G("X", 2049, "KT", 0, n // 4), A("XK", 1024, 1024 + 4 * n), OP.max),
-               lambda: tt(Z, A("XV"), Z, OP.add),
-               lambda: tt(P, nbr("XK", 0, 0), nbr("XK", 0, 1), OP.max)]
-        un = unique()
-        if t == 0:
-            weave(push_constants(), un[:5])
-            weave([own[0]] + dd[:3] + [own[2]] + dd[3:DPRE] + [own[1]])
-        else:
-            weave(dd[:DPRE] + own)
-        for i in range(2, 16):
-            if n < 256 or i // 4 != 1:
-                fold_in(i)
-            if i in (3, 5, 7):
-                weave(dd[DPRE + i // 2 - 1:DPRE + i // 2] if i < 7 else dd[DPRE + 2:])
-        for q, lo, hi in PARTS:
-            gather("DK", "D", q, lo, hi)
-        weave(un[5:], [lambda: tt(P, A("ZS"), P, OP.max),
-                       lambda: tt(Z, P, A("WV"), OP.subtract),
-                       lambda: tt(A("ZS"), P, A("WV"), OP.subtract)])
-        names_by_lane()
-        mms(HI_("P6"), [(HF("OCC", hf), A("BH", 256 * hf, 256 * hf + 256)) for hf in range(2)] + [(A("IB"), A("CT"))], True, False)
-        R = HI_("P7")
-        mm(R, A("BO"), A("OCC"), True, False)
 
-        def compare(q, r, lo, hi):
+        def own(q, q2, lo, hi):
+            tt(A("XK", 1024 * q + 4 * lo, 1024 * q + 4 * hi), G("X", 2049, "KT", 64 * q + lo // 4, 64 * q + hi // 4),
+               A("XK", 1024 * q2 + 4 * lo, 1024 * q2 + 4 * hi), OP.max)
+        if XVV:
+            cp(A("XV"), G("X", 2049, "VU", 0, 16))
+        weave(dd[:DPRE] if t else [])
+        own(0, 1, 0, 128)
+        weave(dd[DPRE:DPRE + 2] if t else un[3:5])
+        own(0, 1, 128, 256)
+        weave(dd[DPRE + 2:] if t else dd)
+        tt(Z, A("XV"), Z, OP.add)
+        tt(P, nbr("XK", 0, 0), nbr("XK", 0, 1), OP.max)
+        for i in (2, 3):
+            fold_in(i)
+        if n:
+            own(3, 2, 0, n)
+        for i in range(8 if n < 256 else 12, 16):
+            fold_in(i)
+        for q, lo, hi in parts:
+            gather("DK", "D", q, lo, hi)
+        weave(un[5:7], [lambda: tt(P, A("ZS"), P, OP.max),
+                        lambda: tt(A("ZS"), P, A("WV"), OP.subtract)])
+        tt(Z, P, A("WV"), OP.subtract)
+        un[7]()
+
+        def compare(q, r, lo, hi, first):
             i = 4 * q + r
             c = A("CMP", 256 * i + lo, 256 * i + hi)
-            tt(c, nbr("DK", q, r, lo, hi), A("P4", 256 + lo, 256 + hi), OP.is_lt)
-            mm(A("P5", lo, hi), A("M0", 15 - i, 143 - i), c, i == 0, i == 15 and hi == 256)
-        cmps = [(lambda *a: lambda: compare(*a))(q, r, lo, hi) for q, lo, hi in PARTS for r in range(4)]
+            if q == 1 and t:
+                tt(c, A("P%d" % (6 + lo // 128), r, 512, 4), A("ZS", lo, hi), OP.is_lt)
+            else:
+                tt(c, nbr("DK", q, r, lo, hi), A("P4", 256 + lo, 256 + hi), OP.is_lt)
+            mm(A("P5", lo, hi), A("M0", 15 - i, 143 - i), c, first, i == 15 and hi == 256)
         zs = [(lambda b: lambda: cp(G("X", XW, "ZO", 2 * b, 2 * b + 2), A("ZS", 32 * b, 32 * b + 32)))(b) for b in range(8)]
-        for k, nz in enumerate(ZPART):
-            weave(cmps[4 * k:4 * k + 4])
-            weave(zs[:nz])
-            zs = zs[nz:]
+        names_by_lane()
+        mms(HI_("W3"), [(HF("OCC", hf), A("BH", 256 * hf, 256 * hf + 256)) for hf in range(2)] + [(A("IB"), A("CT"))], True, False)
+        R = HI_("P7")
+        order = PARTS[:TPOS] + ((1, 0, 128), (1, 128, 256)) + PARTS[TPOS:]
+        for k, (q, lo, hi) in enumerate(order):
+            for r in range(4):
+                compare(q, r, lo, hi, k == 0 and r == 0)
+            weave(zs[:ZPART[k]])
+            zs = zs[ZPART[k]:]
+        mm(R, A("BO"), A("OCC"), True, False)
+        if t == 0:
+            first, rows_of_slots = meeting_constants()
+            weave(first)
         for hf in range(2):
             act(HF("HIT", hf), HF("P5", hf), AF.Sign)
-        mms(HI_("P6"), [(HF("HIT", hf), A("TT", 256 * hf, 256 * hf + 256)) for hf in range(2)], False, True)
+        mms(HI_("W3"), [(HF("HIT", hf), A("TT", 256 * hf, 256 * hf + 256)) for hf in range(2)], False, True)
         mm(R, A("BO"), A("HIT"), False, True)
         act(A("FS"), R, AF.Sign, bias=-8.5)
         act(A("OVR"), R, AF.Relu, bias=cS1, scale=-1.0)
         mms(LO_("P5"), [(A("N4"), A("OCC")), (A("N4"), A("OVR"))], True, False)
         for k in range(2):
-            ts(HF("TI", k), HF("P6", k, 256), SPREAD, OP.mult)
+            ts(HF("TI", k), HF("W3", k, 256), SPREAD, OP.mult)
         for k in range(2):
             ts(HF("TA", k), HF("TI", k), BITS, OP.bitwise_and)
-        tt(A("E0"), HF("TA", 0), HF("P6", 0), OP.add)
-        tt(HF("P6", 1), HF("TA", 1), HF("P6", 1), OP.add)
+        tt(A("E0"), HF("TA", 0), HF("W3", 0), OP.add)
+        tt(HF("W3", 1), HF("TA", 1), HF("W3", 1), OP.add)
         scan(A("INS"), A("FS"), A("ONES"), -192.0, OP.add, OP.add)
         for c in range(4):
             act(A("JK", 256 * c, 256 * c + 256), A("INS"), AF.Sign, bias=C("JB", c), scale=-1.0, acc=C("SA", c))
         act(A("FE"), R, AF.Sign, bias=0.5, scale=-1.0, acc=C("SA", 4))
         if not last:
             act(LO_("P4"), R, AF.Relu, bias=cCap, scale=4096.0)
+        if t == 0:
+            weave(rows_of_slots[:4])
         for s in range(4):
             e, o = "E%d" % (s % 2), 128 + 128 * (s % 2)
             e2, o2 = "E%d" % (1 - s % 2), 256 - 128 * (s % 2)
             for k in range(2):
                 for b, op in enumerate((OP.min, OP.max)):
                     if s == 3:
-                        out = A("P6", 128 * k + b, 128 * k + 128, 2)
+                        out = A("W3", 128 * k + b, 128 * k + 128, 2)
                     else:
-                        out = A(e2, b, 128, 2) if k == 0 else A("P6", o2 + b, o2 + 128, 2)
-                    tt(out, A(e, 64 * k, 64 * k + 64), A("P6", o + 64 * k, o + 64 * k + 64), op)
-            weave(zs[s:s + 1])
+                        out = A(e2, b, 128, 2) if k == 0 else A("W3", o2 + b, o2 + 128, 2)
+                    tt(out, A(e, 64 * k, 64 * k + 64), A("W3", o + 64 * k, o + 64 * k + 64), op)
+            if s % 2 == 0:
+                zs.pop(0)()
+            elif s == 1:
+                pass
+            else:
+                ts(A("SL"), A("SA", 0, 4), 0.5, OP.mult, 128.0, OP.add)
         for k in range(2):
-            tt(HF("KY", k), HF("P6", k), A("SPR"), OP.subtract)
+            tt(HF("KY", k), HF("W3", k), A("SPR"), OP.subtract)
             mm(HF("P5", k), HF("KY", k), A("IB"), False, k == 1)
-        ts(A("SL"), A("SA", 0, 4), 0.5, OP.mult, 128.0, OP.add)
         ts(C(MO, 0), C("SA", 4), -128.0, OP.min, -4096.0, OP.mult)
+        zs.pop(0)()
         scan(A("INE"), A("FE"), A("ONES"), 0.0, OP.add, OP.add)
         tt(LO_("STA"), LO_("P5"), A("OLD"), OP.max)
         ts(A("MSK"), A("JT"), C(MO, 0), OP.is_le, 4096.0, OP.mult)
@@ -463,67 +498,85 @@ def rank_program(g, core, T, topo):
         act(A("GA"), G("STA", 264, "SL", 0, 4))
         fold(A("P6", 256, 288), "FO", "GA", 0)
         tops = [] if last else pop()
-        weave(tops[:1])
-        for k in range(4):
-            cp(A("GU", k, 32, 4), A("P6", 256 + 8 * k, 264 + 8 * k))
+        weave(zs + tops[:1])
+        cp(A("GU"), A("P6", 256, 288))
         w = 512 // PIECES
         for k in range(PIECES):
             h = w // 2
             cp(A(LO, w * k, w * k + h), G("X", 2049, "GU", w * k // 16, (w * k + h) // 16))
             act(A(LO, w * k + h, w * k + w), G("X", 2049, "GU", (w * k + h) // 16, (w * k + w) // 16))
             send(LO, LI, "lb%d_%d" % (t, k), peer, w * k, w * k + w)
-        if t == 0:
-            later_constants = meeting_constants()
         mms(HI_("P5"), [(A("DN"), A("FE")), (A("DHF"), A("INE"))])
         place = [lambda: pick(HI_("P5")),
                  lambda: ts(A("RE"), A("SC", 15, 256, 16), cRe, OP.add, 7.0, OP.max)]
         mms(HI_("P7"), [(A("DN"), A("FS")), (A("DHF"), A("INS"))])
         if not last:
-            weave(place, tops[1:])
-            mm(LO_("P6"), A("BO"), A("TOP"), True, False)
+            weave(place)
+            act(A("TOP"), LO_("STA"))
+            mms(LO_("P6"), [(A("NBO"), A("ST1")), (A("BO"), A("TOP"))], True, False)
         else:
-            act(A("ST1"), LO_("STA"))
             weave(place)
             act(A("DK", 1, 1025), A("X", 1, 1025), scale=-1.0)
-            ts(A("DK", 1025, 2049), A("X", 1025, 2049), -1.0, OP.mult)
+            ts(A("DK", 1025, 1537), A("X", 1025, 1537), -1.0, OP.mult)
         if t == 0:
-            later_constants()
-        cp(A("RM"), A(MI, 8, MW))
-        act(A("RCV"), G(MI, MW, "RE", 0, 16))
+            weave(rows_of_slots[4:])
+            tt(A("ISH"), A("IB"), A("SH"), OP.subtract)
         fold(A("P5", 0, 32), "FO32", MI, 8)
+        cp(A("RM"), G(MI, MW, "LST", 80, 84))
+        if not last:
+            act(A("RCV"), G(MI, MW, "RE", 0, 16))
         for r in range(8):
+            if r == RPOS and not last:
+                mm(LO_("P6"), A("SR", 896, 1024), A("RCV"), False, True)
             mm(A("P4", r, 512, 8), A("SR", 128 * r, 128 * r + 128), A("RM"))
         cp(A("RV"), A("P5", 0, 32))
-        act(LO_("EX"), G("RV", 32, "LST", 0, 16))
-        tt(A("RVM"), A("P5", 0, 32), A("MSK"), OP.add)
-        cp(HI_("EX"), G("RV", 32, "LST", 16, 32))
-        for k in range(4):
-            act(A("RU", k, 32, 4), A("RV", 8 * k, 8 * k + 8))
+        act(A("EX", 0, 128), G("RV", 32, "LST", 48, 56))
+        cp(A("EX", 128, 256), G("RV", 32, "LST", 56, 64))
+        act(A("RU"), A("RV"))
+        act(HI_("EX"), G("RV", 32, "LST", 64, 80))
         act(A("OWN"), G("X", 2049, "RU", 0, 32))
-        if not last:
-            mm(LO_("P6"), A("SR", 896, 1024), A("RCV"), False, True)
+        if last:
+            act(A("DK", 1537, 2049), A("X", 1537, 2049), scale=-1.0)
+            act(A("ST1"), LO_("STA"))
+            act(A("RCV"), G(MI, MW, "RE", 0, 16))
         act(HI_("P7"), HI_("P7"), AF.Relu, bias=C(MI, 0), scale=-8192.0)
-        names = [] if last else lists_of_names()
-        tt(HI_("NE"), HI_("EX"), HI_("P4"), OP.not_equal)
-        tt(LO_("NE"), LO_("EX"), LO_("P4"), OP.not_equal)
-        sets = ((512, 384), (896, 256), (1152, 128))
-        for o, w in sets:
-            tt(A("NE", o, o + w), A("EX", 0, w), A("P4", 512 - w, 512), OP.is_equal)
-        scan(A("SB", 0, 512), A("N4K"), A("NE", 0, 512), 0.0, OP.add, OP.mult)
-        scan(A("SB", 512, 1280), A("RST"), A("NE", 512, 1280), 0.0, OP.max, OP.subtract)
-        mms(A("P5", 64, 96), [(A("IB"), A("RVM")), (A("IB"), A("SB", 15, 512, 16))]
-            + [(A("N4"), A("SB", o + 15, o + w, 16), A("P5", 64, 64 + w // 16)) for o, w in sets])
-        weave(names[:NPRE])
-        names = names[NPRE:]
-        for k in range(4):
-            ts(A("JO", k, 32, 4), A("P5", 64 + 8 * k, 72 + 8 * k), cWin, OP.add, cDum[k], OP.min)
+        names = [lambda: None] * 3 if last else lists_of_names()
+        sets = ((256, 192), (448, 128), (576, 64))
+
+        def equal_names(h):
+            e, o = 256 * h, 640 * h
+            return [lambda: tt(A("NE", o, o + 256), A("EX", e, e + 256), A("P4", e, e + 256), OP.not_equal)] + \
+                [(lambda s, w: lambda: tt(A("NE", o + s, o + s + w), A("EX", e, e + w), A("P4", e + 256 - w, e + 256),
+                                          OP.is_equal))(s, w) for s, w in sets]
+
+        def places(h):
+            o, sm = 640 * h, 64 + 16 * h
+            scan(A("SB", o, o + 256), A("N4K"), A("NE", o, o + 256), 0.0, OP.add, OP.mult)
+            scan(A("SB", o + 256, o + 640), A("RST"), A("NE", o + 256, o + 640), 0.0, OP.max, OP.subtract)
+            mms(A("P5", sm, sm + 16),
+                [(A("FO", 8 - 8 * e, 136 - 8 * e), A("RM", 32 * h + e, 32 * h + 32, 2)) for e in range(2)]
+                + [(A("IB"), A("MSK", 16 * h, 16 * h + 16)), (A("IB"), A("SB", o + 15, o + 256, 16))]
+                + [(A("N4"), A("SB", o + s + 15, o + s + w, 16), A("P5", sm, sm + w // 16)) for s, w in sets])
+
+        def offsets(h):
+            for k in range(4):
+                ts(A("JO", 16 * h + k, 16 * h + 16, 4), A("P5", 64 + 16 * h + 4 * k, 68 + 16 * h + 4 * k),
+                   cWin, OP.add, cDum[k], OP.min)
+        names[0]()
+        weave(equal_names(0))
+        places(0)
+        second = equal_names(1)
+        weave(names[1:] + second[:1])
+        offsets(0)
+        if not last:
+            neighbours("P7", 0)
 
         def stacks():
             tt(A("A1"), A("ST1"), HI_("P7"), OP.min)
-            mms(LO_("P7"), [(A("SH"), A("ST1")), (A("I8" if last else "I7"), A("RCV")), (A("ISH"), A("A1"))])
+            mms(HI_("P5"), [(A("SH"), A("ST1")), (A("I8" if last else "I7"), A("RCV")), (A("ISH"), A("A1"))])
 
         def stacks_out():
-            old_stacks(LO_("P7"))
+            old_stacks(HI_("P5"))
             mm(LO_("P5"), A("PERM"), A("OLD"))
             act(A("YS"), LO_("P5"), AF.Relu, bias=-1.0)
             dma("s", H(T.ystk[:, :]), A("YS"))
@@ -535,20 +588,25 @@ def rank_program(g, core, T, topo):
         join = [(lambda c: lambda: tt(G("X", XW, "JO", 4 * c, 4 * c + 4), part("OWN", c), part(LI, c), OP.max))(c) for c in range(8)]
         if last:
             best = [(lambda c: lambda: tt(part("OWN", c), part("OWN", c), part(LI, c), OP.max))(c) for c in range(8)]
-            join = [(lambda c: lambda: ts(G("DK", XW, "JO", 4 * c, 4 * c + 4), part("OWN", c), -1.0, OP.mult, 0.0, OP.add))(c)
-                    for c in range(8)]
-            weave(best[:2])
-            weave(join, best[2:4] + [stacks] + best[4:])
+            join0 = [(lambda c: lambda: ts(G("DK", XW, "JO", 4 * c, 4 * c + 4), part("OWN", c), -1.0, OP.mult, 0.0, OP.add))(c)
+                     for c in range(8)]
+            join = [(lambda c: lambda: weave([join0[c]] + best[c + 1:c + 2]))(c) for c in range(8)]
+            best[0]()
+        weave(second[1:2] + join[:1] + second[2:] + join[1:2])
+        places(1)
+        join[2]()
+        offsets(1)
+        if last:
+            weave(join[3:], [stacks])
             stacks_out()
         else:
-            weave(names)
-            neighbours()
             repeated_names()
-            weave(join[:BARE], [stacks])
+            act(A("KT"), LO_("P7"))
+            tile_lengths()
+            un = unique()
+            weave(join[3:], [stacks] + un[:3] + [lambda: weave(un[3:5])])
             lengths()
-            act(A("KT"), HI_("P5"))
-            old_stacks(LO_("P7"))
-            weave(join[BARE:], unique()[:5])
+            old_stacks(HI_("P5"))
 
     for q, e in enumerate("sasa"):
         dma(e, H(T.ylab[:, 512 * q:512 * q + 512]), A("DK", 1 + 512 * q, 513 + 512 * q))

@@ -1,47 +1,48 @@
-from concourse.mybir import AluOpType, ActivationFunctionType, AxisListType
+from concourse.mybir import AluOpType, ActivationFunctionType
 
 STEPS = 4
 XW = 2120
-ZPART = (0, 0, 0, 0, 1, 0, 3)
-TPOS = 0
-RPOS = 4
-XVV = 0
-DQ0 = 2
-OWN0 = 128
-OWN_LANES = 64
-DQ = 2
-PARTS = ((0, 0, 256), (2, 0, 256), (3, 0, 96), (3, 96, 192), (3, 192, 256))
-BARE = 3
-NPRE = 2
-DPRE = 4
-PIECES = 2
+ZFIRST = 2
+DQ = 4
+ZAT = (0, 0, 1, 0, 1, 1, 1)
+CUTS = ((0, 128), (128, 256))
+EXA = 128
+XVAT = 1
+ZPE = 0
+RCV1 = 0
+OWN0 = 256
+OWN = 256
+LOV = (128, 0)
+HALVES = ((1, 0, 128), (1, 128, 256))
+PARTS = ((0, 0, 256), (2, 0, 256), (3, 0, 128), (3, 128, 256))
 MW = 72
 
 F, B, I, U, NM = "float32", "bfloat16", "int32", "uint16", "float16"
 _S = {
-    "X": (XW, F), "D": (2064, F), "WB": (2064, B), "LABI": (2048, I), "NBI": (2064, I),
+    "X": (XW, F), "WB": (2064, B), "LABI": (2064, I), "NBI": (2064, I),
     "STI": (256, I), "CNI": (256, I), "CNF": (256, B), "XK": (4096, F), "XV": (256, F), "DK": (4096, F),
-    "CMP": (4096, B), "PI": (8, I), "COL": (48, F), "IM": (256, F), "IS": (256, F),
+    "CMP": (4096, B), "PI": (16, I), "COL": (48, F), "IS": (256, F),
     "M0": (144, B), "IW": (4 * 144, F), "TL": (4 * 144, B), "FO": (144, B), "SR": (1024, B),
-    "RV8": (8, F), "RV16": (16, F), "NI": (256, F), "GI": (256, F), "IP": (512, B), "TT": (512, B), "BH": (512, B),
-    "CT": (256, B), "ONES": (256, B), "DA": (48, F), "HOLD": (256, F), "LST": (84, U),
+    "NI": (256, B), "IP": (512, B), "TT": (512, B), "BH": (512, B),
+    "CT": (256, B), "ONES": (256, B), "DA": (16, F), "HOLD": (256, F), "LST": (84, U),
     "C4K": (512, B), "N4K": (256, B), "RST": (384, B), "SETS": (36, F), "JB": (4, F), "JT": (32, F), "E8T": (8, B), "FO32": (144, F),
-    "VF": (16, F), "VU": (16, U), "KA": (256, NM), "KT": (256, U), "WV": (256, B), "WK": (1024, B), "RVM": (32, NM),
+    "VF": (16, F), "VU": (16, U), "KA": (256, NM), "KT": (256, U), "WV": (256, B), "WF": (256, F), "WK": (1024, B),
     "SC": (256, F), "SB": (1280, B), "SM": (64, F), "EX": (512, NM), "EY": (256, NM), "ZO": (16, U), "JO": (32, U),
     "NE": (1280, B), "OVR": (256, B), "INS": (256, B), "INE": (256, B), "GA": (64, NM),
-    "ZS": (256, F), "HIT": (256, B), "TI": (256, I), "TA": (256, I), "E0": (128, F), "E1": (128, F), "KY": (256, NM), "SPR": (128, F),
-    "HV": (256, F), "STA": (264, F), "ST1": (256, NM), "TOP": (256, NM), "A1": (256, NM), "OLD": (256, NM),
+    "ZS": (256, F), "ZM": (256, F), "HIT": (256, B), "TI": (256, I), "TA": (256, I), "E0": (128, F), "E1": (128, F),
+    "KY": (256, NM), "SPR": (128, F), "STA": (264, F), "ST1": (256, NM), "TOP": (256, NM), "A1": (256, NM), "OLD": (256, NM),
     "OCC": (256, B), "FS": (256, B), "FE": (256, B), "JK": (1024, B), "SA": (8, F), "SL": (4, U), "GU": (32, U),
-    "RE": (16, U), "MSK": (32, B), "RM": (64, NM), "RV": (32, F), "RU": (32, U), "RCV": (256, NM), "OWN": (512, F),
-    "YS": (256, F), "YC": (256, F),
+    "RE": (16, U), "MSK": (32, B), "RM": (64, NM),
+    "RW": (32, F), "RU": (32, U), "RCV": (256, NM), "OWN": (512, F), "YS": (256, F), "YC": (256, F),
 }
 POOL = {}
-for _n, _d, _l in (("CB", B, "IB BO NBO E8 DG DN DHF N4 T2 PERM SH ISH I7 I8"),
+for _n, _d, _l in (("CB", B, "IB BO NBO E8 DG DN DHF N4 T2 PERM SH ISH I7 I8 IN SPH SPL ZERO"),
                    ("CF", F, "IG I32")):
     for _k, _c in enumerate(_l.split()):
         POOL[_c] = (_n, 128 * _k)
     _S[_n] = (128 * len(_l.split()), _d)
 for _t in range(STEPS):
+    _S["D%d" % _t] = (2064, F)
     _S["MO%d" % _t] = (MW, F)
     _S["MI%d" % _t] = (MW, F)
     _S["LO%d" % _t] = (512, F)
@@ -52,7 +53,7 @@ for _k in PSUM:
     SCRATCH[_k] = ("psum", [128, 512], F)
 NDMA = 20
 SEMAPHORES = ["ev", "ea", "ep", "eg", "sent"] + ["d%d" % k for k in range(NDMA)] + \
-    ["nm%d" % t for t in range(STEPS)] + ["lb%d_%d" % (t, k) for t in range(STEPS) for k in range(PIECES)]
+    ["nm%d" % t for t in range(STEPS)] + ["lb%d_%d" % (t, k) for t in range(STEPS) for k in range(2)]
 
 OP = AluOpType
 AF = ActivationFunctionType
@@ -146,15 +147,18 @@ def rank_program(g, core, T, topo):
         else:
             add("g", lambda: g.iota(o[0], pat, base, cm, allow_small_or_imprecise_dtypes=True), [o], [])
 
-    def sel(o, a, cmpop, fill, sg=1):
-        add("g", lambda: g.affine_select(o[0], a[0], [[sg, 128]], cmpop, fill, 0, -sg), [o], [a])
+    def select(o, a, pat, op, fill_, base):
+        add("g", lambda: g.affine_select(o[0], a[0], pat, op, fill_, base, 1), [o], [a])
 
     nd = [0]
 
-    def dma(q, o, a):
+    def dma(q, o, a, adding=False):
         s = "d%d" % nd[0]
         nd[0] += 1
-        add(q, lambda: Q[q].dma_start(o[0], a[0]), [o], [a], kind="d", sem=s)
+        if adding:
+            add(q, lambda: g.dma_start(o[0], a[0], accum_op=OP.add), [o], [a, o], kind="d", sem=s)
+        else:
+            add(q, lambda: Q[q].dma_start(o[0], a[0]), [o], [a], kind="d", sem=s)
 
     def H(ap):
         return (ap, [], [])
@@ -177,30 +181,16 @@ def rank_program(g, core, T, topo):
                     l.pop(0)()
 
     ms(A("NBI", 0, 4), -1)
+    ms(A("LABI", 0, 4), 0)
     ms(A("WB", 0, 8), 1.0)
     dma("s", A("CNI", p=8), H(T.cnt[:, :]))
     dma("a", A("STI"), H(T.stk[:, :]))
-    dma("a", A("NBI", 1025, 2049), H(T.nb[:, 1024:2048]))
-    dma("s", (T.NBI[:, 1:1025], [("NBI", 0, 1025, 1)], []), H(T.nb[:, 0:1024]))
-    for q, e in enumerate("sa"):
-        dma(e, A("LABI", 1024 * q, 1024 * q + 1024), H(T.lab[:, 1024 * q:1024 * q + 1024]))
+    for n_, src in (("NBI", T.nb), ("LABI", T.lab)):
+        dma("a", A(n_, 1025, 2049), H(src[:, 1024:2048]))
+        dma("s", (T[n_][:, 1:1025], [(n_, 0, 1025, 1)], []), H(src[:, 0:1024]))
     dma("s", (T.WB[:, 1:2049], [("WB", 0, 2064, 1)], []), H(T.ln[:, :]))
 
-    iota(C("PI", 0), [[0, 1]], 0, 1, True)
-    iota(A("RV8"), [[1, 2], [2, 2], [4, 2]])
-    iota(A("IM"), [[1, 256]])
-    iota(A("IG"), [[16, 8], [0, 16]])
-    iota(A("IS"), [[0, 16], [1, 16]])
-    iota(A("IW"), [[1, 576]])
-    iota(A("GI"), [[0, 16], [16, 16]])
-    iota(A("SETS", 0, 32), [[16, 2], [1, 4], [4, 4]])
-    iota(A("SETS", 32, 36), [[32, 2], [4, 2]])
-    ms(A("ONES"), 1.0)
-    for k, m in enumerate((15, 112, 1, 3, 12, 8)):
-        ts(C("PI", 1 + k), C("PI", 0), m, OP.bitwise_and)
-    cp(A("COL", 0, 7), A("PI", 0, 7))
-    cP, cA, cG, cOdd, cR, cQ, c8 = [C("COL", k) for k in range(7)]
-    ncol = [7]
+    ncol = [9]
 
     def col(src, m, a, op=OP.add):
         c = C("COL", ncol[0])
@@ -216,56 +206,23 @@ def rank_program(g, core, T, topo):
 
     def fill(o, c):
         iota(o, [[0, len(range(*o[1][0][1:]))]], c)
-    im, im16, im144 = A("IM", 0, 128), A("IM", 0, 16), A("IM", 0, 144)
-    for e in range(2):
-        ts(A("RV16", e, 16, 2), A("RV8"), 8.0 * e, OP.add)
-    c16, cG15, cG12, cG8 = cola(cP, 16.0, 0.0), cola(cG, 1.0, 15.0), cola(cG, 1.0, 12.0), cola(cG, 1.0, 8.0)
-    cWin, cP1 = cola(cA, -4096.0, 61440.0), cola(cP, 1.0, 128.0)
-    cTl, cFo = cola(cR, 1.0, cG12), cola(cA, 0.5, cG8)
-    act(A("LST", 0, 32), A("IM", 0, 32))
-    cTl = cola(cQ, 36.0, cTl)
-    ts(A("DA", 0, 16), im16, cA, OP.is_equal)
-    ts(A("IB"), im, cP, OP.is_equal)
-    tt(A("DA", 32, 48), A("DA", 0, 16), A("RV16"), OP.mult)
-    ts(A("E8"), A("IG"), c16, OP.is_equal)
-    cS = C("COL", 47)
-    add("v", lambda: g.vector.tensor_reduce(cS[0], A("DA", 32, 48)[0], AxisListType.X, OP.add), [cS], [A("DA", 32, 48)])
-    ts(A("BO"), A("IG"), cG, OP.is_equal)
-    cPerm, cS4, cCap = col(cS, 1.0, cG), col(cS, -4096.0, 0.0), col(cS, -4096.0, -4096.0)
-    ts(A("PERM"), im, cPerm, OP.is_equal)
-    cCap = col(C("DA", 15), -1048576.0, cCap)
-    ts(A("HOLD"), A("IS"), cA, OP.is_le, 1052672.0, OP.mult)
-    EXP = ("LST", 0, 16)
 
-    act(A("CNF", p=8), A("CNI", p=8))
-    act(A("TOP"), A("STI"))
-    mm(LO_("P4"), A("E8", p=8), A("CNF", p=8))
-    mms(LO_("P7"), [(A("PERM"), A("TOP")), (A("IB"), A("ONES"))])
-    act(A("HV"), LO_("P4"), AF.Relu, bias=cS4, scale=4096.0)
-    act(LO_("P4"), LO_("P4"), AF.Relu, bias=cCap, scale=4096.0)
-    ts(A("M0"), im144, cG15, OP.is_equal)
-    ts(A("TI", 0, 16), A("RV16"), SPREAD, OP.mult)
-    ts(A("FO"), im144, cFo, OP.is_equal)
-    ts(A("TA", 0, 16), A("TI", 0, 16), BITS, OP.bitwise_and)
-    tt(LO_("STA"), LO_("P7"), A("HV"), OP.min)
-    ts(A("HOLD"), A("HOLD"), -4096.0, OP.add)
-
-    def pop():
-        return [lambda: tt(A("ST1"), LO_("STA"), LO_("P4"), OP.min),
-                lambda: tt(A("TOP"), LO_("STA"), A("ST1"), OP.subtract)]
+    def diagonal(n_, c):
+        select(A(n_), A("ZERO"), [[-1, 128]], OP.not_equal, c, 0)
 
     def pick(src):
         scan(A("SC"), A("HOLD"), src, 0.0, OP.add, OP.min)
 
-    def lists_of_names():
-        return [lambda: pick(LO_("P6")),
-                lambda: ts(A("VU"), A("SC", 15, 256, 16), cWin, OP.add),
-                lambda: ts(A("VF"), A("SC", 15, 256, 16), cWin, OP.add)]
+    def lists_of_names(first=True):
+        if first:
+            pick(LO_("P6"))
+        for n_ in ("VU", "VF"):
+            act(A(n_), A("SC", 15, 256, 16), AF.Identity, bias=cWin)
 
-    def neighbours(bank, lo):
+    def neighbours(bank):
         act(A("KA"), G("NBI", 2049, "VU", 0, 16), AF.Identity, bias=1.0)
-        for q in range(4):
-            mms(A(bank, lo + 64 * q, lo + 64 * q + 64),
+        for q in (1, 0, 2, 3):
+            mms(A(bank, 64 * q, 64 * q + 64),
                 [(A("TL", 144 * q + 12 - 4 * e, 144 * q + 140 - 4 * e), A("KA", e, 256, 4)) for e in range(4)])
 
     def names_by_lane():
@@ -273,7 +230,9 @@ def rank_program(g, core, T, topo):
 
     def lengths():
         act(A("WV"), G("WB", 2049, "VU", 0, 16))
-        mm(HI_("P4"), A("IB"), A("WV"))
+
+    def wide_lengths():
+        select(A("WF"), A("WV"), [[0, 256]], OP.is_ge, 0.0, 0)
 
     def tile_lengths():
         act(A("WK"), G("WB", 2049, "KT", 64, 128))
@@ -291,185 +250,302 @@ def rank_program(g, core, T, topo):
                 lambda: tt(A("SM", 48, 56), A("SM", 48, 56), A("SM", 0, 16, 2), OP.add),
                 lambda: ts(A("ZO", 0, 16, 2), A("SM", 48, 56), cWin, OP.add, cDum[0], OP.min)]
 
-    def old_stacks(src):
-        act(A("OLD"), src)
-        act(A("OCC"), src, AF.Sign)
-
-    def scaled(o, a, c):
-        act(o, a, AF.Identity, scale=val(c))
-        ops[-1]["r"] += c[1] if isinstance(c, tuple) else []
-
-    weave(pop(), [lambda: tt(A("NI"), G("RV16", 16, *EXP), A("GI"), OP.add)])
-    mm(LO_("P6"), A("BO"), A("TOP"))
-    for hf in range(2):
-        ts(A("IP", 256 * hf, 256 * hf + 256), A("NI"), (cP, cP1)[hf], OP.is_equal)
-    sel(A("T2"), A("BO"), OP.is_gt, 0.0, -1)
-    fill(A("X", 0, 1), 0)
-    fill(A("D", 0, 1), 1)
-    fill(A("C4K"), 4096)
-    fill(A("STA", 256, 264), 0)
-    for t in range(STEPS):
-        fill(A("MO%d" % t, 0, 8), 0)
-    fill(A("N4K"), -4096)
-    iota(A("RST"), [[0, 24], [-16, 16]])
-    weave(lists_of_names(), [lambda: ts(A("TL"), A("IW"), cTl, OP.is_equal)])
-    cDg, cS1 = cola(cA, 1.0, -15.0), cola(cS, 1.0, 1.0)
-    cJb, cJt = cola(cA, -2.0, -65.0), cola(c8, 1024.0, 532480.0)
-    scaled(A("DG"), A("IB"), cDg)
-    cDum = [cola(cA, 1.0, 2049.0 + 16 * k) for k in range(4)]
-    act(A("JB"), A("IM", 0, 4), AF.Identity, bias=cJb, scale=-32.0)
-    act(A("JT"), A("SETS", 0, 32), AF.Identity, bias=cJt, scale=16384.0)
-    act(A("LST", 48, 80), A("SETS", 0, 32))
-    cSet = cola(cQ, 4.0, 8.0)
-    old_stacks(A("ST1"))
-    cSet = cola(c8, -3.75, cSet)
-    act(A("CT"), G("RV16", 16, *EXP), AF.Identity, bias=15.0, scale=-1.0)
-    cSet = cola(cR, 4.0, cSet)
-    act(A("I32"), A("IB"))
-    scaled(A("N4"), A("IB"), -4096.0)
-    cSet = cola(cOdd, -3.0, cSet)
-    mms(A("P7"), [(A("T2"), A("IP")), (A("DG"), A("IP"))])
-    mm(A("P4"), A("BO"), A("IP"))
-    act(A("TT"), A("P7"))
-    neighbours("P5", 256)
+    iota(C("PI", 0), [[0, 1]], 0, 1, True)
+    iota(A("IG"), [[16, 8], [0, 16]])
+    iota(A("IS"), [[0, 16], [1, 16]])
+    iota(A("IW"), [[1, 576]])
+    ms(A("ONES"), 1.0)
+    ms(A("ZERO"), 0.0)
+    for k, m in enumerate((15, 112, 1, 3, 12, 8, 2, 4)):
+        ts(C("PI", 1 + k), C("PI", 0), m, OP.bitwise_and)
+    ms(A("C4K"), 4096.0)
+    cp(A("COL", 0, 9), A("PI", 0, 9))
+    cP, cA, cG, cOdd, cR, cQ, c8, c2, c4 = [C("COL", k) for k in range(9)]
+    ms(A("N4K"), -4096.0)
+    ms(A("STA", 256, 264), 0.0)
+    ms(A("X", 0, 1), 0.0)
+    act(A("CNF", p=8), A("CNI", p=8))
+    act(A("TOP"), A("STI"), AF.Identity, bias=1.0)
+    ts(A("E8"), A("IG"), 1.0 / 16, OP.mult, cP, OP.is_equal)
+    ts(A("HOLD"), A("IS"), cA, OP.is_le, 1052672.0, OP.mult)
+    mm(LO_("P4"), A("E8", p=8), A("CNF", p=8))
+    ts(A("BO"), A("IG"), cG, OP.is_equal)
+    cTl = cola(cR, 1.0, cG)
+    cWin = cola(cA, -4096.0, 61440.0)
+    cTl = cola(cQ, 36.0, cTl)
+    cKeep = cola(cA, -4096.0, -4096.0)
+    ts(A("HOLD"), A("HOLD"), -4096.0, OP.add)
+    ts(LO_("P5"), LO_("P4"), -1.0, OP.add, cA, OP.is_equal)
+    im, im144 = A("IW", 0, 128), A("IW", 0, 144)
+    ts(A("IB"), im, cP, OP.is_equal)
+    ts(A("M0"), im144, -15.0, OP.add, cG, OP.is_equal)
+    tt(A("A1"), A("TOP"), LO_("P5"), OP.mult)
+    act(LO_("P4"), LO_("P4"), AF.Relu, bias=cKeep, scale=4096.0)
+    mm(LO_("P6"), A("BO"), A("A1"))
+    ts(A("TL"), A("IW"), -12.0, OP.add, cTl, OP.is_equal)
+    cS = cola(c8, 0.125, 0.0)
+    act(A("LST", 0, 16), A("IS", 0, 16))
+    cS = cola(c4, 0.5, cS)
+    cFo = cola(cA, 0.5, cG)
+    cS = cola(c2, 2.0, cS)
+    cDg = cola(cA, 1.0, -15.0)
+    cS = cola(cOdd, 8.0, cS)
+    cJb = cola(cA, -2.0, -65.0)
+    cPerm = cola(cS, 1.0, cG)
+    lists_of_names()
+    neighbours("P5")
     repeated_names()
-    for q in range(8):
-        cp(A("SPR", 16 * q, 16 * q + 16), A("TA", 0, 16))
-    cp(A("BH"), A("P4"))
+    cDum = [cola(cA, 1.0, 2049.0 + 16 * k) for k in range(4)]
+    act(A("KT"), LO_("P5"))
 
-    def labels(q, f):
-        f(A("X", 1 + 512 * q, 513 + 512 * q), A("LABI", 512 * q, 512 * q + 512))
+    for t in range(STEPS):
+        fill(A("D%d" % t, 0, 1), 1)
+    diagonal("I32", 1.0)
+    diagonal("IN", -1.0)
+    for k in range(4):
+        iota(A("NI", 64 * k, 64 * k + 64), [[4, 2], [8, 2], [16, 16]], k // 2 + 2 * (k % 2))
+    select(A("T2"), A("BO"), [[-1, 128]], OP.is_gt, 0.0, 0)
+
+    iota(A("SETS", 0, 32), [[16, 2], [1, 4], [4, 4]])
+    iota(A("SETS", 32, 36), [[32, 2], [4, 2]])
+    for k in range(4):
+        iota(A("CT", 64 * k, 64 * k + 64), [[-4, 2], [-8, 2], [0, 16]], 15 - k // 2 - 2 * (k % 2))
+    diagonal("N4", -4096.0)
+
+    def late_lists():
+        for t in range(STEPS):
+            fill(A("MO%d" % t, 0, 8), 0)
+        diagonal("DN", 32.5)
+        diagonal("DHF", -0.5)
+        for r in range(0, 8, 2):
+            select(A("SR", 128 * r, 128 * r + 256), A("ONES"), [[-2, 2], [-16, 8], [0, 16]], OP.is_equal, 0.0, -2 * r)
+        iota(A("RST"), [[0, 24], [-16, 16]])
+
+    tt(A("ST1"), A("TOP"), LO_("P4"), OP.min)
+    ts(A("PERM"), im, cPerm, OP.is_equal)
+    ts(A("DA"), A("IS", 0, 16), cA, OP.is_equal)
+    ts(C("TI", 0), cS, SPREAD, OP.mult)
+    ts(A("FO"), im144, -8.0, OP.add, cFo, OP.is_equal)
+    cEven, cRe, cCap = col(cOdd, -1.0, 1.0), col(cWin, 1.0, 39.5), col(cS, -4096.0, -4096.0)
+    for k, m in enumerate((BITS & ~0xFFFF, BITS & 0xFFFF)):
+        ts(C("TA", k), C("TI", 0), m, OP.bitwise_and)
+    mm(LO_("P7"), A("PERM"), A("ST1"))
     un = unique()
-    act(A("KT"), HI_("P5"))
-    for q in (2, 3, 0):
-        labels(q, lambda o, a: ts(o, a, -1.0, OP.mult))
-    labels(1, lambda o, a: act(o, a, scale=-1.0))
-    weave(un[:3])
-    cM1, cEven, cRe = col(cP, 1.0, -1.0), col(cOdd, -1.0, 1.0), col(cWin, 1.0, 39.5)
-    ts(A("E8T"), A("IM", 0, 8), 16.0, OP.mult, cG, OP.is_equal)
-    ts(A("SH"), im, cM1, OP.is_equal, cOdd, OP.mult)
-    c7 = col(C("DA", 14), -1.0, cEven)
+    cM1 = col(cP, 1.0, -1.0)
+    cCap, c7 = col(C("DA", 15), -1048576.0, cCap), col(C("DA", 14), -1.0, cEven)
+    ts(A("DG"), A("IB"), cDg, OP.mult)
+    cp(A("COL", 46, 48), A("TA", 0, 2))
+    ts(A("IP", 0, 256), A("NI"), cP, OP.is_equal)
+    ts(A("IP", 256, 512), A("NI"), -128.0, OP.add, cP, OP.is_equal)
+    ts(A("SPH"), A("IB"), C("COL", 46), OP.mult)
+    ts(A("SPL"), A("IB"), C("COL", 47), OP.mult)
+    weave(un[:2])
+    for lo, hi in ((1025, 2049), (1, 1025)):
+        ts(A("X", lo, hi), A("LABI", lo, hi), -1.0, OP.mult)
+    un[2]()
 
     def meeting_constants():
-        first = [lambda: scaled(A("DN"), A("IB"), 32.5), lambda: scaled(A("DHF"), A("IB"), -0.5),
-                 lambda: scaled(A("NBO"), A("BO"), -1.0), lambda: act(A("FO32"), A("FO")),
-                 lambda: act(A("LST", 80, 84), A("SETS", 32, 36), AF.Identity, bias=cSet),
-                 lambda: scaled(A("I8"), A("IB"), cEven), lambda: scaled(A("I7"), A("IB"), c7)]
-        return first, [(lambda r: lambda: scaled(A("SR", 128 * r, 128 * r + 128), A("BO"), C("DA", 2 * r)))(r) for r in range(8)]
+        cSet, cJt = cola(cQ, 4.0, 8.0), cola(c8, 1024.0, 532480.0)
+        cSet = cola(c8, -3.75, cSet)
+        act(A("JT"), A("SETS", 0, 32), AF.Identity, bias=cJt, scale=16384.0)
+        cSet = cola(cR, 4.0, cSet)
+        act(A("LST", 48, 80), A("SETS", 0, 32))
+        cSet = cola(cOdd, -3.0, cSet)
+        act(A("LST", 80, 84), A("SETS", 32, 36), AF.Identity, bias=cSet)
+
+    def flight_constants():
+        ts(A("SH"), im, cM1, OP.is_equal, cOdd, OP.mult)
+        ts(A("NBO"), A("BO"), -1.0, OP.mult)
+        ts(A("I8"), A("IB"), cEven, OP.mult)
+        ts(A("I7"), A("IB"), c7, OP.mult)
+        ts(A("E8T"), A("IS", 0, 8), 16.0, OP.mult, cG, OP.is_equal)
+        tt(A("ISH"), A("IB"), A("SH"), OP.subtract)
 
     def fold(o, by, src, lo):
         mms(o, [(A(by, 8 - 8 * e, 136 - 8 * e), A(src, lo + e, lo + 64, 2)) for e in range(2)])
 
-    P, Z = LO_("P4"), HI_("P4")
+    P, Z = LO_("P5"), HI_("P4")
+    NEW, R = LO_("W2"), HI_("W2")
+    HITS = ("P5", "P6")
+    LENGTHS = {4: ("P4", 0), 5: ("P5", 256)}
+    BY_DMA = 2048 - 256 * DQ
     for t in range(STEPS):
         last = t == STEPS - 1
         peer = T.cores[rank ^ (1 << (t % 2))]
-        MO, MI, LO, LI = "MO%d" % t, "MI%d" % t, "LO%d" % t, "LI%d" % t
+        D, MO, MI, LO, LI = ["%s%d" % (n_, t) for n_ in ("D", "MO", "MI", "LO", "LI")]
+
+        def gathered(o, win, on, c, d):
+            if win == "X" and t == 0:
+                act(o, G("LABI", 2049, on, c, d), scale=-1.0)
+            else:
+                act(o, G(win, 2049, on, c, d))
 
         def gather(o, win, q, lo=0, hi=256):
-            act(A(o, 1024 * q + 4 * lo, 1024 * q + 4 * hi), G(win, 2049, "KT", 64 * q + lo // 4, 64 * q + hi // 4))
+            gathered(A(o, 1024 * q + 4 * lo, 1024 * q + 4 * hi), win, "KT", 64 * q + lo // 4, 64 * q + hi // 4)
 
         def nbr(n, q, r, lo=0, hi=256):
             return A(n, 1024 * q + 4 * lo + r, 1024 * q + 4 * hi, 4)
-        n = OWN_LANES if t else OWN0
-        gather("XK", "X", 1, 0, 128)
-        gather("XK", "X", 1, 128, 256)
-        if not XVV:
-            act(A("XV"), G("X", 2049, "VU", 0, 16))
-        dq = DQ if t else DQ0
-        for q in range(4):
-            if t == 0 or q == 3:
-                mm(A("W%d" % q), A("IB"), A("WB", 1 + 512 * q, 513 + 512 * q), True, q < 3 or dq == 0)
-        if dq:
-            mm(A("W3", 512 - 256 * dq, 512), A("I32"), A("X", 2049 - 256 * dq, 2049), False, True)
-        if t == 0:
-            lengths()
-        gather("XK", "X", 2)
-        if n < 256:
-            gather("XK", "X", 3, n)
-        if dq:
-            act(A("D", 2049 - 256 * dq, 2049), A("W3", 512 - 256 * dq, 512))
-        parts = PARTS if t else PARTS[:TPOS] + ((1, 0, 128), (1, 128, 256)) + PARTS[TPOS:]
-        for hf in range(2 if t else 0):
-            mms(A("P%d" % (6 + hf)), [(A("IB"), A("WK", 512 * hf, 512 * hf + 512)),
-                                      (A("I32"), A("XK", 1024 + 512 * hf, 1536 + 512 * hf))])
-        dd = [(lambda q: lambda: tt(A("D", 1 + 256 * q, 257 + 256 * q), A("X", 1 + 256 * q, 257 + 256 * q),
-                                    A("W%d" % (q // 2), 256 * (q % 2), 256 * (q % 2) + 256), OP.add))(q) for q in range(8 - dq)]
-
-        def fold_in(i):
-            lo = n if i // 4 == 2 else 0
-            c = A("P4", 256 * (1 - i % 2) + lo, 256 * (2 - i % 2))
-            tt(A("ZS") if i == 14 else c, nbr("XK", i // 4, i % 4, lo), c, OP.max)
 
         def own(q, q2, lo, hi):
             tt(A("XK", 1024 * q + 4 * lo, 1024 * q + 4 * hi), G("X", 2049, "KT", 64 * q + lo // 4, 64 * q + hi // 4),
                A("XK", 1024 * q2 + 4 * lo, 1024 * q2 + 4 * hi), OP.max)
-        if XVV:
-            cp(A("XV"), G("X", 2049, "VU", 0, 16))
-        weave(dd[:DPRE] if t else [])
-        own(0, 1, 0, 128)
-        weave(dd[DPRE:DPRE + 2] if t else un[3:5])
-        own(0, 1, 128, 256)
-        weave(dd[DPRE + 2:] if t else dd)
-        tt(Z, A("XV"), Z, OP.add)
-        tt(P, nbr("XK", 0, 0), nbr("XK", 0, 1), OP.max)
-        for i in (2, 3):
-            fold_in(i)
-        if n:
-            own(3, 2, 0, n)
-        for i in range(8 if n < 256 else 12, 16):
-            fold_in(i)
-        for q, lo, hi in parts:
-            gather("DK", "D", q, lo, hi)
-        weave(un[5:7], [lambda: tt(P, A("ZS"), P, OP.max),
-                        lambda: tt(A("ZS"), P, A("WV"), OP.subtract)])
-        tt(Z, P, A("WV"), OP.subtract)
-        un[7]()
 
-        def compare(q, r, lo, hi, first):
+        def add_lengths(q):
+            bank, at = LENGTHS[q] if t and q >= 4 else ("W%d" % (q // 2), 256 * (q % 2))
+            w = 255 if t and q == 7 - DQ else 256
+            return lambda: tt(A(D, 1 + 256 * q, 1 + 256 * q + w), A("X", 1 + 256 * q, 1 + 256 * q + w), A(bank, at, at + w), OP.add)
+
+        def heights():
+            mms(HI_("W3"), [(HF("OCC", hf), A("BH", 256 * hf, 256 * hf + 256)) for hf in range(2)], False, False)
+            mm(R, A("BO"), A("OCC"), True, False)
+        n = OWN if t else OWN0
+        cuts = CUTS if t else ((0, 128), (128, 256))
+        if t:
+            if DQ:
+                dma("g", A(D, BY_DMA, 2049), A("X", BY_DMA, 2049), True)
+                names_by_lane()
+                mm(HI_("W3"), A("IB"), A("CT"), True, False)
+                heights()
+            else:
+                mm(A("W3"), A("I32"), A("X", 1537, 2049), False, True)
+            for lo, hi in cuts:
+                gather("XK", "X", 1, lo, hi)
+                if lo < 128 <= hi:
+                    mm(A("P6"), A("I32"), A("XK", 1024, 1536), False, True)
+        else:
+            for hf in range(2):
+                gather("XK", "X", 1, 128 * hf, 128 * hf + 128)
+            lengths()
+            for q in range(4):
+                if q == 2:
+                    mm(Z, A("IB"), A("WV"))
+                mm(A("W%d" % q), A("IB"), A("WB", 1 + 512 * q, 513 + 512 * q), True, q < 3)
+            mm(A("W3"), A("I32"), A("X", 1537, 2049), False, True)
+        wide_lengths()
+        for hf in range(2):
+            gather("XK", "X", 2, 128 * hf, 128 * hf + 128)
+            if hf == XVAT:
+                gathered(A("XV"), "X", "VU", 0, 16)
+        dd = [add_lengths(q) for q in range(8 - DQ if t and DQ else 6)]
+        weave(dd[:4] if t else [])
+        for lo, hi in cuts:
+            own(0, 1, lo, hi)
+        weave(dd[4:] if t else [])
+        if t:
+            mm(A("P7"), A("I32"), A("XK", 1536, 2048), False, True)
+        act(P, nbr("XK", 0, 0))
+        if n < 256:
+            gather("XK", "X", 3, n, 256)
+        if t and not DQ:
+            act(A(D, 1537, 2049), A("W3"))
+            names_by_lane()
+            mm(HI_("W3"), A("IB"), A("CT"), True, False)
+            heights()
+        if t == 0:
+            act(A(D, 1537, 2049), A("W3"))
+            late_lists()
+            for u in range(1, STEPS if DQ else 0):
+                dma("g", A("D%d" % u, BY_DMA, 2049), A("WB", BY_DMA, 2049))
+            weave(dd, un[3:])
+            act(A("OCC"), LO_("P7"), AF.Sign)
+            act(A("OLD"), LO_("P7"))
+            cS1 = cola(cS, 1.0, 1.0)
+            act(A("JB"), A("IS", 0, 4), AF.Identity, bias=cJb, scale=-32.0)
+        own(3, 2, 0, min(n, 128))
+        if n > 128:
+            own(3, 2, 128, n)
+        tt(Z, A("XV"), Z, OP.add)
+        if t == 0:
+            mms(A("P6"), [(A("T2"), A("IP")), (A("DG"), A("IP"))])
+            mm(A("P7"), A("BO"), A("IP"))
+            mms(A("W2", 0, 128), [(A("ONES", 0, 128), A("SPH")), (A("ONES", 0, 128), A("SPL"))])
+            names_by_lane()
+            mm(HI_("W3"), A("IB"), A("CT"), True, False)
+        order = [(0, 1), (0, 2), (0, 3), (3, 0), (3, 1), (3, 2)]
+        if n < 256:
+            order[2:2] = [(2, 0), (2, 1)]
+            order[6:6] = [(2, 2), (2, 3)]
+        for k, (q, r) in enumerate(order):
+            lo = n if q == 2 else 0
+            c = A("P4", 256 + lo, 512) if k % 2 else A("P5", lo, 256)
+            tt(A("ZS") if (q, r) == (3, 2) else c, nbr("XK", q, r, lo), c, OP.max)
+        for hf in range(2):
+            tt(HF("P5", hf), nbr("XK", 3, 3, 128 * hf, 128 * hf + 128), HF("P5", hf), OP.max)
+        weave(un[7:] if t else [])
+        for hf in range(2):
+            tt(HF("ZM", hf), HF("ZS", hf), HF("P5", hf), OP.max)
+        if t == 0:
+            cp(A("TT"), A("P6"))
+            tt(Z, A("ZM"), A("WV"), OP.subtract)
+        for part_ in (PARTS if t else HALVES + PARTS):
+            gather("DK", D, *part_)
+            if t == 0 and part_ == PARTS[0]:
+                act(A("BH"), A("P7"))
+                act(A("SPR"), A("W2", 0, 128))
+        if t:
+            act(A("OLD"), NEW)
+
+        def compare(q, r, lo, hi):
             i = 4 * q + r
             c = A("CMP", 256 * i + lo, 256 * i + hi)
             if q == 1 and t:
-                tt(c, A("P%d" % (6 + lo // 128), r, 512, 4), A("ZS", lo, hi), OP.is_lt)
+                tt(c, A("P%d" % (6 + lo // 128), r, 512, 4), A("ZM", lo, hi), OP.is_lt)
             else:
                 tt(c, nbr("DK", q, r, lo, hi), A("P4", 256 + lo, 256 + hi), OP.is_lt)
-            mm(A("P5", lo, hi), A("M0", 15 - i, 143 - i), c, first, i == 15 and hi == 256)
-        zs = [(lambda b: lambda: cp(G("X", XW, "ZO", 2 * b, 2 * b + 2), A("ZS", 32 * b, 32 * b + 32)))(b) for b in range(8)]
-        names_by_lane()
-        mms(HI_("W3"), [(HF("OCC", hf), A("BH", 256 * hf, 256 * hf + 256)) for hf in range(2)] + [(A("IB"), A("CT"))], True, False)
-        R = HI_("P7")
-        order = PARTS[:TPOS] + ((1, 0, 128), (1, 128, 256)) + PARTS[TPOS:]
-        for k, (q, lo, hi) in enumerate(order):
-            for r in range(4):
-                compare(q, r, lo, hi, k == 0 and r == 0)
-            weave(zs[:ZPART[k]])
-            zs = zs[ZPART[k]:]
-        mm(R, A("BO"), A("OCC"), True, False)
+            for hf in range(2 if i < 15 else 0):
+                a, b = max(lo, 128 * hf), min(hi, 128 * hf + 128)
+                if a < b:
+                    mm(A(HITS[hf], a, b), A("M0", 15 - i, 143 - i), A("CMP", 256 * i + a, 256 * i + b),
+                       i == 4 and a == 128 * hf, i == 14 and b == 128 * hf + 128)
+        zs = [(lambda b: lambda: tt(G("X", XW, "ZO", 2 * b, 2 * b + 2), A("ZM", 32 * b, 32 * b + 32),
+                                    A("WF", 32 * b, 32 * b + 32), OP.subtract))(b) for b in range(8)]
+
+        def write(n):
+            for _ in range(n):
+                zs.pop(0)()
         if t == 0:
-            first, rows_of_slots = meeting_constants()
-            weave(first)
+            write(1)
+        for q, lo, hi in HALVES + PARTS:
+            if (q, lo, hi) == HALVES[1] and t:
+                tt(Z, A("ZM"), A("WV"), OP.subtract)
+            if (q, lo, hi) == PARTS[-2] and t == 0:
+                heights()
+            for r in range(4 if q < 3 else 3):
+                compare(q, r, lo, hi)
+        compare(3, 3, 0, 256)
         for hf in range(2):
-            act(HF("HIT", hf), HF("P5", hf), AF.Sign)
-        mms(HI_("W3"), [(HF("HIT", hf), A("TT", 256 * hf, 256 * hf + 256)) for hf in range(2)], False, True)
-        mm(R, A("BO"), A("HIT"), False, True)
+            act(HF("HIT", hf), HF(HITS[hf], hf), AF.Sign)
+            mm(HI_("W3"), HF("HIT", hf), A("TT", 256 * hf, 256 * hf + 256), False, hf == 1)
+            if hf == 0:
+                mm(LO_("P7"), A("BO"), A("CMP", 3840, 4096))
+        mm(R, A("BO"), A("HIT"), False, False)
+        act(A("FS"), LO_("P7"), AF.Sign)
+        mm(R, A("IB"), A("FS"), False, True)
         act(A("FS"), R, AF.Sign, bias=-8.5)
         act(A("OVR"), R, AF.Relu, bias=cS1, scale=-1.0)
         mms(LO_("P5"), [(A("N4"), A("OCC")), (A("N4"), A("OVR"))], True, False)
+        write(ZFIRST if t else ZFIRST - 1)
         for k in range(2):
             ts(HF("TI", k), HF("W3", k, 256), SPREAD, OP.mult)
+        write(1)
         for k in range(2):
             ts(HF("TA", k), HF("TI", k), BITS, OP.bitwise_and)
+        write(ZAT[0])
         tt(A("E0"), HF("TA", 0), HF("W3", 0), OP.add)
         tt(HF("W3", 1), HF("TA", 1), HF("W3", 1), OP.add)
         scan(A("INS"), A("FS"), A("ONES"), -192.0, OP.add, OP.add)
+        act(A("FE"), R, AF.Sign, bias=0.5, scale=-1.0, acc=C("SA", 4))
         for c in range(4):
             act(A("JK", 256 * c, 256 * c + 256), A("INS"), AF.Sign, bias=C("JB", c), scale=-1.0, acc=C("SA", c))
-        act(A("FE"), R, AF.Sign, bias=0.5, scale=-1.0, acc=C("SA", 4))
-        if not last:
-            act(LO_("P4"), R, AF.Relu, bias=cCap, scale=4096.0)
+        act(A("SL"), A("SA", 0, 4), AF.Identity, bias=128.0, scale=0.5)
+        spare = [lambda: None, lambda: ts(C(MO, 0), C("SA", 4), -128.0, OP.min, -4096.0, OP.mult),
+                 lambda: scan(A("INE"), A("FE"), A("ONES"), 0.0, OP.add, OP.add),
+                 lambda: ts(A("MSK"), A("JT"), C(MO, 0), OP.is_le, 4096.0, OP.mult)]
         if t == 0:
-            weave(rows_of_slots[:4])
+            spare.insert(3, lambda: cp(A("FO32"), A("FO")))
         for s in range(4):
+            write(ZAT[1 + s])
+            spare[s]()
             e, o = "E%d" % (s % 2), 128 + 128 * (s % 2)
             e2, o2 = "E%d" % (1 - s % 2), 256 - 128 * (s % 2)
             for k in range(2):
@@ -479,68 +555,47 @@ def rank_program(g, core, T, topo):
                     else:
                         out = A(e2, b, 128, 2) if k == 0 else A("W3", o2 + b, o2 + 128, 2)
                     tt(out, A(e, 64 * k, 64 * k + 64), A("W3", o + 64 * k, o + 64 * k + 64), op)
-            if s % 2 == 0:
-                zs.pop(0)()
-            elif s == 1:
-                pass
-            else:
-                ts(A("SL"), A("SA", 0, 4), 0.5, OP.mult, 128.0, OP.add)
+            if s == 2:
+                mms(LO_("P7"), [(A("DN"), A("FS")), (A("DHF"), A("INS"))])
+                mms(HI_("P7"), [(A("DN"), A("FE")), (A("DHF"), A("INE"))])
+        if not last:
+            act(R, R, AF.Relu, bias=cCap, scale=4096.0)
+        if t == 0:
+            meeting_constants()
+        write(ZAT[5])
         for k in range(2):
             tt(HF("KY", k), HF("W3", k), A("SPR"), OP.subtract)
             mm(HF("P5", k), HF("KY", k), A("IB"), False, k == 1)
-        ts(C(MO, 0), C("SA", 4), -128.0, OP.min, -4096.0, OP.mult)
-        zs.pop(0)()
-        scan(A("INE"), A("FE"), A("ONES"), 0.0, OP.add, OP.add)
+        pick(HI_("P7"))
         tt(LO_("STA"), LO_("P5"), A("OLD"), OP.max)
-        ts(A("MSK"), A("JT"), C(MO, 0), OP.is_le, 4096.0, OP.mult)
-        cp(A(MO, 8, MW), G("STA", 264, "SL", 0, 4))
+        write(ZAT[6])
+        ts(A("RE"), A("SC", 15, 256, 16), cRe, OP.add, 7.0, OP.max)
+        act(A(MO, 8, MW), G("STA", 264, "SL", 0, 4))
         send(MO, MI, "nm%d" % t, peer, 0, MW)
         act(A("GA"), G("STA", 264, "SL", 0, 4))
         fold(A("P6", 256, 288), "FO", "GA", 0)
-        tops = [] if last else pop()
-        weave(zs + tops[:1])
-        cp(A("GU"), A("P6", 256, 288))
-        w = 512 // PIECES
-        for k in range(PIECES):
-            h = w // 2
-            cp(A(LO, w * k, w * k + h), G("X", 2049, "GU", w * k // 16, (w * k + h) // 16))
-            act(A(LO, w * k + h, w * k + w), G("X", 2049, "GU", (w * k + h) // 16, (w * k + w) // 16))
-            send(LO, LI, "lb%d_%d" % (t, k), peer, w * k, w * k + w)
-        mms(HI_("P5"), [(A("DN"), A("FE")), (A("DHF"), A("INE"))])
-        place = [lambda: pick(HI_("P5")),
-                 lambda: ts(A("RE"), A("SC", 15, 256, 16), cRe, OP.add, 7.0, OP.max)]
-        mms(HI_("P7"), [(A("DN"), A("FS")), (A("DHF"), A("INS"))])
         if not last:
-            weave(place)
-            act(A("TOP"), LO_("STA"))
-            mms(LO_("P6"), [(A("NBO"), A("ST1")), (A("BO"), A("TOP"))], True, False)
-        else:
-            weave(place)
-            act(A("DK", 1, 1025), A("X", 1, 1025), scale=-1.0)
-            ts(A("DK", 1025, 1537), A("X", 1025, 1537), -1.0, OP.mult)
-        if t == 0:
-            weave(rows_of_slots[4:])
-            tt(A("ISH"), A("IB"), A("SH"), OP.subtract)
-        fold(A("P5", 0, 32), "FO32", MI, 8)
-        cp(A("RM"), G(MI, MW, "LST", 80, 84))
-        if not last:
-            act(A("RCV"), G(MI, MW, "RE", 0, 16))
-        for r in range(8):
-            if r == RPOS and not last:
-                mm(LO_("P6"), A("SR", 896, 1024), A("RCV"), False, True)
-            mm(A("P4", r, 512, 8), A("SR", 128 * r, 128 * r + 128), A("RM"))
-        cp(A("RV"), A("P5", 0, 32))
-        act(A("EX", 0, 128), G("RV", 32, "LST", 48, 56))
-        cp(A("EX", 128, 256), G("RV", 32, "LST", 56, 64))
-        act(A("RU"), A("RV"))
-        act(HI_("EX"), G("RV", 32, "LST", 64, 80))
-        act(A("OWN"), G("X", 2049, "RU", 0, 32))
+            tt(A("ST1"), LO_("STA"), R, OP.min)
+        write(len(zs))
+        act(A("GU"), A("P6", 256, 288))
+        for k in range(2):
+            w = LOV[k]
+            if w:
+                cp(A(LO, 256 * k, 256 * k + w), G("X", 2049, "GU", 16 * k, 16 * k + w // 16))
+            if w < 256:
+                act(A(LO, 256 * k + w, 256 * k + 256), G("X", 2049, "GU", 16 * k + w // 16, 16 * k + 16))
+            send(LO, LI, "lb%d_%d" % (t, k), peer, 256 * k, 256 * k + 256)
         if last:
-            act(A("DK", 1537, 2049), A("X", 1537, 2049), scale=-1.0)
             act(A("ST1"), LO_("STA"))
-            act(A("RCV"), G(MI, MW, "RE", 0, 16))
-        act(HI_("P7"), HI_("P7"), AF.Relu, bias=C(MI, 0), scale=-8192.0)
-        names = [lambda: None] * 3 if last else lists_of_names()
+            ts(A("DK", 1, 1025), A("X", 1, 1025), -1.0, OP.mult)
+        else:
+            act(A("TOP"), LO_("STA"))
+            if RCV1:
+                mms(LO_("P6"), [(A("NBO"), A("ST1")), (A("BO"), A("TOP"))], True, False)
+        if t == 0:
+            spare[4]()
+            flight_constants()
+
         sets = ((256, 192), (448, 128), (576, 64))
 
         def equal_names(h):
@@ -549,64 +604,106 @@ def rank_program(g, core, T, topo):
                 [(lambda s, w: lambda: tt(A("NE", o + s, o + s + w), A("EX", e, e + w), A("P4", e + 256 - w, e + 256),
                                           OP.is_equal))(s, w) for s, w in sets]
 
-        def places(h):
+        def counts(h):
             o, sm = 640 * h, 64 + 16 * h
-            scan(A("SB", o, o + 256), A("N4K"), A("NE", o, o + 256), 0.0, OP.add, OP.mult)
-            scan(A("SB", o + 256, o + 640), A("RST"), A("NE", o + 256, o + 640), 0.0, OP.max, OP.subtract)
-            mms(A("P5", sm, sm + 16),
-                [(A("FO", 8 - 8 * e, 136 - 8 * e), A("RM", 32 * h + e, 32 * h + 32, 2)) for e in range(2)]
-                + [(A("IB"), A("MSK", 16 * h, 16 * h + 16)), (A("IB"), A("SB", o + 15, o + 256, 16))]
-                + [(A("N4"), A("SB", o + s + 15, o + s + w, 16), A("P5", sm, sm + w // 16)) for s, w in sets])
+
+            def later_sets():
+                scan(A("SB", o + 256, o + 640), A("RST"), A("NE", o + 256, o + 640), 0.0, OP.max, OP.subtract)
+                mms(A("P5", sm, sm + 16),
+                    [(A("IB"), A("EX", 256 * h, 256 * h + 256, 16)), (A("IB"), A("MSK", 16 * h, 16 * h + 16)),
+                     (A("IB"), A("SB", o + 15, o + 256, 16))]
+                    + [(A("N4"), A("SB", o + s + 15, o + s + w, 16), A("P5", sm, sm + w // 16)) for s, w in sets])
+            return [lambda: scan(A("SB", o, o + 256), A("N4K"), A("NE", o, o + 256), 0.0, OP.add, OP.mult), later_sets]
 
         def offsets(h):
             for k in range(4):
                 ts(A("JO", 16 * h + k, 16 * h + 16, 4), A("P5", 64 + 16 * h + 4 * k, 68 + 16 * h + 4 * k),
                    cWin, OP.add, cDum[k], OP.min)
-        names[0]()
-        weave(equal_names(0))
-        places(0)
-        second = equal_names(1)
-        weave(names[1:] + second[:1])
-        offsets(0)
+        fold(A("P5", 0, 32), "FO32", MI, 8)
+        cp(A("RM"), G(MI, MW, "LST", 80, 84))
+        early = RCV1 and not last
+        if early:
+            act(A("RCV"), G(MI, MW, "RE", 0, 16))
+        act(A("RW"), A("P5", 0, 32))
+        act(A("RU"), A("P5", 0, 32))
+        for r in range(8):
+            if early and r == RCV1:
+                mm(LO_("P6"), A("SR", 896, 1024), A("RCV"), False, True)
+            mm(A("P4", r, 512, 8), A("SR", 128 * r, 128 * r + 128), A("RM"))
+        act(A("EX", 0, EXA), G("RW", 16, "LST", 48, 48 + EXA // 16))
+        if EXA < 256:
+            cp(A("EX", EXA, 256), G("RW", 16, "LST", 48 + EXA // 16, 64))
+        if early:
+            pick(LO_("P6"))
+        else:
+            act(A("RCV"), G(MI, MW, "RE", 0, 16))
+            if not last:
+                mms(LO_("P6"), [(A("NBO"), A("ST1")), (A("BO"), A("TOP")), (A("SR", 896, 1024), A("RCV"))])
+        act(HI_("EX"), G("RW", 32, "LST", 64, 80))
+        act(A("OWN"), G("X", 2049, "RU", 0, 32))
+        one, two = equal_names(0) + counts(0), equal_names(1) + counts(1)
+        if last:
+            act(A("DK", 1025, 1793), A("X", 1025, 1793), scale=-1.0)
+        weave([one[k] for k in (2, 3, 0, 1)])
+        if last:
+            ts(A("DK", 1793, 2049), A("X", 1793, 2049), -1.0, OP.mult)
+        elif early:
+            lists_of_names(False)
+            two.pop(0)()
+            two.insert(0, lambda: None)
+        else:
+            lists_of_names()
+        weave(one[4:])
         if not last:
-            neighbours("P7", 0)
+            neighbours("W3")
+        act(LO_("P7"), LO_("P7"), AF.Relu, bias=C(MI, 0), scale=-8192.0)
+        if not last:
+            repeated_names()
+            act(A("KT"), LO_("W3"))
+            lengths()
+            tile_lengths()
+        weave(two[:2])
+        offsets(0)
+        weave(two[2:4])
 
         def stacks():
-            tt(A("A1"), A("ST1"), HI_("P7"), OP.min)
-            mms(HI_("P5"), [(A("SH"), A("ST1")), (A("I8" if last else "I7"), A("RCV")), (A("ISH"), A("A1"))])
+            tt(A("A1"), A("ST1"), LO_("P7"), OP.min)
+            mms(NEW, [(A("SH"), A("ST1")), (A("I8" if last else "I7"), A("RCV")), (A("ISH"), A("A1"))])
 
         def stacks_out():
-            old_stacks(HI_("P5"))
-            mm(LO_("P5"), A("PERM"), A("OLD"))
-            act(A("YS"), LO_("P5"), AF.Relu, bias=-1.0)
+            act(A("OLD"), NEW)
+            act(A("OCC"), NEW, AF.Sign)
+            mm(LO_("P7"), A("PERM"), A("OLD"))
+            act(A("YS"), LO_("P7"), AF.Relu, bias=-1.0)
             dma("s", H(T.ystk[:, :]), A("YS"))
             mm(A("P6", 0, 256, p=8), A("E8T"), A("OCC"))
             act(A("YC", p=8), A("P6", 0, 256, p=8))
             dma("s", H(T.ycnt[:, :]), A("YC", p=8))
-        def part(n, c):
-            return A(n, 64 * c, 64 * c + 64)
-        join = [(lambda c: lambda: tt(G("X", XW, "JO", 4 * c, 4 * c + 4), part("OWN", c), part(LI, c), OP.max))(c) for c in range(8)]
+        def part(n, c, w=1):
+            return A(n, 64 * c, 64 * (c + w))
         if last:
-            best = [(lambda c: lambda: tt(part("OWN", c), part("OWN", c), part(LI, c), OP.max))(c) for c in range(8)]
-            join0 = [(lambda c: lambda: ts(G("DK", XW, "JO", 4 * c, 4 * c + 4), part("OWN", c), -1.0, OP.mult, 0.0, OP.add))(c)
-                     for c in range(8)]
-            join = [(lambda c: lambda: weave([join0[c]] + best[c + 1:c + 2]))(c) for c in range(8)]
-            best[0]()
-        weave(second[1:2] + join[:1] + second[2:] + join[1:2])
-        places(1)
-        join[2]()
-        offsets(1)
-        if last:
-            weave(join[3:], [stacks])
+            best = [(lambda c: lambda: tt(part("OWN", c, 2), part("OWN", c, 2), part(LI, c, 2), OP.max))(c) for c in range(0, 8, 2)]
+            join = [(lambda c: lambda: ts(G("DK", XW, "JO", 4 * c, 4 * c + 4), part("OWN", c), -1.0, OP.mult, 0.0, OP.add))(c)
+                    for c in range(8)]
+            weave(best[:1] + two[4:])
+            weave(join[:4], [best[1], lambda: offsets(1), best[2], stacks])
             stacks_out()
+            weave(join[4:], best[3:])
         else:
-            repeated_names()
-            act(A("KT"), LO_("P7"))
-            tile_lengths()
+            join = [(lambda c: lambda: tt(G("X", XW, "JO", 4 * c, 4 * c + 4), part("OWN", c), part(LI, c), OP.max))(c) for c in range(8)]
             un = unique()
-            weave(join[3:], [stacks] + un[:3] + [lambda: weave(un[3:5])])
-            lengths()
-            old_stacks(HI_("P5"))
+            weave(join, [lambda: weave(two[4:]), stacks, lambda: offsets(1)] + un[:3]
+                  + [lambda: weave(un[3:5]), lambda: weave(un[5:7])])
+            for q in range(4, 8 - (DQ or 2)):
+                mm(A(LENGTHS[q][0], LENGTHS[q][1], LENGTHS[q][1] + 256), A("IB"), A("WB", 1 + 256 * q, 257 + 256 * q))
+            if not DQ:
+                mm(A("W3"), A("IB"), A("WB", 1537, 2049), True, False)
+            act(A("OCC"), NEW, AF.Sign)
+            for hf in range(2):
+                bank = "P%d" % (6 + hf)
+                mms(A(bank), [(A("IB"), A("WK", 512 * hf, 512 * hf + 512))]
+                    + [(A("IB"), HF("WV", hf), A(bank, r, 512, 4)) for r in range(4)], True, False)
+            mm(Z, A("IB"), A("WV"))
 
     for q, e in enumerate("sasa"):
         dma(e, H(T.ylab[:, 512 * q:512 * q + 512]), A("DK", 1 + 512 * q, 513 + 512 * q))

@@ -2,19 +2,26 @@ from concourse.mybir import AluOpType, ActivationFunctionType
 
 STEPS = 4
 XW = 2120
-ZFIRST = 2
-DQ = 4
-ZAT = (0, 0, 1, 0, 1, 1, 1)
-CUTS = ((0, 128), (128, 256))
+BY_V = 1152
+BY_DMA = 1152
+XVFIRST = 0
+RMS = 1
+TIS = 0
+NEORD = 1
+NBA = (1, 0)
+LO_V = (256, 384)
+NEG_S = 128
+SUMS0 = 0
+BY_V0 = 1536
+SPLIT = (1, 0, 0, 0)
 EXA = 128
-XVAT = 1
-ZPE = 0
-RCV1 = 0
-OWN0 = 256
-OWN = 256
-LOV = (128, 0)
 HALVES = ((1, 0, 128), (1, 128, 256))
-PARTS = ((0, 0, 256), (2, 0, 256), (3, 0, 128), (3, 128, 256))
+PARTS = ((0, 0, 256), (2, 0, 256), (3, 0, 192), (3, 192, 256))
+PUSH = ("hit0 w hit1 w", "givers", "w count", "empties ranks", "w", "w", "pick",
+        "w places w cut0 w cut1", "kept mask", "givers_cut")
+JOIN = ("scan lists", "occ", "offsets next", "same0", "same1", "same2 popped0 heights tile1", "tile0", "spare")
+TURN = (1024, 1408, 1536, 1920)
+LABELS = ((0, 256), (256, 384), (384, 512))
 MW = 72
 
 F, B, I, U, NM = "float32", "bfloat16", "int32", "uint16", "float16"
@@ -23,37 +30,37 @@ _S = {
     "STI": (256, I), "CNI": (256, I), "CNF": (256, B), "XK": (4096, F), "XV": (256, F), "DK": (4096, F),
     "CMP": (4096, B), "PI": (16, I), "COL": (48, F), "IS": (256, F),
     "M0": (144, B), "IW": (4 * 144, F), "TL": (4 * 144, B), "FO": (144, B), "SR": (1024, B),
-    "NI": (256, B), "IP": (512, B), "TT": (512, B), "BH": (512, B),
+    "NI": (128, B), "IP": (128, B), "TT": (128, B), "BH": (128, B),
     "CT": (256, B), "ONES": (256, B), "DA": (16, F), "HOLD": (256, F), "LST": (84, U),
-    "C4K": (512, B), "N4K": (256, B), "RST": (384, B), "SETS": (36, F), "JB": (4, F), "JT": (32, F), "E8T": (8, B), "FO32": (144, F),
+    "RZ": (640, B), "EY": (256, NM), "SETS": (36, F), "JB": (4, F), "JT": (32, F), "E8T": (8, B), "FO32": (144, F),
     "VF": (16, F), "VU": (16, U), "KA": (256, NM), "KT": (256, U), "WV": (256, B), "WF": (256, F), "WK": (1024, B),
-    "SC": (256, F), "SB": (1280, B), "SM": (64, F), "EX": (512, NM), "EY": (256, NM), "ZO": (16, U), "JO": (32, U),
-    "NE": (1280, B), "OVR": (256, B), "INS": (256, B), "INE": (256, B), "GA": (64, NM),
+    "SC": (256, F), "SB": (1280, B), "EX": (512, NM), "ZO": (16, U), "JO": (32, U),
+    "NE": (1280, B), "INS": (256, B), "INE": (256, B), "GA": (64, NM),
     "ZS": (256, F), "ZM": (256, F), "HIT": (256, B), "TI": (256, I), "TA": (256, I), "E0": (128, F), "E1": (128, F),
-    "KY": (256, NM), "SPR": (128, F), "STA": (264, F), "ST1": (256, NM), "TOP": (256, NM), "A1": (256, NM), "OLD": (256, NM),
+    "KY": (256, NM), "SPR": (128, F), "SPU": (128, F), "STA": (264, F), "ST1": (256, NM), "TOP": (256, NM), "A1": (256, NM), "OLD": (256, NM),
     "OCC": (256, B), "FS": (256, B), "FE": (256, B), "JK": (1024, B), "SA": (8, F), "SL": (4, U), "GU": (32, U),
     "RE": (16, U), "MSK": (32, B), "RM": (64, NM),
     "RW": (32, F), "RU": (32, U), "RCV": (256, NM), "OWN": (512, F), "YS": (256, F), "YC": (256, F),
 }
 POOL = {}
-for _n, _d, _l in (("CB", B, "IB BO NBO E8 DG DN DHF N4 T2 PERM SH ISH I7 I8 IN SPH SPL ZERO"),
+for _n, _d, _l in (("CB", B, "IB NIB BO NBO E8 DG DN DHF N4 N4X T2 PERM SH ISH I7 I8 ZERO"),
                    ("CF", F, "IG I32")):
     for _k, _c in enumerate(_l.split()):
         POOL[_c] = (_n, 128 * _k)
     _S[_n] = (128 * len(_l.split()), _d)
 for _t in range(STEPS):
-    _S["D%d" % _t] = (2064, F)
-    _S["MO%d" % _t] = (MW, F)
-    _S["MI%d" % _t] = (MW, F)
-    _S["LO%d" % _t] = (512, F)
-    _S["LI%d" % _t] = (512, F)
+    for _n, _w in (("D", 2064), ("MO", MW), ("MI", MW), ("CO", 4), ("CI", 4), ("LO", 512), ("LI", 512)):
+        _S["%s%d" % (_n, _t)] = (_w, F)
 SCRATCH = {k: ("sbuf", [128, w], d) for k, (w, d) in _S.items()}
 PSUM = ["W0", "W1", "W2", "W3", "P4", "P5", "P6", "P7"]
 for _k in PSUM:
     SCRATCH[_k] = ("psum", [128, 512], F)
-NDMA = 20
+BLOCK = {"W3": 16, "ZM": 32, "WF": 32, "SPU": 16}
+for _k, _w in BLOCK.items():
+    SCRATCH[_k] = (SCRATCH[_k][0], [128, SCRATCH[_k][1][1] // _w, _w], F)
+NDMA = 22
 SEMAPHORES = ["ev", "ea", "ep", "eg", "sent"] + ["d%d" % k for k in range(NDMA)] + \
-    ["nm%d" % t for t in range(STEPS)] + ["lb%d_%d" % (t, k) for t in range(STEPS) for k in range(2)]
+    ["%s%d" % (n, t) for n in ("ct", "nm", "la", "lb", "lc")[:2 + len(LABELS)] for t in range(STEPS)]
 
 OP = AluOpType
 AF = ActivationFunctionType
@@ -73,10 +80,20 @@ def rank_program(g, core, T, topo):
             hi = POOL[n][1] + (128 if hi is None else hi)
             lo = POOL[n][1] + lo
             n = POOL[n][0]
+        if n in BLOCK:
+            w = BLOCK[n]
+            hi = w * SCRATCH[n][1][1] if hi is None else hi
+            ap = T[n][:, lo // w, :] if hi - lo == w else T[n][:, lo // w:hi // w, lo % w:w:st]
+            return (ap, [(n, lo, hi, st)], [])
         if hi is None:
             hi = SCRATCH[n][1][1]
         ap = T[n][0:p, lo:hi:st] if st != 1 else T[n][0:p, lo:hi]
         return (ap, [(n, lo, hi, st)], [])
+
+    def HB(n, hf, lo=0):
+        w = BLOCK[n]
+        return (T[n][:, lo // w:(lo + 256) // w, hf * w // 2:(hf + 1) * w // 2],
+                [(n, c, c + w // 2, 1) for c in range(lo + hf * w // 2, lo + 256, w)], [])
 
     def HF(n, hf, base=0):
         return A(n, base + 128 * hf, base + 128 * hf + 128)
@@ -129,10 +146,10 @@ def rank_program(g, core, T, topo):
         if bias is not None:
             kw["bias"] = val(bias)
         if scale is not None:
-            kw["scale"] = scale
+            kw["scale"] = val(scale)
         if acc is not None:
             kw["accum_out"] = acc[0]
-        add("a", lambda: g.scalar.activation(o[0], a[0], f, **kw), [o] + ([acc] if acc else []), [a, bias])
+        add("a", lambda: g.scalar.activation(o[0], a[0], f, **kw), [o] + ([acc] if acc else []), [a, bias, scale])
 
     def mm(o, l, r, st=True, sp=True):
         add("p", lambda: g.tensor.matmul(o[0], l[0], r[0], st, sp), [o], [l, r])
@@ -147,8 +164,8 @@ def rank_program(g, core, T, topo):
         else:
             add("g", lambda: g.iota(o[0], pat, base, cm, allow_small_or_imprecise_dtypes=True), [o], [])
 
-    def select(o, a, pat, op, fill_, base):
-        add("g", lambda: g.affine_select(o[0], a[0], pat, op, fill_, base, 1), [o], [a])
+    def select(o, a, pat, op, fill_, base, cm=1):
+        add("g", lambda: g.affine_select(o[0], a[0], pat, op, fill_, base, cm), [o], [a])
 
     nd = [0]
 
@@ -192,13 +209,7 @@ def rank_program(g, core, T, topo):
 
     ncol = [9]
 
-    def col(src, m, a, op=OP.add):
-        c = C("COL", ncol[0])
-        ncol[0] += 1
-        ts(c, src, m, OP.mult, a, op)
-        return c
-
-    def cola(src, m, a):
+    def col(src, m, a):
         c = C("COL", ncol[0])
         ncol[0] += 1
         act(c, src, AF.Identity, bias=a, scale=m)
@@ -213,42 +224,41 @@ def rank_program(g, core, T, topo):
     def pick(src):
         scan(A("SC"), A("HOLD"), src, 0.0, OP.add, OP.min)
 
-    def lists_of_names(first=True):
-        if first:
-            pick(LO_("P6"))
+    def lists_of_names():
+        pick(LO_("P6"))
         for n_ in ("VU", "VF"):
             act(A(n_), A("SC", 15, 256, 16), AF.Identity, bias=cWin)
 
-    def neighbours(bank):
+    def neighbours():
         act(A("KA"), G("NBI", 2049, "VU", 0, 16), AF.Identity, bias=1.0)
-        for q in (1, 0, 2, 3):
+
+    def tiles(bank, which):
+        for q in which:
             mms(A(bank, 64 * q, 64 * q + 64),
                 [(A("TL", 144 * q + 12 - 4 * e, 144 * q + 140 - 4 * e), A("KA", e, 256, 4)) for e in range(4)])
 
     def names_by_lane():
-        mms(LO_("W3"), [(HF("KA", hf), A("IP", 256 * hf, 256 * hf + 256)) for hf in range(2)])
+        for hf in range(2):
+            mm(HB("W3", hf), HF("KA", hf), A("IP"))
+        mm(HI_("W3"), A("IB"), A("CT"), True, False)
 
     def lengths():
         act(A("WV"), G("WB", 2049, "VU", 0, 16))
-
-    def wide_lengths():
-        select(A("WF"), A("WV"), [[0, 256]], OP.is_ge, 0.0, 0)
-
-    def tile_lengths():
-        act(A("WK"), G("WB", 2049, "KT", 64, 128))
+        for hf in range(2):
+            select(HB("WF", hf), HF("WV", hf), [[0, 128]], OP.is_ge, 0.0, 0)
 
     def repeated_names():
         act(A("EY"), G("VF", 16, "LST", 0, 16))
 
     def unique():
-        return [lambda: tt(LO_("NE"), A("EY"), LO_("P6"), OP.not_equal),
-                lambda: tt(A("NE", 256, 496), A("EY", 0, 240), A("P6", 16, 256), OP.not_equal),
-                lambda: scan(A("SB", 0, 496), A("C4K", 0, 496), A("NE", 0, 496), 0.0, OP.add, OP.mult),
-                lambda: tt(A("SM", 0, 16), A("VF"), A("SB", 15, 256, 16), OP.subtract),
-                lambda: ts(A("SM", 48, 56), A("SB", 271, 496, 32), 65536.0, OP.is_lt, 8192.0, OP.mult),
-                lambda: ts(A("ZO", 1, 16, 2), A("SM", 1, 16, 2), cWin, OP.add, cDum[1], OP.min),
-                lambda: tt(A("SM", 48, 56), A("SM", 48, 56), A("SM", 0, 16, 2), OP.add),
-                lambda: ts(A("ZO", 0, 16, 2), A("SM", 48, 56), cWin, OP.add, cDum[0], OP.min)]
+        def count():
+            scan(A("SB", 0, 384), A("RZ", 0, 384), A("NE", 0, 384), 0.0, OP.mult, OP.subtract)
+            mms(A("P5", 352, 368), [(A("IB"), A("EY", 0, 256, 16)), (A("N4X"), A("SB", 15, 256, 16)),
+                                    (A("N4"), A("SB", 271, 384, 16), A("P5", 352, 360))])
+        return [lambda: tt(LO_("NE"), A("EY"), LO_("P6"), OP.is_equal),
+                lambda: tt(A("NE", 256, 384), HF("EY", 0), HF("P6", 1), OP.is_equal), count] + \
+            [(lambda hf: lambda: ts(A("ZO", hf, 16, 2), A("P5", 352 + 8 * hf, 360 + 8 * hf), cDum[hf], OP.min))(hf)
+             for hf in range(2)]
 
     iota(C("PI", 0), [[0, 1]], 0, 1, True)
     iota(A("IG"), [[16, 8], [0, 16]])
@@ -258,11 +268,9 @@ def rank_program(g, core, T, topo):
     ms(A("ZERO"), 0.0)
     for k, m in enumerate((15, 112, 1, 3, 12, 8, 2, 4)):
         ts(C("PI", 1 + k), C("PI", 0), m, OP.bitwise_and)
-    ms(A("C4K"), 4096.0)
+    ms(A("STA", 256, 264), 0.0)
     cp(A("COL", 0, 9), A("PI", 0, 9))
     cP, cA, cG, cOdd, cR, cQ, c8, c2, c4 = [C("COL", k) for k in range(9)]
-    ms(A("N4K"), -4096.0)
-    ms(A("STA", 256, 264), 0.0)
     ms(A("X", 0, 1), 0.0)
     act(A("CNF", p=8), A("CNI", p=8))
     act(A("TOP"), A("STI"), AF.Identity, bias=1.0)
@@ -270,47 +278,63 @@ def rank_program(g, core, T, topo):
     ts(A("HOLD"), A("IS"), cA, OP.is_le, 1052672.0, OP.mult)
     mm(LO_("P4"), A("E8", p=8), A("CNF", p=8))
     ts(A("BO"), A("IG"), cG, OP.is_equal)
-    cTl = cola(cR, 1.0, cG)
-    cWin = cola(cA, -4096.0, 61440.0)
-    cTl = cola(cQ, 36.0, cTl)
-    cKeep = cola(cA, -4096.0, -4096.0)
-    ts(A("HOLD"), A("HOLD"), -4096.0, OP.add)
+    cTl = col(cR, 1.0, cG)
+    cWin = col(cA, -4096.0, 61440.0)
+    cTl = col(cQ, 36.0, cTl)
+    cKeep = col(cA, -4096.0, -4096.0)
+    ts(A("DA"), A("IS", 0, 16), cA, OP.is_equal)
+    act(A("HOLD"), A("HOLD"), AF.Identity, bias=-4096.0)
     ts(LO_("P5"), LO_("P4"), -1.0, OP.add, cA, OP.is_equal)
     im, im144 = A("IW", 0, 128), A("IW", 0, 144)
     ts(A("IB"), im, cP, OP.is_equal)
-    ts(A("M0"), im144, -15.0, OP.add, cG, OP.is_equal)
     tt(A("A1"), A("TOP"), LO_("P5"), OP.mult)
     act(LO_("P4"), LO_("P4"), AF.Relu, bias=cKeep, scale=4096.0)
     mm(LO_("P6"), A("BO"), A("A1"))
-    ts(A("TL"), A("IW"), -12.0, OP.add, cTl, OP.is_equal)
-    cS = cola(c8, 0.125, 0.0)
+    ts(A("M0"), im144, -15.0, OP.add, cG, OP.is_equal)
+    ts(A("TL", 144, 288), A("IW", 144, 288), -12.0, OP.add, cTl, OP.is_equal)
+    cS = col(c8, 0.125, 0.0)
     act(A("LST", 0, 16), A("IS", 0, 16))
-    cS = cola(c4, 0.5, cS)
-    cFo = cola(cA, 0.5, cG)
-    cS = cola(c2, 2.0, cS)
-    cDg = cola(cA, 1.0, -15.0)
-    cS = cola(cOdd, 8.0, cS)
-    cJb = cola(cA, -2.0, -65.0)
-    cPerm = cola(cS, 1.0, cG)
+    cS = col(c4, 0.5, cS)
+    cFo = col(cA, 0.5, cG)
+    cS = col(c2, 2.0, cS)
+    cDg = col(cA, 1.0, -15.0)
+    cS = col(cOdd, 8.0, cS)
+    cNext = col(C("DA", 15), -1.0, 1.0)
+    cPerm = col(cS, 1.0, cG)
+    cNext = col(cA, 1.0, cNext)
+    cM1, cLast = col(cP, 1.0, -1.0), col(C("DA", 15), 4096.0, -4096.0)
+    cDum = [col(cA, 1.0, 2049.0 + 16 * k) for k in range(4)]
+    act(A("DG"), A("IB"), AF.Identity, scale=cDg)
+    act(A("N4X"), A("IB"), AF.Identity, scale=cLast)
     lists_of_names()
-    neighbours("P5")
+    for lo, hi in ((0, 144), (288, 576)):
+        ts(A("TL", lo, hi), A("IW", lo, hi), -12.0, OP.add, cTl, OP.is_equal)
+    neighbours()
+    tiles("P5", (1, 0, 2, 3))
     repeated_names()
-    cDum = [cola(cA, 1.0, 2049.0 + 16 * k) for k in range(4)]
     act(A("KT"), LO_("P5"))
+    late_cols = {}
+
+    def push_constants():
+        cJb, cCap = col(cA, -2.0, -65.0), col(cS, -4096.0, -4096.0)
+        late_cols["top"], late_cols["re"] = col(cS, -4096.0, 0.0), col(cWin, 1.0, 39.5)
+        act(A("JB"), A("IS", 0, 4), AF.Identity, bias=cJb, scale=-32.0)
+        late_cols["cap"] = col(C("DA", 15), -1048576.0, cCap)
 
     for t in range(STEPS):
         fill(A("D%d" % t, 0, 1), 1)
     diagonal("I32", 1.0)
-    diagonal("IN", -1.0)
+    diagonal("N4", -4096.0)
     for k in range(4):
-        iota(A("NI", 64 * k, 64 * k + 64), [[4, 2], [8, 2], [16, 16]], k // 2 + 2 * (k % 2))
+        iota(A("NI", 32 * k, 32 * k + 32), [[4, 2], [8, 2], [16, 8]], k // 2 + 2 * (k % 2))
     select(A("T2"), A("BO"), [[-1, 128]], OP.is_gt, 0.0, 0)
-
     iota(A("SETS", 0, 32), [[16, 2], [1, 4], [4, 4]])
     iota(A("SETS", 32, 36), [[32, 2], [4, 2]])
     for k in range(4):
         iota(A("CT", 64 * k, 64 * k + 64), [[-4, 2], [-8, 2], [0, 16]], 15 - k // 2 - 2 * (k % 2))
-    diagonal("N4", -4096.0)
+    select(A("RZ", 256, 384), A("ONES", 0, 128), [[0, 8], [1, 16]], OP.not_equal, 0.0, 0, 0)
+    for k in range(4):
+        iota((T.SPU[:, :, 4 * k:4 * k + 4], [("SPU", 0, 128, 1)], []), [[0, 8], [16, 2], [1, 2]], 4096 * (k // 2) + 256 * (k % 2))
 
     def late_lists():
         for t in range(STEPS):
@@ -319,60 +343,48 @@ def rank_program(g, core, T, topo):
         diagonal("DHF", -0.5)
         for r in range(0, 8, 2):
             select(A("SR", 128 * r, 128 * r + 256), A("ONES"), [[-2, 2], [-16, 8], [0, 16]], OP.is_equal, 0.0, -2 * r)
-        iota(A("RST"), [[0, 24], [-16, 16]])
+        select(A("RZ", 384, 640), A("ONES"), [[0, 16], [1, 16]], OP.not_equal, 0.0, 0, 0)
+        diagonal("NIB", -1.0)
+        select(A("I8"), A("IB"), [[0, 64], [1, 2]], OP.is_equal, 0.0, 0, 0)
+        select(A("I7"), A("I8"), [[0, 8], [1, 16]], OP.not_equal, 0.0, -14, 0)
 
     tt(A("ST1"), A("TOP"), LO_("P4"), OP.min)
     ts(A("PERM"), im, cPerm, OP.is_equal)
-    ts(A("DA"), A("IS", 0, 16), cA, OP.is_equal)
-    ts(C("TI", 0), cS, SPREAD, OP.mult)
-    ts(A("FO"), im144, -8.0, OP.add, cFo, OP.is_equal)
-    cEven, cRe, cCap = col(cOdd, -1.0, 1.0), col(cWin, 1.0, 39.5), col(cS, -4096.0, -4096.0)
-    for k, m in enumerate((BITS & ~0xFFFF, BITS & 0xFFFF)):
-        ts(C("TA", k), C("TI", 0), m, OP.bitwise_and)
-    mm(LO_("P7"), A("PERM"), A("ST1"))
+    ts(A("RZ", 0, 256), A("IS"), cNext, OP.not_equal)
+    ts(A("IP"), A("NI"), cP, OP.is_equal)
     un = unique()
-    cM1 = col(cP, 1.0, -1.0)
-    cCap, c7 = col(C("DA", 15), -1048576.0, cCap), col(C("DA", 14), -1.0, cEven)
-    ts(A("DG"), A("IB"), cDg, OP.mult)
-    cp(A("COL", 46, 48), A("TA", 0, 2))
-    ts(A("IP", 0, 256), A("NI"), cP, OP.is_equal)
-    ts(A("IP", 256, 512), A("NI"), -128.0, OP.add, cP, OP.is_equal)
-    ts(A("SPH"), A("IB"), C("COL", 46), OP.mult)
-    ts(A("SPL"), A("IB"), C("COL", 47), OP.mult)
-    weave(un[:2])
-    for lo, hi in ((1025, 2049), (1, 1025)):
+    if NEG_S:
+        act(A("X", 1, 1 + NEG_S), A("LABI", 1, 1 + NEG_S), scale=-1.0)
+    for lo, hi in ((1025, 2049), (1 + NEG_S, 1025)):
         ts(A("X", lo, hi), A("LABI", lo, hi), -1.0, OP.mult)
-    un[2]()
+    weave(un[:2])
 
     def meeting_constants():
-        cSet, cJt = cola(cQ, 4.0, 8.0), cola(c8, 1024.0, 532480.0)
-        cSet = cola(c8, -3.75, cSet)
-        act(A("JT"), A("SETS", 0, 32), AF.Identity, bias=cJt, scale=16384.0)
-        cSet = cola(cR, 4.0, cSet)
+        cSet, cJt = col(cQ, 4.0, 8.0), col(c8, 0.125, 65.0)
+        cSet = col(c8, -3.75, cSet)
+        act(A("JT"), A("SETS", 0, 32), AF.Identity, bias=cJt, scale=2.0)
+        cSet = col(cR, 4.0, cSet)
         act(A("LST", 48, 80), A("SETS", 0, 32))
-        cSet = cola(cOdd, -3.0, cSet)
+        cSet = col(cOdd, -3.0, cSet)
         act(A("LST", 80, 84), A("SETS", 32, 36), AF.Identity, bias=cSet)
 
     def flight_constants():
+        cp(A("FO32"), A("FO"))
         ts(A("SH"), im, cM1, OP.is_equal, cOdd, OP.mult)
         ts(A("NBO"), A("BO"), -1.0, OP.mult)
-        ts(A("I8"), A("IB"), cEven, OP.mult)
-        ts(A("I7"), A("IB"), c7, OP.mult)
         ts(A("E8T"), A("IS", 0, 8), 16.0, OP.mult, cG, OP.is_equal)
         tt(A("ISH"), A("IB"), A("SH"), OP.subtract)
 
     def fold(o, by, src, lo):
         mms(o, [(A(by, 8 - 8 * e, 136 - 8 * e), A(src, lo + e, lo + 64, 2)) for e in range(2)])
 
-    P, Z = LO_("P5"), HI_("P4")
+    P, Z, WP = LO_("P5"), HI_("P4"), LO_("P4")
     NEW, R = LO_("W2"), HI_("W2")
     HITS = ("P5", "P6")
-    LENGTHS = {4: ("P4", 0), 5: ("P5", 256)}
-    BY_DMA = 2048 - 256 * DQ
     for t in range(STEPS):
         last = t == STEPS - 1
         peer = T.cores[rank ^ (1 << (t % 2))]
-        D, MO, MI, LO, LI = ["%s%d" % (n_, t) for n_ in ("D", "MO", "MI", "LO", "LI")]
+        D, MO, MI, CO, CI, LO, LI = ["%s%d" % (n_, t) for n_ in ("D", "MO", "MI", "CO", "CI", "LO", "LI")]
 
         def gathered(o, win, on, c, d):
             if win == "X" and t == 0:
@@ -386,112 +398,141 @@ def rank_program(g, core, T, topo):
         def nbr(n, q, r, lo=0, hi=256):
             return A(n, 1024 * q + 4 * lo + r, 1024 * q + 4 * hi, 4)
 
-        def own(q, q2, lo, hi):
-            tt(A("XK", 1024 * q + 4 * lo, 1024 * q + 4 * hi), G("X", 2049, "KT", 64 * q + lo // 4, 64 * q + hi // 4),
-               A("XK", 1024 * q2 + 4 * lo, 1024 * q2 + 4 * hi), OP.max)
+        def own(q, q2, hf):
+            lo = 512 * hf
+            tt(A("XK", 1024 * q + lo, 1024 * q + lo + 512), G("X", 2049, "KT", 64 * q + 32 * hf, 64 * q + 32 * hf + 32),
+               A("XK", 1024 * q2 + lo, 1024 * q2 + lo + 512), OP.max)
 
-        def add_lengths(q):
-            bank, at = LENGTHS[q] if t and q >= 4 else ("W%d" % (q // 2), 256 * (q % 2))
-            w = 255 if t and q == 7 - DQ else 256
-            return lambda: tt(A(D, 1 + 256 * q, 1 + 256 * q + w), A("X", 1 + 256 * q, 1 + 256 * q + w), A(bank, at, at + w), OP.add)
+        def add_lengths(lo, hi, bank, at):
+            tt(A(D, lo, hi), A("X", lo, hi), A(bank, at, at + hi - lo), OP.add)
+
+        def sums(qs):
+            for q in qs:
+                add_lengths(1 + 256 * q, 257 + 256 * q, "W%d" % (q // 2), 256 * (q % 2))
+
+        def link(c, q, r, hf=None, out=None):
+            c = c if hf is None else HF("P4", hf, 256) if c is Z else HF("P5", hf)
+            lo, hi = (0, 256) if hf is None else (128 * hf, 128 * hf + 128)
+            tt(out or c, nbr("XK", q, r, lo, hi), c, OP.max)
 
         def heights():
-            mms(HI_("W3"), [(HF("OCC", hf), A("BH", 256 * hf, 256 * hf + 256)) for hf in range(2)], False, False)
-            mm(R, A("BO"), A("OCC"), True, False)
-        n = OWN if t else OWN0
-        cuts = CUTS if t else ((0, 128), (128, 256))
-        if t:
-            if DQ:
-                dma("g", A(D, BY_DMA, 2049), A("X", BY_DMA, 2049), True)
-                names_by_lane()
-                mm(HI_("W3"), A("IB"), A("CT"), True, False)
-                heights()
-            else:
-                mm(A("W3"), A("I32"), A("X", 1537, 2049), False, True)
-            for lo, hi in cuts:
-                gather("XK", "X", 1, lo, hi)
-                if lo < 128 <= hi:
-                    mm(A("P6"), A("I32"), A("XK", 1024, 1536), False, True)
-        else:
             for hf in range(2):
-                gather("XK", "X", 1, 128 * hf, 128 * hf + 128)
-            lengths()
-            for q in range(4):
-                if q == 2:
-                    mm(Z, A("IB"), A("WV"))
-                mm(A("W%d" % q), A("IB"), A("WB", 1 + 512 * q, 513 + 512 * q), True, q < 3)
-            mm(A("W3"), A("I32"), A("X", 1537, 2049), False, True)
-        wide_lengths()
-        for hf in range(2):
-            gather("XK", "X", 2, 128 * hf, 128 * hf + 128)
-            if hf == XVAT:
-                gathered(A("XV"), "X", "VU", 0, 16)
-        dd = [add_lengths(q) for q in range(8 - DQ if t and DQ else 6)]
-        weave(dd[:4] if t else [])
-        for lo, hi in cuts:
-            own(0, 1, lo, hi)
-        weave(dd[4:] if t else [])
+                mm(HB("W3", hf, 256), HF("OCC", hf), A("BH"), False, False)
+            mm(R, A("BO"), A("OCC"), True, False)
+
+        def new_labels():
+            for hf in range(2):
+                tt(HF("P4", hf, 256), HB("ZM", hf), HF("P4", hf), OP.subtract)
+
+        def met(hf):
+            if t:
+                mm(HF("W1", hf), A("I32"), HB("ZM", hf), False, hf == 1)
+
+        def meet(hf):
+            tt(HB("ZM", hf), HF("ZS", hf), HF("P5", hf), OP.max)
+            met(hf)
+        split = SPLIT[t]
         if t:
+            dma("g", A(D, BY_DMA, 2049), A("X", BY_DMA, 2049), True)
+            add_lengths(1025, BY_V, "P4", 0)
+            if BY_V < BY_DMA:
+                mms(A("P5", 256, 256 + BY_DMA - BY_V), [(A("IB"), A("WB", BY_V, BY_DMA)), (A("I32"), A("X", BY_V, BY_DMA))])
+            sums((3, 2, 1) if split else (3, 2, 1, 0))
+        for hf in range(2):
+            gather("XK", "X", 1, 128 * hf, 128 * hf + 128)
+            if t and hf == 0 and not XVFIRST:
+                mm(A("P6"), A("I32"), A("XK", 1024, 1536), False, True)
+        if t == 0:
+            for q in range(4):
+                mm(A("W%d" % q), A("IB"), A("WB", 1 + 512 * q, 513 + 512 * q), True, q < 3 or BY_V0 == 2048)
+            if BY_V0 < 2048:
+                mm(A("W3"), A("I32"), A("X", 1537, 2049), False, True)
+            lengths()
+            mm(WP, A("IB"), A("WV"))
+            mm(Z, A("IB"), A("WV"), True, False)
+        gathered(A("XV"), "X", "VU", 0, 16)
+        mm(Z, A("I32"), A("XV"), False, True)
+        if t:
+            if XVFIRST:
+                mm(A("P6"), A("I32"), A("XK", 1024, 1536), False, True)
             mm(A("P7"), A("I32"), A("XK", 1536, 2048), False, True)
-        act(P, nbr("XK", 0, 0))
-        if n < 256:
-            gather("XK", "X", 3, n, 256)
-        if t and not DQ:
-            act(A(D, 1537, 2049), A("W3"))
+            mm(LO_("W1"), A("NIB"), A("WV"), True, False)
+            if BY_V < BY_DMA:
+                act(A(D, BY_V, BY_DMA), A("P5", 256, 256 + BY_DMA - BY_V))
+        gather("XK", "X", 2, 0, 128 if split else 256)
+        act(HF("P5", 0) if split else P, nbr("XK", 2, 0, 0, 128 if split else 256))
+        if t and split:
+            own(0, 1, 0)
+            sums((0,))
+            own(3, 0, 0)
+            own(0, 1, 1)
+            link(Z, 3, 0, 0)
+            link(P, 3, 1, 0)
+            own(3, 0, 1)
+        else:
+            sums(range(0 if t else SUMS0))
+            own(0, 1, 0)
+            if t == 0:
+                un[2]()
+            own(0, 1, 1)
+            if t == 0:
+                if BY_V0 < 2048:
+                    act(A(D, 1537, 2049), A("W3"))
+                late_lists()
+                for u in range(1, STEPS):
+                    dma("g", A("D%d" % u, BY_DMA, 2049), A("WB", BY_DMA, 2049))
+                sums(range(SUMS0, BY_V0 // 256))
+            own(3, 0, 0)
+            own(3, 0, 1)
+            if split:
+                link(Z, 3, 0, 0)
+                link(P, 3, 1, 0)
+        if t == 0:
+            mms(HF("P6", 0), [(A("T2"), A("IP")), (A("DG"), A("IP"))])
+            mm(A("P6", 256, 384), A("BO"), A("IP"))
+            mm(NEW, A("PERM"), A("ST1"))
             names_by_lane()
-            mm(HI_("W3"), A("IB"), A("CT"), True, False)
-            heights()
+        late = list(un[3:]) if t == 0 or split or "spare" not in JOIN[7] else []
         if t == 0:
-            act(A(D, 1537, 2049), A("W3"))
-            late_lists()
-            for u in range(1, STEPS if DQ else 0):
-                dma("g", A("D%d" % u, BY_DMA, 2049), A("WB", BY_DMA, 2049))
-            weave(dd, un[3:])
-            act(A("OCC"), LO_("P7"), AF.Sign)
-            act(A("OLD"), LO_("P7"))
-            cS1 = cola(cS, 1.0, 1.0)
-            act(A("JB"), A("IS", 0, 4), AF.Identity, bias=cJb, scale=-32.0)
-        own(3, 2, 0, min(n, 128))
-        if n > 128:
-            own(3, 2, 128, n)
-        tt(Z, A("XV"), Z, OP.add)
-        if t == 0:
-            mms(A("P6"), [(A("T2"), A("IP")), (A("DG"), A("IP"))])
-            mm(A("P7"), A("BO"), A("IP"))
-            mms(A("W2", 0, 128), [(A("ONES", 0, 128), A("SPH")), (A("ONES", 0, 128), A("SPL"))])
-            names_by_lane()
-            mm(HI_("W3"), A("IB"), A("CT"), True, False)
-        order = [(0, 1), (0, 2), (0, 3), (3, 0), (3, 1), (3, 2)]
-        if n < 256:
-            order[2:2] = [(2, 0), (2, 1)]
-            order[6:6] = [(2, 2), (2, 3)]
-        for k, (q, r) in enumerate(order):
-            lo = n if q == 2 else 0
-            c = A("P4", 256 + lo, 512) if k % 2 else A("P5", lo, 256)
-            tt(A("ZS") if (q, r) == (3, 2) else c, nbr("XK", q, r, lo), c, OP.max)
-        for hf in range(2):
-            tt(HF("P5", hf), nbr("XK", 3, 3, 128 * hf, 128 * hf + 128), HF("P5", hf), OP.max)
-        weave(un[7:] if t else [])
-        for hf in range(2):
-            tt(HF("ZM", hf), HF("ZS", hf), HF("P5", hf), OP.max)
-        if t == 0:
-            cp(A("TT"), A("P6"))
-            tt(Z, A("ZM"), A("WV"), OP.subtract)
+            late += [lambda: cp(A("TT"), HF("P6", 0)), lambda: cp(A("BH"), A("P6", 256, 384)),
+                     lambda: ts(A("FO"), im144, -8.0, OP.add, cFo, OP.is_equal)]
+        if split:
+            if t:
+                link(Z, 3, 2, 0)
+                link(P, 3, 3, 0)
+            own(2, 3, 1)
+            if t == 0:
+                link(Z, 3, 2, 0)
+                link(P, 3, 3, 0)
+            weave([lambda: link(Z, 2, 1, 0), lambda: link(P, 2, 2, 0), lambda: link(Z, 2, 0, 1),
+                   lambda: link(Z, 2, 3, 0, HF("ZS", 0)), late[0], lambda: link(Z, 2, 1, 1), late[1], lambda: meet(0),
+                   lambda: link(Z, 2, 2, 1)] + late[2:])
+        else:
+            link(Z, 3, 0, 0)
+            link(Z, 3, 0, 1)
+            for k, (q, r) in enumerate(((3, 1), (3, 2), (3, 3), (2, 1), (2, 2))):
+                link(Z if k % 2 else P, q, r)
+            for hf in range(2):
+                link(Z, 2, 3, hf, HF("ZS", hf))
+            weave(late[:1])
+            meet(0)
+            meet(1)
+            weave(late[1:])
         for part_ in (PARTS if t else HALVES + PARTS):
             gather("DK", D, *part_)
-            if t == 0 and part_ == PARTS[0]:
-                act(A("BH"), A("P7"))
-                act(A("SPR"), A("W2", 0, 128))
-        if t:
+        if t == 0:
+            act(A("OCC"), NEW, AF.Sign)
+            push_constants()
+        else:
             act(A("OLD"), NEW)
 
         def compare(q, r, lo, hi):
             i = 4 * q + r
             c = A("CMP", 256 * i + lo, 256 * i + hi)
             if q == 1 and t:
-                tt(c, A("P%d" % (6 + lo // 128), r, 512, 4), A("ZM", lo, hi), OP.is_lt)
+                tt(c, A("P%d" % (6 + lo // 128), r, 512, 4), HB("ZM", lo // 128), OP.is_lt)
             else:
-                tt(c, nbr("DK", q, r, lo, hi), A("P4", 256 + lo, 256 + hi), OP.is_lt)
+                tt(c, nbr("DK", q, r, lo, hi), A("W1", lo, hi) if t else A("P4", 256 + lo, 256 + hi), OP.is_lt)
             for hf in range(2 if i < 15 else 0):
                 a, b = max(lo, 128 * hf), min(hi, 128 * hf + 128)
                 if a < b:
@@ -499,53 +540,83 @@ def rank_program(g, core, T, topo):
                        i == 4 and a == 128 * hf, i == 14 and b == 128 * hf + 128)
         zs = [(lambda b: lambda: tt(G("X", XW, "ZO", 2 * b, 2 * b + 2), A("ZM", 32 * b, 32 * b + 32),
                                     A("WF", 32 * b, 32 * b + 32), OP.subtract))(b) for b in range(8)]
-
-        def write(n):
-            for _ in range(n):
-                zs.pop(0)()
         if t == 0:
-            write(1)
+            if split:
+                link(Z, 2, 3, 1, HB("ZM", 1))
+                zs.pop(0)()
+            new_labels()
+            if not split:
+                zs.pop(0)()
         for q, lo, hi in HALVES + PARTS:
-            if (q, lo, hi) == HALVES[1] and t:
-                tt(Z, A("ZM"), A("WV"), OP.subtract)
-            if (q, lo, hi) == PARTS[-2] and t == 0:
+            if (q, lo, hi) == PARTS[-1] and t == 0:
                 heights()
             for r in range(4 if q < 3 else 3):
+                if (q, r, lo) == (1, 2, 0) and t and split:
+                    link(Z, 2, 3, 1, HB("ZM", 1))
+                    met(1)
                 compare(q, r, lo, hi)
         compare(3, 3, 0, 256)
-        for hf in range(2):
+
+        def hits(hf):
             act(HF("HIT", hf), HF(HITS[hf], hf), AF.Sign)
-            mm(HI_("W3"), HF("HIT", hf), A("TT", 256 * hf, 256 * hf + 256), False, hf == 1)
-            if hf == 0:
-                mm(LO_("P7"), A("BO"), A("CMP", 3840, 4096))
+            mm(HB("W3", hf, 256), HF("HIT", hf), A("TT"), False, hf == 1)
+
+        def givers():
+            scan(A("INS"), A("FS"), A("ONES"), -192.0, OP.add, OP.add)
+            for c in range(4):
+                act(A("JK", 256 * c, 256 * c + 256), A("INS"), AF.Sign, bias=C("JB", c), scale=-1.0, acc=C("SA", c))
+            act(NEW, R, AF.Relu, bias=late_cols["top"], scale=4096.0)
+            if not last:
+                act(R, R, AF.Relu, bias=late_cols["cap"], scale=4096.0)
+            act(A("SL"), A("SA", 0, 4), AF.Identity, bias=128.0, scale=0.5)
+            if t == 0:
+                meeting_constants()
+
+        def count():
+            ts(C(CO, 0), C("SA", 4), -128.0, OP.min, -0.5, OP.mult)
+            send(CO, CI, "ct%d" % t, peer, 0, 1)
+
+        def ranks():
+            mms(HI_("P7"), [(A("DN"), A("FE")), (A("DHF"), A("INE"))])
+            mms(LO_("P7"), [(A("DN"), A("FS")), (A("DHF"), A("INS"))])
+        small = {
+            "w": lambda: zs.pop(0)() if zs else None, "hit0": lambda: hits(0), "hit1": lambda: hits(1),
+            "givers": givers, "count": count, "ranks": ranks, "pick": lambda: pick(HI_("P7")),
+            "empties": lambda: scan(A("INE"), A("FE"), A("ONES"), 0.0, OP.add, OP.add),
+            "places": lambda: ts(A("RE"), A("SC", 15, 256, 16), late_cols["re"], OP.add, 7.0, OP.max),
+            "cut0": lambda: tt(A("ST1" if last else "TOP"), LO_("STA"), NEW, OP.min),
+            "cut1": lambda: None if last else tt(A("ST1"), LO_("STA"), R, OP.min),
+            "kept": lambda: ts(LO_("P7"), LO_("P7"), C(CI, 0), OP.is_lt, 4096.0, OP.mult),
+            "givers_cut": lambda: tt(A("A1"), A("ST1"), LO_("P7"), OP.min),
+            "mask": lambda: ts(A("MSK"), A("JT"), C(CO, 0), OP.is_le, 4096.0, OP.mult)}
+
+        def spare(k):
+            for n_ in PUSH[k].split():
+                small[n_]()
+        mm(LO_("P7"), A("BO"), A("CMP", 3840, 4096))
+        spare(0)
         mm(R, A("BO"), A("HIT"), False, False)
         act(A("FS"), LO_("P7"), AF.Sign)
+        for k in range(TIS):
+            act(HF("TI", k), HF("W3", k, 256), scale=SPREAD)
         mm(R, A("IB"), A("FS"), False, True)
         act(A("FS"), R, AF.Sign, bias=-8.5)
-        act(A("OVR"), R, AF.Relu, bias=cS1, scale=-1.0)
-        mms(LO_("P5"), [(A("N4"), A("OCC")), (A("N4"), A("OVR"))], True, False)
-        write(ZFIRST if t else ZFIRST - 1)
-        for k in range(2):
+        act(A("FE"), R, AF.Sign, bias=0.5, scale=-1.0, acc=C("SA", 4))
+        if t == 0:
+            act(A("OLD"), NEW)
+            act(A("SPR"), A("SPU"), scale=float(BITS & -BITS))
+        for hf in range(2):
+            mm(HF(HITS[hf], hf), A("N4"), HF("OCC", hf), True, False)
+        if t and not last:
+            mm(LO_("W1"), A("IB"), A("WB", 513, 769))
+        for k in range(TIS, 2):
             ts(HF("TI", k), HF("W3", k, 256), SPREAD, OP.mult)
-        write(1)
         for k in range(2):
             ts(HF("TA", k), HF("TI", k), BITS, OP.bitwise_and)
-        write(ZAT[0])
         tt(A("E0"), HF("TA", 0), HF("W3", 0), OP.add)
         tt(HF("W3", 1), HF("TA", 1), HF("W3", 1), OP.add)
-        scan(A("INS"), A("FS"), A("ONES"), -192.0, OP.add, OP.add)
-        act(A("FE"), R, AF.Sign, bias=0.5, scale=-1.0, acc=C("SA", 4))
-        for c in range(4):
-            act(A("JK", 256 * c, 256 * c + 256), A("INS"), AF.Sign, bias=C("JB", c), scale=-1.0, acc=C("SA", c))
-        act(A("SL"), A("SA", 0, 4), AF.Identity, bias=128.0, scale=0.5)
-        spare = [lambda: None, lambda: ts(C(MO, 0), C("SA", 4), -128.0, OP.min, -4096.0, OP.mult),
-                 lambda: scan(A("INE"), A("FE"), A("ONES"), 0.0, OP.add, OP.add),
-                 lambda: ts(A("MSK"), A("JT"), C(MO, 0), OP.is_le, 4096.0, OP.mult)]
-        if t == 0:
-            spare.insert(3, lambda: cp(A("FO32"), A("FO")))
         for s in range(4):
-            write(ZAT[1 + s])
-            spare[s]()
+            spare(1 + s)
             e, o = "E%d" % (s % 2), 128 + 128 * (s % 2)
             e2, o2 = "E%d" % (1 - s % 2), 256 - 128 * (s % 2)
             for k in range(2):
@@ -555,158 +626,149 @@ def rank_program(g, core, T, topo):
                     else:
                         out = A(e2, b, 128, 2) if k == 0 else A("W3", o2 + b, o2 + 128, 2)
                     tt(out, A(e, 64 * k, 64 * k + 64), A("W3", o + 64 * k, o + 64 * k + 64), op)
-            if s == 2:
-                mms(LO_("P7"), [(A("DN"), A("FS")), (A("DHF"), A("INS"))])
-                mms(HI_("P7"), [(A("DN"), A("FE")), (A("DHF"), A("INE"))])
-        if not last:
-            act(R, R, AF.Relu, bias=cCap, scale=4096.0)
-        if t == 0:
-            meeting_constants()
-        write(ZAT[5])
+        spare(5)
         for k in range(2):
             tt(HF("KY", k), HF("W3", k), A("SPR"), OP.subtract)
-            mm(HF("P5", k), HF("KY", k), A("IB"), False, k == 1)
-        pick(HI_("P7"))
-        tt(LO_("STA"), LO_("P5"), A("OLD"), OP.max)
-        write(ZAT[6])
-        ts(A("RE"), A("SC", 15, 256, 16), cRe, OP.add, 7.0, OP.max)
+            mm(HF(HITS[k], k), HF("KY", k), A("IB"), False, True)
+        spare(6)
+        for k in range(2):
+            tt(HF("STA", k), HF(HITS[k], k), HF("OLD", k), OP.max)
         act(A(MO, 8, MW), G("STA", 264, "SL", 0, 4))
         send(MO, MI, "nm%d" % t, peer, 0, MW)
         act(A("GA"), G("STA", 264, "SL", 0, 4))
         fold(A("P6", 256, 288), "FO", "GA", 0)
-        if not last:
-            tt(A("ST1"), LO_("STA"), R, OP.min)
-        write(len(zs))
+        spare(7)
         act(A("GU"), A("P6", 256, 288))
-        for k in range(2):
-            w = LOV[k]
-            if w:
-                cp(A(LO, 256 * k, 256 * k + w), G("X", 2049, "GU", 16 * k, 16 * k + w // 16))
-            if w < 256:
-                act(A(LO, 256 * k + w, 256 * k + 256), G("X", 2049, "GU", 16 * k + w // 16, 16 * k + 16))
-            send(LO, LI, "lb%d_%d" % (t, k), peer, 256 * k, 256 * k + 256)
-        if last:
-            act(A("ST1"), LO_("STA"))
-            ts(A("DK", 1, 1025), A("X", 1, 1025), -1.0, OP.mult)
-        else:
-            act(A("TOP"), LO_("STA"))
-            if RCV1:
-                mms(LO_("P6"), [(A("NBO"), A("ST1")), (A("BO"), A("TOP"))], True, False)
+        act(A(LO, 0, LO_V[0]), G("X", 2049, "GU", 0, LO_V[0] // 16))
+        send(LO, LI, "la%d" % t, peer, *LABELS[0])
+        for lo, hi in ((LO_V[0], LO_V[1]),) if LO_V[1] < 512 else LABELS[1:]:
+            act(A(LO, lo, hi), G("X", 2049, "GU", lo // 16, hi // 16))
         if t == 0:
-            spare[4]()
             flight_constants()
+        spare(8)
+        if LO_V[1] < 512:
+            cp(A(LO, LO_V[1], 512), G("X", 2049, "GU", LO_V[1] // 16, 32))
+        for k, (lo, hi) in enumerate(LABELS[1:]):
+            send(LO, LI, "l%s%d" % ("bc"[k], t), peer, lo, hi)
+
+        def turn(lo, hi):
+            if last:
+                ts(A("DK", 1 + lo, 1 + hi), A("X", 1 + lo, 1 + hi), -1.0, OP.mult)
+        turn(0, TURN[0])
 
         sets = ((256, 192), (448, 128), (576, 64))
 
         def equal_names(h):
             e, o = 256 * h, 640 * h
-            return [lambda: tt(A("NE", o, o + 256), A("EX", e, e + 256), A("P4", e, e + 256), OP.not_equal)] + \
+            return [lambda: tt(A("NE", o, o + 256), A("EX", e, e + 256), A("P4", e, e + 256), OP.is_equal)] + \
                 [(lambda s, w: lambda: tt(A("NE", o + s, o + s + w), A("EX", e, e + w), A("P4", e + 256 - w, e + 256),
                                           OP.is_equal))(s, w) for s, w in sets]
 
         def counts(h):
             o, sm = 640 * h, 64 + 16 * h
-
-            def later_sets():
-                scan(A("SB", o + 256, o + 640), A("RST"), A("NE", o + 256, o + 640), 0.0, OP.max, OP.subtract)
-                mms(A("P5", sm, sm + 16),
-                    [(A("IB"), A("EX", 256 * h, 256 * h + 256, 16)), (A("IB"), A("MSK", 16 * h, 16 * h + 16)),
-                     (A("IB"), A("SB", o + 15, o + 256, 16))]
-                    + [(A("N4"), A("SB", o + s + 15, o + s + w, 16), A("P5", sm, sm + w // 16)) for s, w in sets])
-            return [lambda: scan(A("SB", o, o + 256), A("N4K"), A("NE", o, o + 256), 0.0, OP.add, OP.mult), later_sets]
+            scan(A("SB", o, o + 256), LO_("RZ"), A("NE", o, o + 256), 0.0, OP.mult, OP.subtract)
+            scan(A("SB", o + 256, o + 640), A("RZ", 256, 640), A("NE", o + 256, o + 640), 0.0, OP.mult, OP.subtract)
+            mms(A("P5", sm, sm + 16),
+                [(A("IB"), A("EX", 256 * h, 256 * h + 256, 16)), (A("IB"), A("MSK", 16 * h, 16 * h + 16)),
+                 (A("N4X"), A("SB", o + 15, o + 256, 16))]
+                + [(A("N4"), A("SB", o + s + 15, o + s + w, 16), A("P5", sm, sm + w // 16)) for s, w in sets])
 
         def offsets(h):
             for k in range(4):
-                ts(A("JO", 16 * h + k, 16 * h + 16, 4), A("P5", 64 + 16 * h + 4 * k, 68 + 16 * h + 4 * k),
-                   cWin, OP.add, cDum[k], OP.min)
+                ts(A("JO", 16 * h + k, 16 * h + 16, 4), A("P5", 64 + 16 * h + 4 * k, 68 + 16 * h + 4 * k), cDum[k], OP.min)
+        (act if RMS else cp)(A("RM"), G(MI, MW, "LST", 80, 84))
         fold(A("P5", 0, 32), "FO32", MI, 8)
-        cp(A("RM"), G(MI, MW, "LST", 80, 84))
-        early = RCV1 and not last
-        if early:
-            act(A("RCV"), G(MI, MW, "RE", 0, 16))
+        spare(9)
+        turn(TURN[0], TURN[1])
         act(A("RW"), A("P5", 0, 32))
-        act(A("RU"), A("P5", 0, 32))
         for r in range(8):
-            if early and r == RCV1:
-                mm(LO_("P6"), A("SR", 896, 1024), A("RCV"), False, True)
             mm(A("P4", r, 512, 8), A("SR", 128 * r, 128 * r + 128), A("RM"))
+        if not last:
+            mms(LO_("P6"), [(A("BO"), A("TOP")), (A("NBO"), A("ST1"))], True, False)
         act(A("EX", 0, EXA), G("RW", 16, "LST", 48, 48 + EXA // 16))
-        if EXA < 256:
-            cp(A("EX", EXA, 256), G("RW", 16, "LST", 48 + EXA // 16, 64))
-        if early:
-            pick(LO_("P6"))
-        else:
-            act(A("RCV"), G(MI, MW, "RE", 0, 16))
-            if not last:
-                mms(LO_("P6"), [(A("NBO"), A("ST1")), (A("BO"), A("TOP")), (A("SR", 896, 1024), A("RCV"))])
+        cp(A("EX", EXA, 256), G("RW", 16, "LST", 48 + EXA // 16, 64))
+        turn(TURN[1], TURN[2])
+        act(A("RCV"), G(MI, MW, "RE", 0, 16))
+        act(A("RU"), A("RW"))
+        if not last:
+            mm(LO_("P6"), A("SR", 896, 1024), A("RCV"), False, True)
         act(HI_("EX"), G("RW", 32, "LST", 64, 80))
         act(A("OWN"), G("X", 2049, "RU", 0, 32))
-        one, two = equal_names(0) + counts(0), equal_names(1) + counts(1)
+        one, two = equal_names(0), equal_names(1)
         if last:
-            act(A("DK", 1025, 1793), A("X", 1025, 1793), scale=-1.0)
+            act(A("DK", 1 + TURN[2], 1 + TURN[3]), A("X", 1 + TURN[2], 1 + TURN[3]), scale=-1.0)
         weave([one[k] for k in (2, 3, 0, 1)])
+        if NEORD:
+            counts(0)
         if last:
-            ts(A("DK", 1793, 2049), A("X", 1793, 2049), -1.0, OP.mult)
-        elif early:
-            lists_of_names(False)
-            two.pop(0)()
-            two.insert(0, lambda: None)
+            turn(TURN[3], 2048)
         else:
             lists_of_names()
-        weave(one[4:])
+        if not NEORD:
+            counts(0)
+        if NEORD < 2:
+            two[2]()
+        mms(NEW, [(A("SH"), A("ST1")), (A("ISH"), A("A1")), (A("I8" if last else "I7"), A("RCV"))])
         if not last:
-            neighbours("W3")
-        act(LO_("P7"), LO_("P7"), AF.Relu, bias=C(MI, 0), scale=-8192.0)
-        if not last:
+            neighbours()
+            tiles("W3", NBA)
             repeated_names()
-            act(A("KT"), LO_("W3"))
             lengths()
-            tile_lengths()
-        weave(two[:2])
+        two[0]()
         offsets(0)
-        weave(two[2:4])
+        weave([two[1], two[3]] if NEORD < 2 else two[1:])
 
-        def stacks():
-            tt(A("A1"), A("ST1"), LO_("P7"), OP.min)
-            mms(NEW, [(A("SH"), A("ST1")), (A("I8" if last else "I7"), A("RCV")), (A("ISH"), A("A1"))])
-
-        def stacks_out():
-            act(A("OLD"), NEW)
-            act(A("OCC"), NEW, AF.Sign)
-            mm(LO_("P7"), A("PERM"), A("OLD"))
-            act(A("YS"), LO_("P7"), AF.Relu, bias=-1.0)
-            dma("s", H(T.ystk[:, :]), A("YS"))
-            mm(A("P6", 0, 256, p=8), A("E8T"), A("OCC"))
-            act(A("YC", p=8), A("P6", 0, 256, p=8))
-            dma("s", H(T.ycnt[:, :]), A("YC", p=8))
         def part(n, c, w=1):
             return A(n, 64 * c, 64 * (c + w))
+
+        def occupied():
+            ts(A("OCC"), NEW, 0.0, OP.is_gt)
         if last:
             best = [(lambda c: lambda: tt(part("OWN", c, 2), part("OWN", c, 2), part(LI, c, 2), OP.max))(c) for c in range(0, 8, 2)]
             join = [(lambda c: lambda: ts(G("DK", XW, "JO", 4 * c, 4 * c + 4), part("OWN", c), -1.0, OP.mult, 0.0, OP.add))(c)
                     for c in range(8)]
-            weave(best[:1] + two[4:])
-            weave(join[:4], [best[1], lambda: offsets(1), best[2], stacks])
-            stacks_out()
-            weave(join[4:], best[3:])
+            act(A("OLD"), NEW)
+            mm(LO_("P7"), A("PERM"), A("OLD"))
+            act(A("YS"), LO_("P7"), AF.Relu, bias=-1.0)
+            dma("s", H(T.ystk[:, :]), A("YS"))
+            weave(best[:2])
+            weave(join[:6], [lambda: counts(1), best[2], lambda: offsets(1), best[3], occupied])
+            mm(A("P6", 0, 256, p=8), A("E8T"), A("OCC"))
+            act(A("YC", p=8), A("P6", 0, 256, p=8))
+            dma("s", H(T.ycnt[:, :]), A("YC", p=8))
+            weave(join[6:])
+            for q, e in enumerate("sa"):
+                dma(e, H(T.ylab[:, 1024 * q:1024 * q + 1024]), A("DK", 1 + 1024 * q, 1025 + 1024 * q))
         else:
             join = [(lambda c: lambda: tt(G("X", XW, "JO", 4 * c, 4 * c + 4), part("OWN", c), part(LI, c), OP.max))(c) for c in range(8)]
             un = unique()
-            weave(join, [lambda: weave(two[4:]), stacks, lambda: offsets(1)] + un[:3]
-                  + [lambda: weave(un[3:5]), lambda: weave(un[5:7])])
-            for q in range(4, 8 - (DQ or 2)):
-                mm(A(LENGTHS[q][0], LENGTHS[q][1], LENGTHS[q][1] + 256), A("IB"), A("WB", 1 + 256 * q, 257 + 256 * q))
-            if not DQ:
-                mm(A("W3"), A("IB"), A("WB", 1537, 2049), True, False)
-            act(A("OCC"), NEW, AF.Sign)
-            for hf in range(2):
-                bank = "P%d" % (6 + hf)
-                mms(A(bank), [(A("IB"), A("WK", 512 * hf, 512 * hf + 512))]
-                    + [(A("IB"), HF("WV", hf), A(bank, r, 512, 4)) for r in range(4)], True, False)
-            mm(Z, A("IB"), A("WV"))
 
-    for q, e in enumerate("sasa"):
-        dma(e, H(T.ylab[:, 512 * q:512 * q + 512]), A("DK", 1 + 512 * q, 513 + 512 * q))
+            def lists():
+                tiles("W3", [q for q in range(4) if q not in NBA])
+                act(A("KT"), LO_("W3"))
+                for hf in (1, 0):
+                    act(A("WK", 512 * hf, 512 * hf + 512), G("WB", 2049, "KT", 64 + 32 * hf, 96 + 32 * hf))
+
+            def popped(hf):
+                bank = "P%d" % (6 + hf)
+                mms(A(bank), [(A("IB"), HF("WV", hf), A(bank, r, 512, 4)) for r in range(4)], True, False)
+
+            def tile(hf):
+                mm(A("P%d" % (6 + hf)), A("IB"), A("WK", 512 * hf, 512 * hf + 512), False, False)
+
+            def next_sums():
+                names_by_lane()
+                mm(A("P4", 0, BY_V - 1025), A("IB"), A("WB", 1025, BY_V))
+                mm(Z, A("IB"), A("WV"), True, False)
+                popped(1)
+            between = {"scan": lambda: counts(1), "lists": lists, "occ": occupied, "offsets": lambda: offsets(1),
+                       "next": next_sums, "same0": un[0], "same1": un[1], "same2": un[2], "heights": heights,
+                       "spare": lambda: weave([] if SPLIT[t + 1] else un[3:]),
+                       "popped0": lambda: popped(0), "tile0": lambda: tile(0), "tile1": lambda: tile(1)}
+            for c in range(8):
+                join[c]()
+                for n_ in JOIN[c].split():
+                    between[n_]()
 
     emit(g, T, Q, ops, nsent[0])
 

from concourse.mybir import AluOpType, ActivationFunctionType

STEPS = 4
XW = 2120
BY_V = 1152
BY_DMA = 1152
XVFIRST = 0
RMS = 1
TIS = 0
NEORD = 1
NBA = (1, 0)
LO_V = (256, 384)
NEG_S = 128
SUMS0 = 0
BY_V0 = 1536
SPLIT = (1, 0, 0, 0)
EXA = 128
HALVES = ((1, 0, 128), (1, 128, 256))
PARTS = ((0, 0, 256), (2, 0, 256), (3, 0, 192), (3, 192, 256))
PUSH = ("hit0 w hit1 w", "givers", "w count", "empties ranks", "w", "w", "pick",
        "w places w cut0 w cut1", "kept mask", "givers_cut")
JOIN = ("scan lists", "occ", "offsets next", "same0", "same1", "same2 popped0 heights tile1", "tile0", "spare")
TURN = (1024, 1408, 1536, 1920)
LABELS = ((0, 256), (256, 384), (384, 512))
MW = 72

F, B, I, U, NM = "float32", "bfloat16", "int32", "uint16", "float16"
_S = {
    "X": (XW, F), "WB": (2064, B), "LABI": (2064, I), "NBI": (2064, I),
    "STI": (256, I), "CNI": (256, I), "CNF": (256, B), "XK": (4096, F), "XV": (256, F), "DK": (4096, F),
    "CMP": (4096, B), "PI": (16, I), "COL": (48, F), "IS": (256, F),
    "M0": (144, B), "IW": (4 * 144, F), "TL": (4 * 144, B), "FO": (144, B), "SR": (1024, B),
    "NI": (128, B), "IP": (128, B), "TT": (128, B), "BH": (128, B),
    "CT": (256, B), "ONES": (256, B), "DA": (16, F), "HOLD": (256, F), "LST": (84, U),
    "RZ": (640, B), "EY": (256, NM), "SETS": (36, F), "JB": (4, F), "JT": (32, F), "E8T": (8, B), "FO32": (144, F),
    "VF": (16, F), "VU": (16, U), "KA": (256, NM), "KT": (256, U), "WV": (256, B), "WF": (256, F), "WK": (1024, B),
    "SC": (256, F), "SB": (1280, B), "EX": (512, NM), "ZO": (16, U), "JO": (32, U),
    "NE": (1280, B), "INS": (256, B), "INE": (256, B), "GA": (64, NM),
    "ZS": (256, F), "ZM": (256, F), "HIT": (256, B), "TI": (256, I), "TA": (256, I), "E0": (128, F), "E1": (128, F),
    "KY": (256, NM), "SPR": (128, F), "SPU": (128, F), "STA": (264, F), "ST1": (256, NM), "TOP": (256, NM), "A1": (256, NM), "OLD": (256, NM),
    "OCC": (256, B), "FS": (256, B), "FE": (256, B), "JK": (1024, B), "SA": (8, F), "SL": (4, U), "GU": (32, U),
    "RE": (16, U), "MSK": (32, B), "RM": (64, NM),
    "RW": (32, F), "RU": (32, U), "RCV": (256, NM), "OWN": (512, F), "YS": (256, F), "YC": (256, F),
}
POOL = {}
for _n, _d, _l in (("CB", B, "IB NIB BO NBO E8 DG DN DHF N4 N4X T2 PERM SH ISH I7 I8 ZERO"),
                   ("CF", F, "IG I32")):
    for _k, _c in enumerate(_l.split()):
        POOL[_c] = (_n, 128 * _k)
    _S[_n] = (128 * len(_l.split()), _d)
for _t in range(STEPS):
    for _n, _w in (("D", 2064), ("MO", MW), ("MI", MW), ("CO", 4), ("CI", 4), ("LO", 512), ("LI", 512)):
        _S["%s%d" % (_n, _t)] = (_w, F)
SCRATCH = {k: ("sbuf", [128, w], d) for k, (w, d) in _S.items()}
PSUM = ["W0", "W1", "W2", "W3", "P4", "P5", "P6", "P7"]
for _k in PSUM:
    SCRATCH[_k] = ("psum", [128, 512], F)
BLOCK = {"W3": 16, "ZM": 32, "WF": 32, "SPU": 16}
for _k, _w in BLOCK.items():
    SCRATCH[_k] = (SCRATCH[_k][0], [128, SCRATCH[_k][1][1] // _w, _w], F)
NDMA = 22
SEMAPHORES = ["ev", "ea", "ep", "eg", "sent"] + ["d%d" % k for k in range(NDMA)] + \
    ["%s%d" % (n, t) for n in ("ct", "nm", "la", "lb", "lc")[:2 + len(LABELS)] for t in range(STEPS)]

OP = AluOpType
AF = ActivationFunctionType
SPREAD = 33825.0 * 256.0
BITS = 0x888800


def rank_program(g, core, T, topo):
    rank = T.rank_of(core)
    if rank is None:
        return
    ops = []
    Q = {"v": g.vector, "a": g.scalar, "p": g.tensor, "g": g, "s": g.sync}

    def A(n, lo=0, hi=None, st=1, p=128):
        if n in POOL:
            hi = POOL[n][1] + (128 if hi is None else hi)
            lo = POOL[n][1] + lo
            n = POOL[n][0]
        if n in BLOCK:
            w = BLOCK[n]
            hi = w * SCRATCH[n][1][1] if hi is None else hi
            ap = T[n][:, lo // w, :] if hi - lo == w else T[n][:, lo // w:hi // w, lo % w:w:st]
            return (ap, [(n, lo, hi, st)], [])
        if hi is None:
            hi = SCRATCH[n][1][1]
        ap = T[n][0:p, lo:hi:st] if st != 1 else T[n][0:p, lo:hi]
        return (ap, [(n, lo, hi, st)], [])

    def HB(n, hf, lo=0):
        w = BLOCK[n]
        return (T[n][:, lo // w:(lo + 256) // w, hf * w // 2:(hf + 1) * w // 2],
                [(n, c, c + w // 2, 1) for c in range(lo + hf * w // 2, lo + 256, w)], [])

    def HF(n, hf, base=0):
        return A(n, base + 128 * hf, base + 128 * hf + 128)

    def LO_(n):
        return A(n, 0, 256)

    def HI_(n):
        return A(n, 256, 512)

    def C(n, c):
        return A(n, c, c + 1)

    def G(n, hi, on, c, d, lo=0):
        return (T[n][:, lo:hi].indirect(T[on][:, c:d]), [(n, lo, hi, 1)], [(on, c, d, 1)])

    def val(x):
        return x[0] if isinstance(x, tuple) else x

    def add(eng, fn, out, ins, kind="c", sem=None):
        rd, wr = [], []
        for o in out:
            wr += o[1]
            rd += o[2]
        for x in ins:
            if isinstance(x, tuple):
                rd += x[1] + x[2]
        ops.append({"e": eng, "fn": fn, "r": rd, "w": wr, "k": kind, "sem": sem})

    def tt(o, a, b, op):
        add("v", lambda: g.vector.tensor_tensor(o[0], a[0], b[0], op), [o], [a, b])

    def ts(o, a, s1, op0, s2=None, op1=None):
        if op1 is None:
            add("v", lambda: g.vector.tensor_scalar(o[0], a[0], val(s1), None, op0), [o], [a, s1])
        else:
            add("v", lambda: g.vector.tensor_scalar(o[0], a[0], val(s1), val(s2), op0, op1), [o], [a, s1, s2])

    def cp(o, a):
        add("v", lambda: g.vector.tensor_copy(o[0], a[0]), [o], [a])

    def ms(o, c):
        add("v", lambda: g.vector.memset(o[0], c), [o], [])

    def scan(o, d0, d1, init, op0, op1):
        add("v", lambda: g.vector.tensor_tensor_scan(o[0], d0[0], d1[0], init, op0, op1), [o], [d0, d1])

    def act(o, a, f=AF.Copy, bias=None, scale=None, acc=None):
        kw = {}
        if bias is not None:
            kw["bias"] = val(bias)
        if scale is not None:
            kw["scale"] = val(scale)
        if acc is not None:
            kw["accum_out"] = acc[0]
        add("a", lambda: g.scalar.activation(o[0], a[0], f, **kw), [o] + ([acc] if acc else []), [a, bias, scale])

    def mm(o, l, r, st=True, sp=True):
        add("p", lambda: g.tensor.matmul(o[0], l[0], r[0], st, sp), [o], [l, r])

    def mms(o, pairs, st=True, sp=True):
        for k, q in enumerate(pairs):
            mm(q[2] if len(q) > 2 else o, q[0], q[1], st and k == 0, sp and k == len(pairs) - 1)

    def iota(o, pat, base=0, cm=0, isint=False):
        if isint:
            add("g", lambda: g.iota(o[0], pat, base, cm), [o], [])
        else:
            add("g", lambda: g.iota(o[0], pat, base, cm, allow_small_or_imprecise_dtypes=True), [o], [])

    def select(o, a, pat, op, fill_, base, cm=1):
        add("g", lambda: g.affine_select(o[0], a[0], pat, op, fill_, base, cm), [o], [a])

    nd = [0]

    def dma(q, o, a, adding=False):
        s = "d%d" % nd[0]
        nd[0] += 1
        if adding:
            add(q, lambda: g.dma_start(o[0], a[0], accum_op=OP.add), [o], [a, o], kind="d", sem=s)
        else:
            add(q, lambda: Q[q].dma_start(o[0], a[0]), [o], [a], kind="d", sem=s)

    def H(ap):
        return (ap, [], [])

    nsent = [0]

    def send(src, dst, sem, peer, lo, hi):
        rid, pid, _ = topo.addr(peer)
        m = topo.mask(core, peer)
        nsent[0] += len(topo.engines(core, peer))
        o, a = A(dst, lo, hi), A(src, lo, hi)
        add("g", lambda: g.remote_dma(o[0], a[0], T.sem[sem], T.sem.sent, pid, rid, m), [], [a], kind="r")
        ops.append({"e": "x", "fn": None, "r": [], "w": o[1], "k": "x", "sem": (sem, len(topo.engines(peer, core)))})

    def weave(*lists):
        lists = [list(l) for l in lists]
        while any(lists):
            for l in lists:
                if l:
                    l.pop(0)()

    ms(A("NBI", 0, 4), -1)
    ms(A("LABI", 0, 4), 0)
    ms(A("WB", 0, 8), 1.0)
    dma("s", A("CNI", p=8), H(T.cnt[:, :]))
    dma("a", A("STI"), H(T.stk[:, :]))
    for n_, src in (("NBI", T.nb), ("LABI", T.lab)):
        dma("a", A(n_, 1025, 2049), H(src[:, 1024:2048]))
        dma("s", (T[n_][:, 1:1025], [(n_, 0, 1025, 1)], []), H(src[:, 0:1024]))
    dma("s", (T.WB[:, 1:2049], [("WB", 0, 2064, 1)], []), H(T.ln[:, :]))

    ncol = [9]

    def col(src, m, a):
        c = C("COL", ncol[0])
        ncol[0] += 1
        act(c, src, AF.Identity, bias=a, scale=m)
        return c

    def fill(o, c):
        iota(o, [[0, len(range(*o[1][0][1:]))]], c)

    def diagonal(n_, c):
        select(A(n_), A("ZERO"), [[-1, 128]], OP.not_equal, c, 0)

    def pick(src):
        scan(A("SC"), A("HOLD"), src, 0.0, OP.add, OP.min)

    def lists_of_names():
        pick(LO_("P6"))
        for n_ in ("VU", "VF"):
            act(A(n_), A("SC", 15, 256, 16), AF.Identity, bias=cWin)

    def neighbours():
        act(A("KA"), G("NBI", 2049, "VU", 0, 16), AF.Identity, bias=1.0)

    def tiles(bank, which):
        for q in which:
            mms(A(bank, 64 * q, 64 * q + 64),
                [(A("TL", 144 * q + 12 - 4 * e, 144 * q + 140 - 4 * e), A("KA", e, 256, 4)) for e in range(4)])

    def names_by_lane():
        for hf in range(2):
            mm(HB("W3", hf), HF("KA", hf), A("IP"))
        mm(HI_("W3"), A("IB"), A("CT"), True, False)

    def lengths():
        act(A("WV"), G("WB", 2049, "VU", 0, 16))
        for hf in range(2):
            select(HB("WF", hf), HF("WV", hf), [[0, 128]], OP.is_ge, 0.0, 0)

    def repeated_names():
        act(A("EY"), G("VF", 16, "LST", 0, 16))

    def unique():
        def count():
            scan(A("SB", 0, 384), A("RZ", 0, 384), A("NE", 0, 384), 0.0, OP.mult, OP.subtract)
            mms(A("P5", 352, 368), [(A("IB"), A("EY", 0, 256, 16)), (A("N4X"), A("SB", 15, 256, 16)),
                                    (A("N4"), A("SB", 271, 384, 16), A("P5", 352, 360))])
        return [lambda: tt(LO_("NE"), A("EY"), LO_("P6"), OP.is_equal),
                lambda: tt(A("NE", 256, 384), HF("EY", 0), HF("P6", 1), OP.is_equal), count] + \
            [(lambda hf: lambda: ts(A("ZO", hf, 16, 2), A("P5", 352 + 8 * hf, 360 + 8 * hf), cDum[hf], OP.min))(hf)
             for hf in range(2)]

    iota(C("PI", 0), [[0, 1]], 0, 1, True)
    iota(A("IG"), [[16, 8], [0, 16]])
    iota(A("IS"), [[0, 16], [1, 16]])
    iota(A("IW"), [[1, 576]])
    ms(A("ONES"), 1.0)
    ms(A("ZERO"), 0.0)
    for k, m in enumerate((15, 112, 1, 3, 12, 8, 2, 4)):
        ts(C("PI", 1 + k), C("PI", 0), m, OP.bitwise_and)
    ms(A("STA", 256, 264), 0.0)
    cp(A("COL", 0, 9), A("PI", 0, 9))
    cP, cA, cG, cOdd, cR, cQ, c8, c2, c4 = [C("COL", k) for k in range(9)]
    ms(A("X", 0, 1), 0.0)
    act(A("CNF", p=8), A("CNI", p=8))
    act(A("TOP"), A("STI"), AF.Identity, bias=1.0)
    ts(A("E8"), A("IG"), 1.0 / 16, OP.mult, cP, OP.is_equal)
    ts(A("HOLD"), A("IS"), cA, OP.is_le, 1052672.0, OP.mult)
    mm(LO_("P4"), A("E8", p=8), A("CNF", p=8))
    ts(A("BO"), A("IG"), cG, OP.is_equal)
    cTl = col(cR, 1.0, cG)
    cWin = col(cA, -4096.0, 61440.0)
    cTl = col(cQ, 36.0, cTl)
    cKeep = col(cA, -4096.0, -4096.0)
    ts(A("DA"), A("IS", 0, 16), cA, OP.is_equal)
    act(A("HOLD"), A("HOLD"), AF.Identity, bias=-4096.0)
    ts(LO_("P5"), LO_("P4"), -1.0, OP.add, cA, OP.is_equal)
    im, im144 = A("IW", 0, 128), A("IW", 0, 144)
    ts(A("IB"), im, cP, OP.is_equal)
    tt(A("A1"), A("TOP"), LO_("P5"), OP.mult)
    act(LO_("P4"), LO_("P4"), AF.Relu, bias=cKeep, scale=4096.0)
    mm(LO_("P6"), A("BO"), A("A1"))
    ts(A("M0"), im144, -15.0, OP.add, cG, OP.is_equal)
    ts(A("TL", 144, 288), A("IW", 144, 288), -12.0, OP.add, cTl, OP.is_equal)
    cS = col(c8, 0.125, 0.0)
    act(A("LST", 0, 16), A("IS", 0, 16))
    cS = col(c4, 0.5, cS)
    cFo = col(cA, 0.5, cG)
    cS = col(c2, 2.0, cS)
    cDg = col(cA, 1.0, -15.0)
    cS = col(cOdd, 8.0, cS)
    cNext = col(C("DA", 15), -1.0, 1.0)
    cPerm = col(cS, 1.0, cG)
    cNext = col(cA, 1.0, cNext)
    cM1, cLast = col(cP, 1.0, -1.0), col(C("DA", 15), 4096.0, -4096.0)
    cDum = [col(cA, 1.0, 2049.0 + 16 * k) for k in range(4)]
    act(A("DG"), A("IB"), AF.Identity, scale=cDg)
    act(A("N4X"), A("IB"), AF.Identity, scale=cLast)
    lists_of_names()
    for lo, hi in ((0, 144), (288, 576)):
        ts(A("TL", lo, hi), A("IW", lo, hi), -12.0, OP.add, cTl, OP.is_equal)
    neighbours()
    tiles("P5", (1, 0, 2, 3))
    repeated_names()
    act(A("KT"), LO_("P5"))
    late_cols = {}

    def push_constants():
        cJb, cCap = col(cA, -2.0, -65.0), col(cS, -4096.0, -4096.0)
        late_cols["top"], late_cols["re"] = col(cS, -4096.0, 0.0), col(cWin, 1.0, 39.5)
        act(A("JB"), A("IS", 0, 4), AF.Identity, bias=cJb, scale=-32.0)
        late_cols["cap"] = col(C("DA", 15), -1048576.0, cCap)

    for t in range(STEPS):
        fill(A("D%d" % t, 0, 1), 1)
    diagonal("I32", 1.0)
    diagonal("N4", -4096.0)
    for k in range(4):
        iota(A("NI", 32 * k, 32 * k + 32), [[4, 2], [8, 2], [16, 8]], k // 2 + 2 * (k % 2))
    select(A("T2"), A("BO"), [[-1, 128]], OP.is_gt, 0.0, 0)
    iota(A("SETS", 0, 32), [[16, 2], [1, 4], [4, 4]])
    iota(A("SETS", 32, 36), [[32, 2], [4, 2]])
    for k in range(4):
        iota(A("CT", 64 * k, 64 * k + 64), [[-4, 2], [-8, 2], [0, 16]], 15 - k // 2 - 2 * (k % 2))
    select(A("RZ", 256, 384), A("ONES", 0, 128), [[0, 8], [1, 16]], OP.not_equal, 0.0, 0, 0)
    for k in range(4):
        iota((T.SPU[:, :, 4 * k:4 * k + 4], [("SPU", 0, 128, 1)], []), [[0, 8], [16, 2], [1, 2]], 4096 * (k // 2) + 256 * (k % 2))

    def late_lists():
        for t in range(STEPS):
            fill(A("MO%d" % t, 0, 8), 0)
        diagonal("DN", 32.5)
        diagonal("DHF", -0.5)
        for r in range(0, 8, 2):
            select(A("SR", 128 * r, 128 * r + 256), A("ONES"), [[-2, 2], [-16, 8], [0, 16]], OP.is_equal, 0.0, -2 * r)
        select(A("RZ", 384, 640), A("ONES"), [[0, 16], [1, 16]], OP.not_equal, 0.0, 0, 0)
        diagonal("NIB", -1.0)
        select(A("I8"), A("IB"), [[0, 64], [1, 2]], OP.is_equal, 0.0, 0, 0)
        select(A("I7"), A("I8"), [[0, 8], [1, 16]], OP.not_equal, 0.0, -14, 0)

    tt(A("ST1"), A("TOP"), LO_("P4"), OP.min)
    ts(A("PERM"), im, cPerm, OP.is_equal)
    ts(A("RZ", 0, 256), A("IS"), cNext, OP.not_equal)
    ts(A("IP"), A("NI"), cP, OP.is_equal)
    un = unique()
    if NEG_S:
        act(A("X", 1, 1 + NEG_S), A("LABI", 1, 1 + NEG_S), scale=-1.0)
    for lo, hi in ((1025, 2049), (1 + NEG_S, 1025)):
        ts(A("X", lo, hi), A("LABI", lo, hi), -1.0, OP.mult)
    weave(un[:2])

    def meeting_constants():
        cSet, cJt = col(cQ, 4.0, 8.0), col(c8, 0.125, 65.0)
        cSet = col(c8, -3.75, cSet)
        act(A("JT"), A("SETS", 0, 32), AF.Identity, bias=cJt, scale=2.0)
        cSet = col(cR, 4.0, cSet)
        act(A("LST", 48, 80), A("SETS", 0, 32))
        cSet = col(cOdd, -3.0, cSet)
        act(A("LST", 80, 84), A("SETS", 32, 36), AF.Identity, bias=cSet)

    def flight_constants():
        cp(A("FO32"), A("FO"))
        ts(A("SH"), im, cM1, OP.is_equal, cOdd, OP.mult)
        ts(A("NBO"), A("BO"), -1.0, OP.mult)
        ts(A("E8T"), A("IS", 0, 8), 16.0, OP.mult, cG, OP.is_equal)
        tt(A("ISH"), A("IB"), A("SH"), OP.subtract)

    def fold(o, by, src, lo):
        mms(o, [(A(by, 8 - 8 * e, 136 - 8 * e), A(src, lo + e, lo + 64, 2)) for e in range(2)])

    P, Z, WP = LO_("P5"), HI_("P4"), LO_("P4")
    NEW, R = LO_("W2"), HI_("W2")
    HITS = ("P5", "P6")
    for t in range(STEPS):
        last = t == STEPS - 1
        peer = T.cores[rank ^ (1 << (t % 2))]
        D, MO, MI, CO, CI, LO, LI = ["%s%d" % (n_, t) for n_ in ("D", "MO", "MI", "CO", "CI", "LO", "LI")]

        def gathered(o, win, on, c, d):
            if win == "X" and t == 0:
                act(o, G("LABI", 2049, on, c, d), scale=-1.0)
            else:
                act(o, G(win, 2049, on, c, d))

        def gather(o, win, q, lo=0, hi=256):
            gathered(A(o, 1024 * q + 4 * lo, 1024 * q + 4 * hi), win, "KT", 64 * q + lo // 4, 64 * q + hi // 4)

        def nbr(n, q, r, lo=0, hi=256):
            return A(n, 1024 * q + 4 * lo + r, 1024 * q + 4 * hi, 4)

        def own(q, q2, hf):
            lo = 512 * hf
            tt(A("XK", 1024 * q + lo, 1024 * q + lo + 512), G("X", 2049, "KT", 64 * q + 32 * hf, 64 * q + 32 * hf + 32),
               A("XK", 1024 * q2 + lo, 1024 * q2 + lo + 512), OP.max)

        def add_lengths(lo, hi, bank, at):
            tt(A(D, lo, hi), A("X", lo, hi), A(bank, at, at + hi - lo), OP.add)

        def sums(qs):
            for q in qs:
                add_lengths(1 + 256 * q, 257 + 256 * q, "W%d" % (q // 2), 256 * (q % 2))

        def link(c, q, r, hf=None, out=None):
            c = c if hf is None else HF("P4", hf, 256) if c is Z else HF("P5", hf)
            lo, hi = (0, 256) if hf is None else (128 * hf, 128 * hf + 128)
            tt(out or c, nbr("XK", q, r, lo, hi), c, OP.max)

        def heights():
            for hf in range(2):
                mm(HB("W3", hf, 256), HF("OCC", hf), A("BH"), False, False)
            mm(R, A("BO"), A("OCC"), True, False)

        def new_labels():
            for hf in range(2):
                tt(HF("P4", hf, 256), HB("ZM", hf), HF("P4", hf), OP.subtract)

        def met(hf):
            if t:
                mm(HF("W1", hf), A("I32"), HB("ZM", hf), False, hf == 1)

        def meet(hf):
            tt(HB("ZM", hf), HF("ZS", hf), HF("P5", hf), OP.max)
            met(hf)
        split = SPLIT[t]
        if t:
            dma("g", A(D, BY_DMA, 2049), A("X", BY_DMA, 2049), True)
            add_lengths(1025, BY_V, "P4", 0)
            if BY_V < BY_DMA:
                mms(A("P5", 256, 256 + BY_DMA - BY_V), [(A("IB"), A("WB", BY_V, BY_DMA)), (A("I32"), A("X", BY_V, BY_DMA))])
            sums((3, 2, 1) if split else (3, 2, 1, 0))
        for hf in range(2):
            gather("XK", "X", 1, 128 * hf, 128 * hf + 128)
            if t and hf == 0 and not XVFIRST:
                mm(A("P6"), A("I32"), A("XK", 1024, 1536), False, True)
        if t == 0:
            for q in range(4):
                mm(A("W%d" % q), A("IB"), A("WB", 1 + 512 * q, 513 + 512 * q), True, q < 3 or BY_V0 == 2048)
            if BY_V0 < 2048:
                mm(A("W3"), A("I32"), A("X", 1537, 2049), False, True)
            lengths()
            mm(WP, A("IB"), A("WV"))
            mm(Z, A("IB"), A("WV"), True, False)
        gathered(A("XV"), "X", "VU", 0, 16)
        mm(Z, A("I32"), A("XV"), False, True)
        if t:
            if XVFIRST:
                mm(A("P6"), A("I32"), A("XK", 1024, 1536), False, True)
            mm(A("P7"), A("I32"), A("XK", 1536, 2048), False, True)
            mm(LO_("W1"), A("NIB"), A("WV"), True, False)
            if BY_V < BY_DMA:
                act(A(D, BY_V, BY_DMA), A("P5", 256, 256 + BY_DMA - BY_V))
        gather("XK", "X", 2, 0, 128 if split else 256)
        act(HF("P5", 0) if split else P, nbr("XK", 2, 0, 0, 128 if split else 256))
        if t and split:
            own(0, 1, 0)
            sums((0,))
            own(3, 0, 0)
            own(0, 1, 1)
            link(Z, 3, 0, 0)
            link(P, 3, 1, 0)
            own(3, 0, 1)
        else:
            sums(range(0 if t else SUMS0))
            own(0, 1, 0)
            if t == 0:
                un[2]()
            own(0, 1, 1)
            if t == 0:
                if BY_V0 < 2048:
                    act(A(D, 1537, 2049), A("W3"))
                late_lists()
                for u in range(1, STEPS):
                    dma("g", A("D%d" % u, BY_DMA, 2049), A("WB", BY_DMA, 2049))
                sums(range(SUMS0, BY_V0 // 256))
            own(3, 0, 0)
            own(3, 0, 1)
            if split:
                link(Z, 3, 0, 0)
                link(P, 3, 1, 0)
        if t == 0:
            mms(HF("P6", 0), [(A("T2"), A("IP")), (A("DG"), A("IP"))])
            mm(A("P6", 256, 384), A("BO"), A("IP"))
            mm(NEW, A("PERM"), A("ST1"))
            names_by_lane()
        late = list(un[3:]) if t == 0 or split or "spare" not in JOIN[7] else []
        if t == 0:
            late += [lambda: cp(A("TT"), HF("P6", 0)), lambda: cp(A("BH"), A("P6", 256, 384)),
                     lambda: ts(A("FO"), im144, -8.0, OP.add, cFo, OP.is_equal)]
        if split:
            if t:
                link(Z, 3, 2, 0)
                link(P, 3, 3, 0)
            own(2, 3, 1)
            if t == 0:
                link(Z, 3, 2, 0)
                link(P, 3, 3, 0)
            weave([lambda: link(Z, 2, 1, 0), lambda: link(P, 2, 2, 0), lambda: link(Z, 2, 0, 1),
                   lambda: link(Z, 2, 3, 0, HF("ZS", 0)), late[0], lambda: link(Z, 2, 1, 1), late[1], lambda: meet(0),
                   lambda: link(Z, 2, 2, 1)] + late[2:])
        else:
            link(Z, 3, 0, 0)
            link(Z, 3, 0, 1)
            for k, (q, r) in enumerate(((3, 1), (3, 2), (3, 3), (2, 1), (2, 2))):
                link(Z if k % 2 else P, q, r)
            for hf in range(2):
                link(Z, 2, 3, hf, HF("ZS", hf))
            weave(late[:1])
            meet(0)
            meet(1)
            weave(late[1:])
        for part_ in (PARTS if t else HALVES + PARTS):
            gather("DK", D, *part_)
        if t == 0:
            act(A("OCC"), NEW, AF.Sign)
            push_constants()
        else:
            act(A("OLD"), NEW)

        def compare(q, r, lo, hi):
            i = 4 * q + r
            c = A("CMP", 256 * i + lo, 256 * i + hi)
            if q == 1 and t:
                tt(c, A("P%d" % (6 + lo // 128), r, 512, 4), HB("ZM", lo // 128), OP.is_lt)
            else:
                tt(c, nbr("DK", q, r, lo, hi), A("W1", lo, hi) if t else A("P4", 256 + lo, 256 + hi), OP.is_lt)
            for hf in range(2 if i < 15 else 0):
                a, b = max(lo, 128 * hf), min(hi, 128 * hf + 128)
                if a < b:
                    mm(A(HITS[hf], a, b), A("M0", 15 - i, 143 - i), A("CMP", 256 * i + a, 256 * i + b),
                       i == 4 and a == 128 * hf, i == 14 and b == 128 * hf + 128)
        zs = [(lambda b: lambda: tt(G("X", XW, "ZO", 2 * b, 2 * b + 2), A("ZM", 32 * b, 32 * b + 32),
                                    A("WF", 32 * b, 32 * b + 32), OP.subtract))(b) for b in range(8)]
        if t == 0:
            if split:
                link(Z, 2, 3, 1, HB("ZM", 1))
                zs.pop(0)()
            new_labels()
            if not split:
                zs.pop(0)()
        for q, lo, hi in HALVES + PARTS:
            if (q, lo, hi) == PARTS[-1] and t == 0:
                heights()
            for r in range(4 if q < 3 else 3):
                if (q, r, lo) == (1, 2, 0) and t and split:
                    link(Z, 2, 3, 1, HB("ZM", 1))
                    met(1)
                compare(q, r, lo, hi)
        compare(3, 3, 0, 256)

        def hits(hf):
            act(HF("HIT", hf), HF(HITS[hf], hf), AF.Sign)
            mm(HB("W3", hf, 256), HF("HIT", hf), A("TT"), False, hf == 1)

        def givers():
            scan(A("INS"), A("FS"), A("ONES"), -192.0, OP.add, OP.add)
            for c in range(4):
                act(A("JK", 256 * c, 256 * c + 256), A("INS"), AF.Sign, bias=C("JB", c), scale=-1.0, acc=C("SA", c))
            act(NEW, R, AF.Relu, bias=late_cols["top"], scale=4096.0)
            if not last:
                act(R, R, AF.Relu, bias=late_cols["cap"], scale=4096.0)
            act(A("SL"), A("SA", 0, 4), AF.Identity, bias=128.0, scale=0.5)
            if t == 0:
                meeting_constants()

        def count():
            ts(C(CO, 0), C("SA", 4), -128.0, OP.min, -0.5, OP.mult)
            send(CO, CI, "ct%d" % t, peer, 0, 1)

        def ranks():
            mms(HI_("P7"), [(A("DN"), A("FE")), (A("DHF"), A("INE"))])
            mms(LO_("P7"), [(A("DN"), A("FS")), (A("DHF"), A("INS"))])
        small = {
            "w": lambda: zs.pop(0)() if zs else None, "hit0": lambda: hits(0), "hit1": lambda: hits(1),
            "givers": givers, "count": count, "ranks": ranks, "pick": lambda: pick(HI_("P7")),
            "empties": lambda: scan(A("INE"), A("FE"), A("ONES"), 0.0, OP.add, OP.add),
            "places": lambda: ts(A("RE"), A("SC", 15, 256, 16), late_cols["re"], OP.add, 7.0, OP.max),
            "cut0": lambda: tt(A("ST1" if last else "TOP"), LO_("STA"), NEW, OP.min),
            "cut1": lambda: None if last else tt(A("ST1"), LO_("STA"), R, OP.min),
            "kept": lambda: ts(LO_("P7"), LO_("P7"), C(CI, 0), OP.is_lt, 4096.0, OP.mult),
            "givers_cut": lambda: tt(A("A1"), A("ST1"), LO_("P7"), OP.min),
            "mask": lambda: ts(A("MSK"), A("JT"), C(CO, 0), OP.is_le, 4096.0, OP.mult)}

        def spare(k):
            for n_ in PUSH[k].split():
                small[n_]()
        mm(LO_("P7"), A("BO"), A("CMP", 3840, 4096))
        spare(0)
        mm(R, A("BO"), A("HIT"), False, False)
        act(A("FS"), LO_("P7"), AF.Sign)
        for k in range(TIS):
            act(HF("TI", k), HF("W3", k, 256), scale=SPREAD)
        mm(R, A("IB"), A("FS"), False, True)
        act(A("FS"), R, AF.Sign, bias=-8.5)
        act(A("FE"), R, AF.Sign, bias=0.5, scale=-1.0, acc=C("SA", 4))
        if t == 0:
            act(A("OLD"), NEW)
            act(A("SPR"), A("SPU"), scale=float(BITS & -BITS))
        for hf in range(2):
            mm(HF(HITS[hf], hf), A("N4"), HF("OCC", hf), True, False)
        if t and not last:
            mm(LO_("W1"), A("IB"), A("WB", 513, 769))
        for k in range(TIS, 2):
            ts(HF("TI", k), HF("W3", k, 256), SPREAD, OP.mult)
        for k in range(2):
            ts(HF("TA", k), HF("TI", k), BITS, OP.bitwise_and)
        tt(A("E0"), HF("TA", 0), HF("W3", 0), OP.add)
        tt(HF("W3", 1), HF("TA", 1), HF("W3", 1), OP.add)
        for s in range(4):
            spare(1 + s)
            e, o = "E%d" % (s % 2), 128 + 128 * (s % 2)
            e2, o2 = "E%d" % (1 - s % 2), 256 - 128 * (s % 2)
            for k in range(2):
                for b, op in enumerate((OP.min, OP.max)):
                    if s == 3:
                        out = A("W3", 128 * k + b, 128 * k + 128, 2)
                    else:
                        out = A(e2, b, 128, 2) if k == 0 else A("W3", o2 + b, o2 + 128, 2)
                    tt(out, A(e, 64 * k, 64 * k + 64), A("W3", o + 64 * k, o + 64 * k + 64), op)
        spare(5)
        for k in range(2):
            tt(HF("KY", k), HF("W3", k), A("SPR"), OP.subtract)
            mm(HF(HITS[k], k), HF("KY", k), A("IB"), False, True)
        spare(6)
        for k in range(2):
            tt(HF("STA", k), HF(HITS[k], k), HF("OLD", k), OP.max)
        act(A(MO, 8, MW), G("STA", 264, "SL", 0, 4))
        send(MO, MI, "nm%d" % t, peer, 0, MW)
        act(A("GA"), G("STA", 264, "SL", 0, 4))
        fold(A("P6", 256, 288), "FO", "GA", 0)
        spare(7)
        act(A("GU"), A("P6", 256, 288))
        act(A(LO, 0, LO_V[0]), G("X", 2049, "GU", 0, LO_V[0] // 16))
        send(LO, LI, "la%d" % t, peer, *LABELS[0])
        for lo, hi in ((LO_V[0], LO_V[1]),) if LO_V[1] < 512 else LABELS[1:]:
            act(A(LO, lo, hi), G("X", 2049, "GU", lo // 16, hi // 16))
        if t == 0:
            flight_constants()
        spare(8)
        if LO_V[1] < 512:
            cp(A(LO, LO_V[1], 512), G("X", 2049, "GU", LO_V[1] // 16, 32))
        for k, (lo, hi) in enumerate(LABELS[1:]):
            send(LO, LI, "l%s%d" % ("bc"[k], t), peer, lo, hi)

        def turn(lo, hi):
            if last:
                ts(A("DK", 1 + lo, 1 + hi), A("X", 1 + lo, 1 + hi), -1.0, OP.mult)
        turn(0, TURN[0])

        sets = ((256, 192), (448, 128), (576, 64))

        def equal_names(h):
            e, o = 256 * h, 640 * h
            return [lambda: tt(A("NE", o, o + 256), A("EX", e, e + 256), A("P4", e, e + 256), OP.is_equal)] + \
                [(lambda s, w: lambda: tt(A("NE", o + s, o + s + w), A("EX", e, e + w), A("P4", e + 256 - w, e + 256),
                                          OP.is_equal))(s, w) for s, w in sets]

        def counts(h):
            o, sm = 640 * h, 64 + 16 * h
            scan(A("SB", o, o + 256), LO_("RZ"), A("NE", o, o + 256), 0.0, OP.mult, OP.subtract)
            scan(A("SB", o + 256, o + 640), A("RZ", 256, 640), A("NE", o + 256, o + 640), 0.0, OP.mult, OP.subtract)
            mms(A("P5", sm, sm + 16),
                [(A("IB"), A("EX", 256 * h, 256 * h + 256, 16)), (A("IB"), A("MSK", 16 * h, 16 * h + 16)),
                 (A("N4X"), A("SB", o + 15, o + 256, 16))]
                + [(A("N4"), A("SB", o + s + 15, o + s + w, 16), A("P5", sm, sm + w // 16)) for s, w in sets])

        def offsets(h):
            for k in range(4):
                ts(A("JO", 16 * h + k, 16 * h + 16, 4), A("P5", 64 + 16 * h + 4 * k, 68 + 16 * h + 4 * k), cDum[k], OP.min)
        (act if RMS else cp)(A("RM"), G(MI, MW, "LST", 80, 84))
        fold(A("P5", 0, 32), "FO32", MI, 8)
        spare(9)
        turn(TURN[0], TURN[1])
        act(A("RW"), A("P5", 0, 32))
        for r in range(8):
            mm(A("P4", r, 512, 8), A("SR", 128 * r, 128 * r + 128), A("RM"))
        if not last:
            mms(LO_("P6"), [(A("BO"), A("TOP")), (A("NBO"), A("ST1"))], True, False)
        act(A("EX", 0, EXA), G("RW", 16, "LST", 48, 48 + EXA // 16))
        cp(A("EX", EXA, 256), G("RW", 16, "LST", 48 + EXA // 16, 64))
        turn(TURN[1], TURN[2])
        act(A("RCV"), G(MI, MW, "RE", 0, 16))
        act(A("RU"), A("RW"))
        if not last:
            mm(LO_("P6"), A("SR", 896, 1024), A("RCV"), False, True)
        act(HI_("EX"), G("RW", 32, "LST", 64, 80))
        act(A("OWN"), G("X", 2049, "RU", 0, 32))
        one, two = equal_names(0), equal_names(1)
        if last:
            act(A("DK", 1 + TURN[2], 1 + TURN[3]), A("X", 1 + TURN[2], 1 + TURN[3]), scale=-1.0)
        weave([one[k] for k in (2, 3, 0, 1)])
        if NEORD:
            counts(0)
        if last:
            turn(TURN[3], 2048)
        else:
            lists_of_names()
        if not NEORD:
            counts(0)
        if NEORD < 2:
            two[2]()
        mms(NEW, [(A("SH"), A("ST1")), (A("ISH"), A("A1")), (A("I8" if last else "I7"), A("RCV"))])
        if not last:
            neighbours()
            tiles("W3", NBA)
            repeated_names()
            lengths()
        two[0]()
        offsets(0)
        weave([two[1], two[3]] if NEORD < 2 else two[1:])

        def part(n, c, w=1):
            return A(n, 64 * c, 64 * (c + w))

        def occupied():
            ts(A("OCC"), NEW, 0.0, OP.is_gt)
        if last:
            best = [(lambda c: lambda: tt(part("OWN", c, 2), part("OWN", c, 2), part(LI, c, 2), OP.max))(c) for c in range(0, 8, 2)]
            join = [(lambda c: lambda: ts(G("DK", XW, "JO", 4 * c, 4 * c + 4), part("OWN", c), -1.0, OP.mult, 0.0, OP.add))(c)
                    for c in range(8)]
            act(A("OLD"), NEW)
            mm(LO_("P7"), A("PERM"), A("OLD"))
            act(A("YS"), LO_("P7"), AF.Relu, bias=-1.0)
            dma("s", H(T.ystk[:, :]), A("YS"))
            weave(best[:2])
            weave(join[:6], [lambda: counts(1), best[2], lambda: offsets(1), best[3], occupied])
            mm(A("P6", 0, 256, p=8), A("E8T"), A("OCC"))
            act(A("YC", p=8), A("P6", 0, 256, p=8))
            dma("s", H(T.ycnt[:, :]), A("YC", p=8))
            weave(join[6:])
            for q, e in enumerate("sa"):
                dma(e, H(T.ylab[:, 1024 * q:1024 * q + 1024]), A("DK", 1 + 1024 * q, 1025 + 1024 * q))
        else:
            join = [(lambda c: lambda: tt(G("X", XW, "JO", 4 * c, 4 * c + 4), part("OWN", c), part(LI, c), OP.max))(c) for c in range(8)]
            un = unique()

            def lists():
                tiles("W3", [q for q in range(4) if q not in NBA])
                act(A("KT"), LO_("W3"))
                for hf in (1, 0):
                    act(A("WK", 512 * hf, 512 * hf + 512), G("WB", 2049, "KT", 64 + 32 * hf, 96 + 32 * hf))

            def popped(hf):
                bank = "P%d" % (6 + hf)
                mms(A(bank), [(A("IB"), HF("WV", hf), A(bank, r, 512, 4)) for r in range(4)], True, False)

            def tile(hf):
                mm(A("P%d" % (6 + hf)), A("IB"), A("WK", 512 * hf, 512 * hf + 512), False, False)

            def next_sums():
                names_by_lane()
                mm(A("P4", 0, BY_V - 1025), A("IB"), A("WB", 1025, BY_V))
                mm(Z, A("IB"), A("WV"), True, False)
                popped(1)
            between = {"scan": lambda: counts(1), "lists": lists, "occ": occupied, "offsets": lambda: offsets(1),
                       "next": next_sums, "same0": un[0], "same1": un[1], "same2": un[2], "heights": heights,
                       "spare": lambda: weave([] if SPLIT[t + 1] else un[3:]),
                       "popped0": lambda: popped(0), "tile0": lambda: tile(0), "tile1": lambda: tile(1)}
            for c in range(8):
                join[c]()
                for n_ in JOIN[c].split():
                    between[n_]()

    emit(g, T, Q, ops, nsent[0])


def emit(g, T, Q, ops, nsent):
    touch, bank = {}, {}
    know = {e: {} for e in Q}
    for j, o in enumerate(ops):
        e = o["e"]
        o["id"] = e if o["k"] == "c" else ("u", j)
        deps = set()
        for acc, isw in ((o["r"], False), (o["w"], True)):
            for (n, lo, hi, st) in acc:
                deps.update(i for q, i in bank.get(n, {}).items() if q != e)
                for w in ((True, False) if isw else (True,)):
                    for (i, l2, h2, s2) in touch.get((n, w), ()):
                        if lo < h2 and l2 < hi and not (st == s2 and (lo - l2) % st):
                            if not (e == "p" and ops[i]["e"] == "p") and ops[i]["k"] != "r":
                                deps.add(i)
        for acc, isw in ((o["r"], False), (o["w"], True)):
            for (n, lo, hi, st) in acc:
                if n in PSUM:
                    bank.setdefault(n, {})[e] = j
                if isw and st == 1:
                    for w in (True, False):
                        touch[(n, w)] = [x for x in touch.get((n, w), ()) if x[1] < lo or hi < x[2] or x[0] == j]
                touch.setdefault((n, isw), []).append((j, lo, hi, st))
        o["wait"] = []
        if e == "x":
            o["clock"] = {}
            continue
        kn = know[e]
        for i in sorted(deps, reverse=True):
            p = ops[i]
            if kn.get(p["id"], -1) >= i:
                continue
            o["wait"].append(i)
            p["need"] = True
            kn[p["id"]] = i
            for k, v in p["clock"].items():
                if kn.get(k, -1) < v:
                    kn[k] = v
        o["clock"] = dict(kn)
    cnt = {e: 0 for e in Q}
    for o in ops:
        if o["k"] == "c":
            if o.get("need"):
                cnt[o["e"]] += 1
                o["tok"] = ("e" + o["e"], cnt[o["e"]])
        elif o["k"] == "d":
            o["tok"] = (o["sem"], 16)
        elif o["k"] == "x":
            o["tok"] = o["sem"]
    for o in ops:
        if o["k"] == "x":
            continue
        for i in o["wait"]:
            s, v = ops[i]["tok"]
            Q[o["e"]].wait_ge(T.sem[s], v)
        ins = o["fn"]()
        if o["k"] == "d" or (o["k"] == "c" and o.get("need")):
            ins.then_inc(T.sem[o["tok"][0]], 16 if o["k"] == "d" else 1)
    for e in "vapg":
        if cnt[e]:
            g.wait_ge(T.sem["e" + e], cnt[e])
    g.wait_ge(T.sem.sent, nsent)
    for o in ops:
        if o["k"] == "d" or o["k"] == "x":
            g.wait_ge(T.sem[o["tok"][0]], o["tok"][1])
